import numpy as np
import ml_dtypes


def mxq(x, axis, fmt="e4m3"):
    dtype, down = {"e4m3": (ml_dtypes.float8_e4m3fn, 7), "e5m2": (ml_dtypes.float8_e5m2, 14)}[fmt]
    v = np.moveaxis(np.asarray(x, np.float32).astype(ml_dtypes.bfloat16).astype(np.float64), axis, -1)
    blocks = v.reshape(v.shape[:-1] + (-1, 32))
    amax = np.abs(blocks).max(-1, keepdims=True)
    byte = np.maximum(np.where(amax > 0, np.frexp(amax)[1] - 1 + 127, 0) - down, 1)
    scale = np.exp2(byte - 127.0)
    codes = (blocks / scale).astype(np.float32).astype(dtype).astype(np.float64)
    return np.moveaxis((codes * scale).reshape(v.shape), -1, axis)


WIDE = False


def mx_kscale(k):
    if not WIDE:
        return np.ones(k)
    levels = np.array([10, -10, 5, -5, 0])
    if k % 512:
        return np.exp2(np.random.permutation(np.resize(levels, k // 32))).repeat(32)
    a = np.empty((k // 512, 16))
    for p in range(k // 512):
        a[p, :8] = np.random.permutation(np.resize(levels, 8))
        for g in range(8):
            far = levels[np.abs(levels - a[p, g]) >= 10]
            a[p, g + 8] = far[np.random.randint(len(far))]
    return np.exp2(a.ravel()).repeat(32)


BF16 = ml_dtypes.bfloat16


def bf(x):
    return np.asarray(x, np.float32).astype(BF16)


def f64(x):
    return np.asarray(x).astype(np.float64)

def planes(Y):
    n, m = Y.shape
    b = f64(bf(Y)).reshape(n // 32, 32, m)
    amax = np.abs(b).max(1)
    byte = np.clip(np.where(amax > 0, np.frexp(amax)[1] - 1 + 127 - 7, 1), 1, 254)
    codes = (b * np.exp2(127.0 - byte)[:, None, :]).reshape(n, m).astype(np.float32).astype(ml_dtypes.float8_e4m3fn).view(np.uint8)
    words = codes.reshape(n // 512, 128, 4, m).transpose(0, 1, 3, 2)
    return np.ascontiguousarray(words), np.ascontiguousarray(byte.astype(np.uint8).reshape(n // 512, 16, m))


R, B, N, C, E = 2, 128, 8, 512, 512


def split_features(x, w, bias):
    y = mxq(x.reshape(R, B * N, C), 2, "e4m3") @ mxq(w, 1, "e4m3")
    z = y.reshape(R, B, N, E) + bias[:, None, None, :]
    return np.maximum(z, 0.0)


def softmax_over_splits(l):
    shifted = l - np.max(l, axis=0, keepdims=True)
    e = np.exp(shifted)
    return e / np.sum(e, axis=0, keepdims=True)


def setup_inputs():
    s, t = mx_kscale(C), mx_kscale(E)
    return {"x": bf(np.random.standard_normal((R, B, N, C)) * s),
            "w": bf(np.random.standard_normal((R, C, E)) / np.sqrt(C) / s[:, None]),
            "bias": bf(np.random.standard_normal((R, E)) * 0.3),
            "gs": bf(np.random.standard_normal(E) * t),
            "wa": bf(np.random.standard_normal((R, E, E)) * 1.5 / np.sqrt(E) / t[:, None]),
            "ba": bf(np.random.standard_normal((R, E)) * 0.5)}


def core(x, w, bias, gs, wa, ba):
    u = split_features(f64(x), f64(w), f64(bias))
    s = np.mean(np.sum(u, axis=0), axis=1)
    sg = s * f64(gs)[None, :]
    l = (mxq(sg, 1, "e4m3") @ mxq(f64(wa), 1, "e4m3")) + f64(ba)[:, None, :]
    a = softmax_over_splits(l)
    return np.sum(a[:, :, None, :] * u, axis=0)


def reference(x, w, bias, gs, wa, ba):
    R_out = core(x, w, bias, gs, wa, ba)
    words, scales = planes(np.moveaxis(R_out, 2, 0).reshape(512, -1))
    return R_out, words, scales

@@ -1,0 +1,463 @@
+from contextlib import ExitStack
+
+import concourse.mybir as mybir
+from concourse.masks import make_identity
+
+F32 = mybir.dt.float32
+BF16 = mybir.dt.bfloat16
+U32 = mybir.dt.uint32
+I32 = mybir.dt.int32
+U8 = mybir.dt.uint8
+FP8X4 = mybir.dt.float8_e4m3fn_x4
+ADD = mybir.AluOpType.add
+MUL = mybir.AluOpType.mult
+MAX = mybir.AluOpType.max
+AF = mybir.ActivationFunctionType
+
+R, B, N, C, E = 2, 128, 8, 512, 512
+T = B * N
+FLOPS = 2 * R * T * C * E + 2 * R * B * E * E
+
+CH = 256
+CB = CH // N
+NCH = T // CH
+
+
+def tile_radixsplitattentionpointwise_x1_kernel(tc, x, w, bias, gs, wa, ba, out_0, out_1, out_2):
+    nc = tc.nc
+    with ExitStack() as ctx:
+        sb = ctx.enter_context(tc.tile_pool(name="sb", bufs=1))
+        pp = ctx.enter_context(tc.psum_pool(name="pp", bufs=1))
+        ctx.enter_context(tc.manual_schedule())
+
+        def big(name, shape, dtype):
+            return sb.tile(shape, dtype, name=name, align_bytes=64)
+
+        brow = big("brow", [128, 512], BF16)
+        nc.vector.memset(brow[:], 0.0)
+        nc.scalar.dma_start(out=brow[0:2, :], in_=bias)
+        nc.scalar.dma_start(out=brow[2:3, :], in_=gs.unsqueeze(0))
+        nc.scalar.dma_start(out=brow[3:5, :], in_=ba)
+        zero = big("zero", [128, 1], F32)
+        nc.vector.memset(zero[:], 0.0)
+        half = big("half", [128, 1], F32)
+        nc.scalar.activation(out=half[:], in_=zero[:], func=AF.Sigmoid)
+
+        identf = big("identf", [128, 128], F32)
+        make_identity(nc, identf[:])
+        identb = big("identb", [128, 128], BF16)
+        nc.vector.tensor_copy(out=identb[:], in_=identf[:])
+        grp = big("grp", [128, CB], F32)
+        nc.vector.reduce_sum(out=grp[:], in_=identf[:].rearrange("p (b n) -> p b n", n=4), axis=mybir.AxisListType.X)
+        sgc = {}
+        sgs = {}
+        for c in range(NCH):
+            sgc[c] = big("sgc%d" % c, [128, B], U32)
+            sgs[c] = big("sgs%d" % c, [128, B], U8)
+            nc.gpsimd.memset(sgc[c][:], 0)
+            nc.gpsimd.memset(sgs[c][:].bitcast(U32), 0)
+
+        xs = {}
+        xg = {}
+        xc = {}
+        xsc = {}
+        for c in range(NCH):
+            for r in range(R):
+                k = "%d%d" % (r, c)
+                xs[r, c] = big("xs" + k, [128, 1024], BF16)
+                xg[r, c] = big("xg" + k, [128, 1024], BF16)
+                xc[r, c] = big("xc" + k, [128, CH], U32)
+                xsc[r, c] = big("xsc" + k, [128, CH], U8)
+        wr = {}
+        wg = {}
+        wc = {}
+        ws = {}
+        for nm in ("w1", "w0", "a1", "a0"):
+            wr[nm] = big("wr" + nm, [128, 4, 512], BF16)
+            wg[nm] = big("wg" + nm, [128, 2048], BF16)
+            wc[nm] = big("wc" + nm, [128, 512], U32)
+            ws[nm] = big("ws" + nm, [128, 512], U8)
+        wsrc = {"w0": w[0], "w1": w[1], "a0": wa[0], "a1": wa[1]}
+
+        def load_x(r, c):
+            nc.sync.dma_start(
+                out=xs[r, c][:],
+                in_=x[r, CB * c : CB * (c + 1)].rearrange("b n c -> (b n) c").rearrange("(q j) c -> q (j c)", j=2),
+            )
+
+        def load_w(nm):
+            nc.sync.dma_start(out=wr[nm][:], in_=wsrc[nm].rearrange("(p j) c -> p j c", j=4))
+
+        vec = big("vec", [128, 5, 4], F32)
+        bd = big("bd", [128, 4], F32)
+        gsb = big("gsb", [128, CB, 4], F32)
+        ct = pp.tile([128, 4, 128], BF16, name="ct", tag="st", bufs=2)
+
+        def consts_pe():
+            for t in range(4):
+                nc.tensor.transpose(ct[:, t, :], brow[:, t::4], identb[:])
+
+        def consts():
+            nc.vector.tensor_copy(out=vec[:], in_=ct[:, :, 0:5].rearrange("p t r -> p r t"))
+
+        def consts2():
+            nc.gpsimd.tensor_sub(out=bd[:], in0=vec[:, 3, :], in1=vec[:, 4, :])
+            nc.gpsimd.tensor_scalar(
+                out=gsb[:], in0=vec[:, 2:3, :].to_broadcast([128, CB, 4]), scalar1=half[:], scalar2=0.25, op0=MUL, op1=MUL
+            )
+
+        xt = {}
+
+        def x_tr(r, c):
+            ps = pp.tile([128, 2, 2, 128], F32, name="xt%d%d" % (r, c), tag="tp", bufs=2)
+            xt[r, c] = ps
+            words = xs[r, c][:].bitcast(F32)
+            for j in range(2):
+                for u in range(2):
+                    nc.tensor.transpose(ps[:, j, u, :], words[:, 256 * j + u : 256 * (j + 1) : 2], identf[:])
+
+        def x_cp(r, c, eng):
+            dst = xg[r, c][:].bitcast(F32).rearrange("p (j q u) -> p j q u", j=2, u=2)
+            src = xt[r, c][:].rearrange("p j u q -> p j q u")
+            if eng == "v":
+                nc.vector.tensor_copy(out=dst, in_=src)
+            else:
+                nc.scalar.copy(out=dst, in_=src)
+
+        def x_q(r, c):
+            nc.vector.quantize_mx(out=xc[r, c][:].bitcast(FP8X4), scales=xsc[r, c][:], in_=xg[r, c][:])
+
+        def w_cp(nm, t0, t1, eng):
+            dst = wg[nm][:].rearrange("p (t m j) -> p t m j", t=4, j=4)[:, t0:t1]
+            src = wr[nm][:].rearrange("p j (m t) -> p t m j", t=4)[:, t0:t1]
+            if eng == "v":
+                if nm == "a1":
+                    nc.vector.tensor_scalar(out=dst, in0=src, scalar1=-1.0, scalar2=None, op0=MUL)
+                else:
+                    nc.vector.tensor_copy(out=dst, in_=src)
+            elif nm == "a1":
+                nc.scalar.activation(out=dst, in_=src, func=AF.Copy, scale=-1.0)
+            else:
+                nc.scalar.copy(out=dst, in_=src)
+
+        def w_q(nm, t0, t1):
+            nc.vector.quantize_mx(
+                out=wc[nm][:, 128 * t0 : 128 * t1].bitcast(FP8X4),
+                scales=ws[nm][:, 128 * t0 : 128 * t1],
+                in_=wg[nm][:, 512 * t0 : 512 * t1],
+            )
+
+        z = {}
+        u = {}
+        dd = {}
+        mm = {}
+        oo = {}
+        ob = {}
+        oc = {}
+        ot = {}
+        for c in range(NCH):
+            k = "%d" % c
+            u[0, c] = big("u0" + k, [128, 2, 4, 128], F32)
+            u[1, c] = big("u1" + k, [128, 2, 4, 128], F32)
+            dd[c] = big("dd" + k, [128, 2, 4, 128], F32)
+            mm[c] = big("mm" + k, [128, 2, 4, 128], F32)
+            oo[c] = big("oo" + k, [128, 2, 4, 128], F32)
+            ob[c] = big("ob" + k, [128, CH * 4], BF16)
+            oc[c] = big("oc" + k, [128, CH], U32)
+            ot[c] = big("ot" + k, [128, 2, 128, 4], F32)
+        osc = big("osc", [128, T], U8)
+
+        def mx1(r, c):
+            for i in range(2):
+                ps = pp.tile([128, 2, CH], F32, name="z%d%d%d" % (r, c, i), tag="z", bufs=3)
+                z[r, c, i] = ps
+                for k in range(2):
+                    t = 2 * i + k
+                    nc.tensor.matmul_mx(
+                        out=ps[:, k, :],
+                        lhsT=wc["w%d" % r][:, 128 * t : 128 * (t + 1)].bitcast(FP8X4),
+                        lhsT_scale=ws["w%d" % r][:, 128 * t : 128 * (t + 1)],
+                        rhs=xc[r, c][:].bitcast(FP8X4),
+                        rhs_scale=xsc[r, c][:],
+                        start=True,
+                        stop=True,
+                    )
+
+        def relu(r, c, eng="ssss"):
+            for t in range(4):
+                src = z[r, c, t // 2][:, t % 2, :].rearrange("p (j q) -> p j q", j=2)
+                if eng[t] == "s":
+                    nc.scalar.activation(out=u[r, c][:, :, t, :], in_=src, func=AF.Relu, bias=vec[:, r, t : t + 1])
+                else:
+                    nc.vector.tensor_scalar(
+                        out=u[r, c][:, :, t, :], in0=src, scalar1=vec[:, r, t : t + 1], scalar2=0.0, op0=ADD, op1=MAX
+                    )
+
+        def diff(c):
+            nc.vector.tensor_sub(out=dd[c][:], in0=u[0, c][:], in1=u[1, c][:])
+
+        pst = {}
+        ut = {}
+        pss = {}
+
+        def sum_t(c, plain=0):
+            pst[c] = pp.tile([128, 4, 128], F32, name="pst%d" % c, tag="st", bufs=2)
+            for t in range(4):
+                for i in range(4):
+                    nc.tensor.matmul(
+                        out=pst[c][:, t, :], lhsT=u[1 - i // 2, c][:, i % 2, t, :], rhs=identf[:],
+                        start=(i == 0), stop=(i == 3), is_transpose=(i >= plain),
+                    )
+
+        def sum_cp(c, eng):
+            ut[c] = big("ut%d" % c, [128, 4, 128], F32)
+            if eng == "v":
+                nc.vector.tensor_copy(out=ut[c][:], in_=pst[c][:])
+            else:
+                nc.scalar.copy(out=ut[c][:], in_=pst[c][:])
+
+        def sum_g(c):
+            pss[c] = pp.tile([128, 4, CB], F32, name="pss%d" % c, tag="st", bufs=2)
+            for t in range(4):
+                nc.tensor.matmul(out=pss[c][:, t, :], lhsT=ut[c][:, t, :], rhs=grp[:], start=True, stop=True)
+
+        sgb = {}
+        lps = {}
+        a0 = {}
+        for c in range(NCH):
+            sgb[c] = big("sgb%d" % c, [128, CB, 4], BF16)
+            a0[c] = big("a0g%d" % c, [128, 4, CB], F32)
+
+        def sgate(c):
+            nc.vector.tensor_mul(out=sgb[c][:], in0=pss[c][:].rearrange("p t b -> p b t"), in1=gsb[:])
+
+        def sg_q(c):
+            nc.vector.quantize_mx(
+                out=sgc[c][:, 0:CB].bitcast(FP8X4), scales=sgs[c][:, 0:CB], in_=sgb[c][:].rearrange("p b t -> p (b t)")
+            )
+
+        def mx2(c):
+            lps[c] = pp.tile([128, 4, B], F32, name="l%d" % c, tag="l", bufs=1)
+            for t in range(4):
+                for i, nm in enumerate(("a0", "a1")):
+                    nc.tensor.matmul_mx(
+                        out=lps[c][:, t, :],
+                        lhsT=wc[nm][:, 128 * t : 128 * (t + 1)].bitcast(FP8X4),
+                        lhsT_scale=ws[nm][:, 128 * t : 128 * (t + 1)],
+                        rhs=sgc[c][:].bitcast(FP8X4),
+                        rhs_scale=sgs[c][:],
+                        start=(i == 0),
+                        stop=(i == 1),
+                    )
+
+        def sigm(c):
+            for t in range(4):
+                nc.scalar.activation(out=a0[c][:, t, :], in_=lps[c][:, t, 0:CB], func=AF.Sigmoid, bias=bd[:, t : t + 1])
+
+        def mul_a(c, j):
+            nc.vector.tensor_mul(
+                out=mm[c][:, j].rearrange("p t (b i) -> p t b i", i=4),
+                in0=dd[c][:, j].rearrange("p t (b i) -> p t b i", i=4),
+                in1=a0[c][:].unsqueeze(3).to_broadcast([128, 4, CB, 4]),
+            )
+
+        def o_add(c, j):
+            nc.vector.tensor_add(out=oo[c][:, j], in0=mm[c][:, j], in1=u[1, c][:, j])
+
+        def obf(c, eng):
+            dst = ob[c][:].rearrange("p (q i k) -> p q k i", i=2, k=8)
+            src = oo[c][:].rearrange("p j t q -> p (j t) q").rearrange("p k (q i) -> p q k i", i=2)
+            if eng == "v":
+                nc.vector.tensor_copy(out=dst, in_=src)
+            else:
+                nc.scalar.copy(out=dst, in_=src)
+
+        def o_q(c):
+            nc.vector.quantize_mx(out=oc[c][:].bitcast(FP8X4), scales=osc[:, CH * c : CH * (c + 1)], in_=ob[c][:])
+
+        ops = {}
+
+        def o_tr(c, j, tag="tp"):
+            ps = pp.tile([128, 4, 128], F32, name="o%d%d" % (c, j), tag=tag, bufs=3 if tag == "z" else 2)
+            ops[c, j] = ps
+            for t in range(4):
+                nc.tensor.transpose(ps[:, t, :], oo[c][:, j, t, :], identf[:])
+
+        def o_cp(c, j, eng):
+            src = ops[c, j][:].rearrange("q t p -> q p t")
+            if eng == "v":
+                nc.vector.tensor_copy(out=ot[c][:, j], in_=src)
+            else:
+                nc.scalar.copy(out=ot[c][:, j], in_=src)
+
+        rows = out_0.rearrange("b n e -> (b n) e").rearrange("(c q j) e -> c q j e", c=NCH, j=2)
+        words = out_1.rearrange("g p m t -> (g p) (m t)").bitcast(I32)
+        srows = out_2.rearrange("g q m -> (g q) m").bitcast(I32)
+
+        def o_st(c):
+            nc.sync.dma_start(
+                out=rows[c].rearrange("q j e -> q (j e)"), in_=ot[c][:].rearrange("q j p t -> q (j p t)")
+            )
+
+        def o_st1(c, j):
+            nc.sync.dma_start(out=rows[c, :, j, :], in_=ot[c][:, j].rearrange("q p t -> q (p t)"))
+
+        def w_st(c):
+            nc.sync.dma_start(out=words[:, CH * c : CH * (c + 1)], in_=oc[c][:].bitcast(I32))
+
+        def s_st(c0, c1):
+            for q in range(4):
+                nc.scalar.dma_start(
+                    out=srows[4 * q : 4 * q + 4, CH // 4 * c0 : CH // 4 * c1],
+                    in_=osc[32 * q : 32 * q + 4, CH * c0 : CH * c1].bitcast(I32),
+                )
+
+        load_x(1, 0)
+        x_tr(1, 0)
+        load_x(0, 0)
+        x_cp(1, 0, "s")
+        load_x(0, 3)
+        x_tr(0, 0)
+        x_tr(0, 3)
+        load_w("w1")
+        x_q(1, 0)
+        load_w("w0")
+        load_x(1, 1)
+        consts_pe()
+        w_cp("w1", 2, 4, "s")
+        load_x(1, 2)
+        load_x(0, 1)
+        x_cp(0, 0, "s")
+        load_x(1, 3)
+        w_cp("w0", 0, 2, "s")
+        w_cp("w1", 0, 2, "v")
+        w_q("w1", 0, 2)
+        x_cp(0, 3, "v")
+        w_q("w1", 2, 4)
+        mx1(1, 0)
+        x_tr(1, 1)
+        x_tr(1, 2)
+        consts()
+        x_q(0, 0)
+        w_cp("w0", 2, 4, "v")
+        w_q("w0", 0, 2)
+        w_q("w0", 2, 4)
+        relu(1, 0, "sssv")
+        x_cp(1, 1, "s")
+        mx1(0, 0)
+        load_w("a0")
+        x_q(0, 3)
+        x_q(1, 1)
+        x_tr(0, 1)
+        relu(0, 0, "ssss")
+        x_cp(0, 1, "s")
+        x_cp(1, 2, "v")
+        w_cp("a0", 0, 4, "v")
+        load_x(0, 2)
+        diff(0)
+        mx1(1, 1)
+        x_q(0, 1)
+        sum_t(0, 0)
+        relu(1, 1, "ssss")
+        x_tr(0, 2)
+        x_q(1, 2)
+        load_w("a1")
+        w_cp("a1", 0, 4, "v")
+        x_tr(1, 3)
+        w_q("a0", 0, 4)
+        sum_cp(0, "s")
+        consts2()
+        x_cp(0, 2, "s")
+        w_q("a1", 0, 4)
+        mx1(0, 1)
+        relu(0, 1, "ssss")
+        x_cp(1, 3, "s")
+        x_q(0, 2)
+        sum_g(0)
+        mx1(1, 2)
+        sgate(0)
+        relu(1, 2, "ssss")
+        sum_t(1, 0)
+        x_q(1, 3)
+        sg_q(0)
+        mx1(0, 2)
+        sum_cp(1, "v")
+        relu(0, 2, "ssss")
+        mx2(0)
+        sigm(0)
+        diff(1)
+        sum_g(1)
+        sgate(1)
+        mx1(1, 3)
+        diff(2)
+        sum_t(2, 0)
+        sg_q(1)
+        mx2(1)
+        relu(1, 3, "ssss")
+        mul_a(0, 0)
+        sum_cp(2, "s")
+        mx1(0, 3)
+        mul_a(0, 1)
+        sigm(1)
+        o_add(0, 0)
+        relu(0, 3, "ssss")
+        sum_g(2)
+        o_add(0, 1)
+        mul_a(1, 1)
+        sum_t(3, 0)
+        sgate(2)
+        mul_a(1, 0)
+        obf(0, "s")
+        sg_q(2)
+        sum_cp(3, "s")
+        o_tr(0, 1)
+        o_tr(0, 0)
+        o_cp(0, 1, "s")
+        diff(3)
+        o_add(1, 1)
+        mx2(2)
+        sigm(2)
+        o_cp(0, 0, "s")
+        sum_g(3)
+        o_add(1, 0)
+        mul_a(2, 0)
+        o_st(0)
+        sgate(3)
+        obf(1, "s")
+        o_q(0)
+        o_tr(1, 0)
+        o_tr(1, 1)
+        o_cp(1, 0, "s")
+        sg_q(3)
+        mx2(3)
+        mul_a(2, 1)
+        o_cp(1, 1, "s")
+        o_st(1)
+        o_add(2, 0)
+        w_st(0)
+        o_add(2, 1)
+        sigm(3)
+        obf(2, "s")
+        o_q(1)
+        w_st(1)
+        mul_a(3, 0)
+        mul_a(3, 1)
+        o_add(3, 0)
+        o_tr(2, 0)
+        o_cp(2, 0, "s")
+        o_q(2)
+        o_add(3, 1)
+        o_tr(2, 1)
+        o_cp(2, 1, "s")
+        w_st(2)
+        obf(3, "v")
+        o_st(2)
+        o_tr(3, 0)
+        o_cp(3, 0, "s")
+        o_st1(3, 0)
+        o_q(3)
+        w_st(3)
+        o_tr(3, 1)
+        o_cp(3, 1, "s")
+        s_st(0, 4)
+        o_st1(3, 1)

@@ -10,6 +10,7 @@ I32 = mybir.dt.int32
 U8 = mybir.dt.uint8
 FP8X4 = mybir.dt.float8_e4m3fn_x4
 ADD = mybir.AluOpType.add
+SUB = mybir.AluOpType.subtract
 MUL = mybir.AluOpType.mult
 MAX = mybir.AluOpType.max
 AF = mybir.ActivationFunctionType
@@ -18,9 +19,9 @@ R, B, N, C, E = 2, 128, 8, 512, 512
 T = B * N
 FLOPS = 2 * R * T * C * E + 2 * R * B * E * E
 
-CH = 256
-CB = CH // N
-NCH = T // CH
+CB = 32
+CH = CB * N
+NCH = B // CB
 
 
 def tile_radixsplitattentionpointwise_x1_kernel(tc, x, w, bias, gs, wa, ba, out_0, out_1, out_2):
@@ -33,11 +34,12 @@ def tile_radixsplitattentionpointwise_x1_kernel(tc, x, w, bias, gs, wa, ba, out_
         def big(name, shape, dtype):
             return sb.tile(shape, dtype, name=name, align_bytes=64)
 
-        brow = big("brow", [128, 512], BF16)
-        nc.vector.memset(brow[:], 0.0)
-        nc.scalar.dma_start(out=brow[0:2, :], in_=bias)
-        nc.scalar.dma_start(out=brow[2:3, :], in_=gs.unsqueeze(0))
-        nc.scalar.dma_start(out=brow[3:5, :], in_=ba)
+        biasc = big("biasc", [128, 2, 16], BF16)
+        bac = big("bac", [128, 2, 16], BF16)
+        gsc = big("gsc", [128, 16], BF16)
+        nc.scalar.dma_start(out=biasc[:, :, 0:4], in_=bias.rearrange("r (p t) -> p r t", t=4))
+        nc.scalar.dma_start(out=gsc[:, 0:4], in_=gs.rearrange("(p t) -> p t", t=4))
+        nc.scalar.dma_start(out=bac[:, :, 0:4], in_=ba.rearrange("r (p t) -> p r t", t=4))
         zero = big("zero", [128, 1], F32)
         nc.vector.memset(zero[:], 0.0)
         half = big("half", [128, 1], F32)
@@ -47,8 +49,10 @@ def tile_radixsplitattentionpointwise_x1_kernel(tc, x, w, bias, gs, wa, ba, out_
         make_identity(nc, identf[:])
         identb = big("identb", [128, 128], BF16)
         nc.vector.tensor_copy(out=identb[:], in_=identf[:])
+        fold = big("fold", [128, 64], F32)
+        nc.vector.scalar_tensor_tensor(out=fold[:], in0=identf[:, 64:128], scalar=2.0, in1=identf[:, 0:64], op0=MUL, op1=ADD)
         grp = big("grp", [128, CB], F32)
-        nc.vector.reduce_sum(out=grp[:], in_=identf[:].rearrange("p (b n) -> p b n", n=4), axis=mybir.AxisListType.X)
+        nc.vector.reduce_sum(out=grp[:], in_=fold[:].rearrange("p (b i) -> p b i", i=2), axis=mybir.AxisListType.X)
         sgc = {}
         sgs = {}
         for c in range(NCH):
@@ -57,56 +61,36 @@ def tile_radixsplitattentionpointwise_x1_kernel(tc, x, w, bias, gs, wa, ba, out_
             nc.gpsimd.memset(sgc[c][:], 0)
             nc.gpsimd.memset(sgs[c][:].bitcast(U32), 0)
 
+        nb0 = big("nb0", [128, 4], F32)
+        pb0 = big("pb0", [128, 4], F32)
+        b0x8 = big("b0x8", [128, 4, CB], BF16)
+        pb1 = big("pb1", [128, 4], F32)
+        gs8 = big("gs8", [128, 4], F32)
+        bd = big("bd", [128, 4], F32)
+        nc.gpsimd.tensor_scalar(out=pb1[:], in0=biasc[:, 1, 0:4], scalar1=1.0, scalar2=0.0, op0=MUL, op1=ADD)
+        nc.gpsimd.tensor_scalar(out=nb0[:], in0=biasc[:, 0, 0:4], scalar1=-1.0, scalar2=0.0, op0=MUL, op1=ADD)
+        nc.gpsimd.tensor_scalar(out=pb0[:], in0=biasc[:, 0, 0:4], scalar1=1.0, scalar2=0.0, op0=MUL, op1=ADD)
+        nc.gpsimd.tensor_scalar(
+            out=b0x8[:], in0=biasc[:, 0, 0:4].unsqueeze(2).to_broadcast([128, 4, CB]), scalar1=8.0, scalar2=0.0, op0=MUL, op1=ADD
+        )
+        nc.gpsimd.tensor_scalar(out=gs8[:], in0=gsc[:, 0:4], scalar1=half[:], scalar2=0.25, op0=MUL, op1=MUL)
+        nc.gpsimd.tensor_sub(out=bd[:], in0=bac[:, 0, 0:4], in1=bac[:, 1, 0:4])
+
         xs = {}
         xg = {}
         xc = {}
         xsc = {}
+        xt = {}
         for c in range(NCH):
             for r in range(R):
-                k = "%d%d" % (r, c)
-                xs[r, c] = big("xs" + k, [128, 1024], BF16)
-                xg[r, c] = big("xg" + k, [128, 1024], BF16)
-                xc[r, c] = big("xc" + k, [128, CH], U32)
-                xsc[r, c] = big("xsc" + k, [128, CH], U8)
-        wr = {}
-        wg = {}
-        wc = {}
-        ws = {}
-        for nm in ("w1", "w0", "a1", "a0"):
-            wr[nm] = big("wr" + nm, [128, 4, 512], BF16)
-            wg[nm] = big("wg" + nm, [128, 2048], BF16)
-            wc[nm] = big("wc" + nm, [128, 512], U32)
-            ws[nm] = big("ws" + nm, [128, 512], U8)
-        wsrc = {"w0": w[0], "w1": w[1], "a0": wa[0], "a1": wa[1]}
+                xs[r, c] = big("xs%d%d" % (r, c), [128, 1024], BF16)
+                xg[r, c] = big("xg%d%d" % (r, c), [128, 1024], BF16)
+                xc[r, c] = big("xc%d%d" % (r, c), [128, CH], U32)
+                xsc[r, c] = big("xsc%d%d" % (r, c), [128, CH], U8)
 
         def load_x(r, c):
-            nc.sync.dma_start(
-                out=xs[r, c][:],
-                in_=x[r, CB * c : CB * (c + 1)].rearrange("b n c -> (b n) c").rearrange("(q j) c -> q (j c)", j=2),
-            )
-
-        def load_w(nm):
-            nc.sync.dma_start(out=wr[nm][:], in_=wsrc[nm].rearrange("(p j) c -> p j c", j=4))
-
-        vec = big("vec", [128, 5, 4], F32)
-        bd = big("bd", [128, 4], F32)
-        gsb = big("gsb", [128, CB, 4], F32)
-        ct = pp.tile([128, 4, 128], BF16, name="ct", tag="st", bufs=2)
-
-        def consts_pe():
-            for t in range(4):
-                nc.tensor.transpose(ct[:, t, :], brow[:, t::4], identb[:])
-
-        def consts():
-            nc.vector.tensor_copy(out=vec[:], in_=ct[:, :, 0:5].rearrange("p t r -> p r t"))
-
-        def consts2():
-            nc.gpsimd.tensor_sub(out=bd[:], in0=vec[:, 3, :], in1=vec[:, 4, :])
-            nc.gpsimd.tensor_scalar(
-                out=gsb[:], in0=vec[:, 2:3, :].to_broadcast([128, CB, 4]), scalar1=half[:], scalar2=0.25, op0=MUL, op1=MUL
-            )
-
-        xt = {}
+            rows = x[r, CB * c : CB * (c + 1)].rearrange("b n c -> (b n) c").rearrange("(q j) c -> q (j c)", j=2)
+            nc.sync.dma_start(out=xs[r, c][:], in_=rows)
 
         def x_tr(r, c):
             ps = pp.tile([128, 2, 2, 128], F32, name="xt%d%d" % (r, c), tag="tp", bufs=2)
@@ -116,120 +100,109 @@ def tile_radixsplitattentionpointwise_x1_kernel(tc, x, w, bias, gs, wa, ba, out_
                 for u in range(2):
                     nc.tensor.transpose(ps[:, j, u, :], words[:, 256 * j + u : 256 * (j + 1) : 2], identf[:])
 
-        def x_cp(r, c, eng):
-            dst = xg[r, c][:].bitcast(F32).rearrange("p (j q u) -> p j q u", j=2, u=2)
-            src = xt[r, c][:].rearrange("p j u q -> p j q u")
-            if eng == "v":
-                nc.vector.tensor_copy(out=dst, in_=src)
-            else:
-                nc.scalar.copy(out=dst, in_=src)
+        def x_cp(r, c):
+            dst = xg[r, c][:].bitcast(F32).rearrange("p (k j q u) -> p k j q u", k=2, j=2, u=2)
+            nc.scalar.copy(out=dst, in_=xt[r, c][:].rearrange("p j u (q k) -> p k j q u", k=2))
 
         def x_q(r, c):
             nc.vector.quantize_mx(out=xc[r, c][:].bitcast(FP8X4), scales=xsc[r, c][:], in_=xg[r, c][:])
 
-        def w_cp(nm, t0, t1, eng):
-            dst = wg[nm][:].rearrange("p (t m j) -> p t m j", t=4, j=4)[:, t0:t1]
-            src = wr[nm][:].rearrange("p j (m t) -> p t m j", t=4)[:, t0:t1]
-            if eng == "v":
-                if nm == "a1":
-                    nc.vector.tensor_scalar(out=dst, in0=src, scalar1=-1.0, scalar2=None, op0=MUL)
-                else:
-                    nc.vector.tensor_copy(out=dst, in_=src)
-            elif nm == "a1":
-                nc.scalar.activation(out=dst, in_=src, func=AF.Copy, scale=-1.0)
+        wsrc = {"w0": w[0], "w1": w[1], "a0": wa[0], "a1": wa[1]}
+        wr = {}
+        wg = {}
+        wc = {}
+        ws = {}
+        for nm in wsrc:
+            wg[nm] = big("wg" + nm, [128, 2048], BF16)
+            wc[nm] = big("wc" + nm, [128, 512], U32)
+            ws[nm] = big("ws" + nm, [128, 512], U8)
+
+        def load_w(nm, m0, m1):
+            wr[nm, m0] = big("wr%s%d" % (nm, m0), [128, 4, 4 * (m1 - m0)], BF16)
+            nc.sync.dma_start(out=wr[nm, m0][:], in_=wsrc[nm].rearrange("(p j) c -> p j c", j=4)[:, :, 4 * m0 : 4 * m1])
+
+        def w_cp(nm, base, m0, m1, eng):
+            dst = wg[nm][:].rearrange("p (t m j) -> p m j t", t=4, j=4)[:, m0:m1]
+            src = wr[nm, base][:].rearrange("p j (m t) -> p m j t", t=4)[:, m0 - base : m1 - base]
+            sign = -1.0 if nm == "a1" else 1.0
+            if eng is nc.vector:
+                nc.vector.tensor_scalar(out=dst, in0=src, scalar1=sign, scalar2=None, op0=MUL)
             else:
-                nc.scalar.copy(out=dst, in_=src)
+                nc.scalar.activation(out=dst, in_=src, func=AF.Copy, scale=sign)
 
-        def w_q(nm, t0, t1):
-            nc.vector.quantize_mx(
-                out=wc[nm][:, 128 * t0 : 128 * t1].bitcast(FP8X4),
-                scales=ws[nm][:, 128 * t0 : 128 * t1],
-                in_=wg[nm][:, 512 * t0 : 512 * t1],
-            )
+        def w_q(nm):
+            nc.vector.quantize_mx(out=wc[nm][:].bitcast(FP8X4), scales=ws[nm][:], in_=wg[nm][:])
 
-        z = {}
-        u = {}
-        dd = {}
+        y = {}
+        du = {}
         mm = {}
-        oo = {}
-        ob = {}
-        oc = {}
-        ot = {}
         for c in range(NCH):
-            k = "%d" % c
-            u[0, c] = big("u0" + k, [128, 2, 4, 128], F32)
-            u[1, c] = big("u1" + k, [128, 2, 4, 128], F32)
-            dd[c] = big("dd" + k, [128, 2, 4, 128], F32)
-            mm[c] = big("mm" + k, [128, 2, 4, 128], F32)
-            oo[c] = big("oo" + k, [128, 2, 4, 128], F32)
-            ob[c] = big("ob" + k, [128, CH * 4], BF16)
-            oc[c] = big("oc" + k, [128, CH], U32)
-            ot[c] = big("ot" + k, [128, 2, 128, 4], F32)
-        osc = big("osc", [128, T], U8)
+            du[c] = big("du%d" % c, [128, 4, 4, 2, 64], F32)
+            mm[c] = big("mm%d" % c, [128, 4, 4, 64], F32)
 
-        def mx1(r, c):
-            for i in range(2):
-                ps = pp.tile([128, 2, CH], F32, name="z%d%d%d" % (r, c, i), tag="z", bufs=3)
-                z[r, c, i] = ps
-                for k in range(2):
-                    t = 2 * i + k
-                    nc.tensor.matmul_mx(
-                        out=ps[:, k, :],
-                        lhsT=wc["w%d" % r][:, 128 * t : 128 * (t + 1)].bitcast(FP8X4),
-                        lhsT_scale=ws["w%d" % r][:, 128 * t : 128 * (t + 1)],
-                        rhs=xc[r, c][:].bitcast(FP8X4),
-                        rhs_scale=xsc[r, c][:],
-                        start=True,
-                        stop=True,
-                    )
+        def mx1(r, c, i):
+            y[r, c, i] = pp.tile([128, 2, 4, 64], F32, name="y%d%d%d" % (r, c, i), tag="y", bufs=4)
+            for k in range(2):
+                t = 2 * i + k
+                nc.tensor.matmul_mx(
+                    out=y[r, c, i][:, k].rearrange("p g q -> p (g q)"),
+                    lhsT=wc["w%d" % r][:, 128 * t : 128 * (t + 1)].bitcast(FP8X4),
+                    lhsT_scale=ws["w%d" % r][:, 128 * t : 128 * (t + 1)],
+                    rhs=xc[r, c][:].bitcast(FP8X4),
+                    rhs_scale=xsc[r, c][:],
+                    start=True,
+                    stop=True,
+                )
 
-        def relu(r, c, eng="ssss"):
-            for t in range(4):
-                src = z[r, c, t // 2][:, t % 2, :].rearrange("p (j q) -> p j q", j=2)
-                if eng[t] == "s":
-                    nc.scalar.activation(out=u[r, c][:, :, t, :], in_=src, func=AF.Relu, bias=vec[:, r, t : t + 1])
-                else:
-                    nc.vector.tensor_scalar(
-                        out=u[r, c][:, :, t, :], in0=src, scalar1=vec[:, r, t : t + 1], scalar2=0.0, op0=ADD, op1=MAX
-                    )
+        def relu1(c, t):
+            nc.scalar.activation(out=du[c][:, t, :, 1, :], in_=y[1, c, t // 2][:, t % 2], func=AF.Relu, bias=pb1[:, t : t + 1])
 
-        def diff(c):
-            nc.vector.tensor_sub(out=dd[c][:], in0=u[0, c][:], in1=u[1, c][:])
+        def diff0(c, t):
+            nc.vector.scalar_tensor_tensor(
+                out=du[c][:, t, :, 0, :],
+                in0=y[0, c, t // 2][:, t % 2],
+                scalar=nb0[:, t : t + 1],
+                in1=du[c][:, t, :, 1, :],
+                op0=MAX,
+                op1=SUB,
+            )
 
         pst = {}
         ut = {}
         pss = {}
 
-        def sum_t(c, plain=0):
-            pst[c] = pp.tile([128, 4, 128], F32, name="pst%d" % c, tag="st", bufs=2)
-            for t in range(4):
-                for i in range(4):
-                    nc.tensor.matmul(
-                        out=pst[c][:, t, :], lhsT=u[1 - i // 2, c][:, i % 2, t, :], rhs=identf[:],
-                        start=(i == 0), stop=(i == 3), is_transpose=(i >= plain),
-                    )
+        def sum_t(c, t):
+            if t == 0:
+                pst[c] = pp.tile([128, 4, 128], F32, name="pst%d" % c, tag="st", bufs=1)
+            for g in range(4):
+                nc.tensor.matmul(
+                    out=pst[c][:, t, :],
+                    lhsT=du[c][:, t, g].rearrange("p a q -> p (a q)"),
+                    rhs=identf[:],
+                    start=(g == 0),
+                    stop=(g == 3),
+                    is_transpose=True,
+                )
 
-        def sum_cp(c, eng):
+        def sum_cp(c):
             ut[c] = big("ut%d" % c, [128, 4, 128], F32)
-            if eng == "v":
-                nc.vector.tensor_copy(out=ut[c][:], in_=pst[c][:])
-            else:
-                nc.scalar.copy(out=ut[c][:], in_=pst[c][:])
+            nc.scalar.copy(out=ut[c][:], in_=pst[c][:])
 
         def sum_g(c):
-            pss[c] = pp.tile([128, 4, CB], F32, name="pss%d" % c, tag="st", bufs=2)
+            pss[c] = pp.tile([128, 4, CB], F32, name="pss%d" % c, tag="tp", bufs=2)
             for t in range(4):
-                nc.tensor.matmul(out=pss[c][:, t, :], lhsT=ut[c][:, t, :], rhs=grp[:], start=True, stop=True)
+                nc.tensor.matmul(out=pss[c][:, t, :], lhsT=identb[:], rhs=b0x8[:, t, :], start=True, stop=False)
+                nc.tensor.matmul(out=pss[c][:, t, :], lhsT=ut[c][:, t, :], rhs=grp[:], start=False, stop=True)
 
         sgb = {}
         lps = {}
         a0 = {}
-        for c in range(NCH):
-            sgb[c] = big("sgb%d" % c, [128, CB, 4], BF16)
-            a0[c] = big("a0g%d" % c, [128, 4, CB], F32)
 
         def sgate(c):
-            nc.vector.tensor_mul(out=sgb[c][:], in0=pss[c][:].rearrange("p t b -> p b t"), in1=gsb[:])
+            sgb[c] = big("sgb%d" % c, [128, CB, 4], BF16)
+            nc.vector.tensor_mul(
+                out=sgb[c][:], in0=pss[c][:].rearrange("p t b -> p b t"), in1=gs8[:].unsqueeze(1).to_broadcast([128, CB, 4])
+            )
 
         def sg_q(c):
             nc.vector.quantize_mx(
@@ -237,7 +210,7 @@ def tile_radixsplitattentionpointwise_x1_kernel(tc, x, w, bias, gs, wa, ba, out_
             )
 
         def mx2(c):
-            lps[c] = pp.tile([128, 4, B], F32, name="l%d" % c, tag="l", bufs=1)
+            lps[c] = pp.tile([128, 4, B], F32, name="l%d" % c, tag="ch", bufs=1)
             for t in range(4):
                 for i, nm in enumerate(("a0", "a1")):
                     nc.tensor.matmul_mx(
@@ -251,213 +224,198 @@ def tile_radixsplitattentionpointwise_x1_kernel(tc, x, w, bias, gs, wa, ba, out_
                     )
 
         def sigm(c):
+            a0[c] = big("a0g%d" % c, [128, 4, CB, 2], F32)
             for t in range(4):
-                nc.scalar.activation(out=a0[c][:, t, :], in_=lps[c][:, t, 0:CB], func=AF.Sigmoid, bias=bd[:, t : t + 1])
+                nc.scalar.activation(
+                    out=a0[c][:, t],
+                    in_=lps[c][:, t, 0:CB].unsqueeze(2).to_broadcast([128, CB, 2]),
+                    func=AF.Sigmoid,
+                    bias=bd[:, t : t + 1],
+                )
 
-        def mul_a(c, j):
-            nc.vector.tensor_mul(
-                out=mm[c][:, j].rearrange("p t (b i) -> p t b i", i=4),
-                in0=dd[c][:, j].rearrange("p t (b i) -> p t b i", i=4),
-                in1=a0[c][:].unsqueeze(3).to_broadcast([128, 4, CB, 4]),
+        oo = {}
+        ob = {}
+        oc = {}
+        ot = {}
+        ops = {}
+        for s in range(4):
+            oo[s] = big("oo%d" % s, [128, 2, 4, 128], F32)
+            ob[s] = big("ob%d" % s, [128, CH * 4], BF16)
+            oc[s] = big("oc%d" % s, [128, CH], U32)
+            ot[s] = big("ot%d" % s, [128, 2, 128, 4], F32)
+        osc = big("osc", [128, T], U8)
+
+        def mul_a(c, t):
+            nc.vector.scalar_tensor_tensor(
+                out=mm[c][:, t],
+                in0=du[c][:, t, :, 0, :],
+                scalar=pb0[:, t : t + 1],
+                in1=a0[c][:, t].rearrange("p b i -> p (b i)").unsqueeze(1).to_broadcast([128, 4, 64]),
+                op0=ADD,
+                op1=MUL,
             )
 
         def o_add(c, j):
-            nc.vector.tensor_add(out=oo[c][:, j], in0=mm[c][:, j], in1=u[1, c][:, j])
+            nc.vector.tensor_add(
+                out=oo[c][:, j].rearrange("p t (q k) -> p t q k", k=2),
+                in0=mm[c][:].rearrange("p t (k j) q -> p j t q k", j=2)[:, j],
+                in1=du[c][:, :, :, 1, :].rearrange("p t (k j) q -> p j t q k", j=2)[:, j],
+            )
 
-        def obf(c, eng):
-            dst = ob[c][:].rearrange("p (q i k) -> p q k i", i=2, k=8)
-            src = oo[c][:].rearrange("p j t q -> p (j t) q").rearrange("p k (q i) -> p q k i", i=2)
-            if eng == "v":
+        def o_bf(s, eng):
+            dst = ob[s][:].rearrange("p (q i k) -> p q k i", i=2, k=8)
+            src = oo[s][:].rearrange("p j t q -> p (j t) q").rearrange("p k (q i) -> p q k i", i=2)
+            if eng is nc.vector:
                 nc.vector.tensor_copy(out=dst, in_=src)
             else:
                 nc.scalar.copy(out=dst, in_=src)
 
-        def o_q(c):
-            nc.vector.quantize_mx(out=oc[c][:].bitcast(FP8X4), scales=osc[:, CH * c : CH * (c + 1)], in_=ob[c][:])
+        def o_q(s):
+            nc.vector.quantize_mx(out=oc[s][:].bitcast(FP8X4), scales=osc[:, CH * s : CH * (s + 1)], in_=ob[s][:])
 
-        ops = {}
-
-        def o_tr(c, j, tag="tp"):
-            ps = pp.tile([128, 4, 128], F32, name="o%d%d" % (c, j), tag=tag, bufs=3 if tag == "z" else 2)
-            ops[c, j] = ps
+        def o_tr(s, j):
+            ps = pp.tile([128, 4, 128], F32, name="o%d%d" % (s, j), tag="y", bufs=4)
+            ops[s, j] = ps
             for t in range(4):
-                nc.tensor.transpose(ps[:, t, :], oo[c][:, j, t, :], identf[:])
+                nc.tensor.transpose(ps[:, t, :], oo[s][:, j, t, :], identf[:])
 
-        def o_cp(c, j, eng):
-            src = ops[c, j][:].rearrange("q t p -> q p t")
-            if eng == "v":
-                nc.vector.tensor_copy(out=ot[c][:, j], in_=src)
-            else:
-                nc.scalar.copy(out=ot[c][:, j], in_=src)
+        def o_cp(s, j):
+            nc.scalar.copy(out=ot[s][:, j], in_=ops[s, j][:].rearrange("q t p -> q p t"))
 
-        rows = out_0.rearrange("b n e -> (b n) e").rearrange("(c q j) e -> c q j e", c=NCH, j=2)
+        rows = out_0.rearrange("b n e -> (b n) e").rearrange("(s q j) e -> s q j e", s=4, j=2)
         words = out_1.rearrange("g p m t -> (g p) (m t)").bitcast(I32)
         srows = out_2.rearrange("g q m -> (g q) m").bitcast(I32)
 
-        def o_st(c):
-            nc.sync.dma_start(
-                out=rows[c].rearrange("q j e -> q (j e)"), in_=ot[c][:].rearrange("q j p t -> q (j p t)")
-            )
+        def o_st(s, j):
+            nc.sync.dma_start(out=rows[s, :, j, :], in_=ot[s][:, j].rearrange("q p t -> q (p t)"))
 
-        def o_st1(c, j):
-            nc.sync.dma_start(out=rows[c, :, j, :], in_=ot[c][:, j].rearrange("q p t -> q (p t)"))
+        def w_st(s):
+            nc.sync.dma_start(out=words[:, CH * s : CH * (s + 1)], in_=oc[s][:].bitcast(I32))
 
-        def w_st(c):
-            nc.sync.dma_start(out=words[:, CH * c : CH * (c + 1)], in_=oc[c][:].bitcast(I32))
-
-        def s_st(c0, c1):
+        def s_st():
             for q in range(4):
-                nc.scalar.dma_start(
-                    out=srows[4 * q : 4 * q + 4, CH // 4 * c0 : CH // 4 * c1],
-                    in_=osc[32 * q : 32 * q + 4, CH * c0 : CH * c1].bitcast(I32),
-                )
+                nc.scalar.dma_start(out=srows[4 * q : 4 * q + 4, :], in_=osc[32 * q : 32 * q + 4, :].bitcast(I32))
+
+        V, S = nc.vector, nc.scalar
+
+        def x_turn(r, c):
+            x_tr(r, c)
+            x_cp(r, c)
+
+        def first(c, i):
+            mx1(1, c, i)
+            relu1(c, 2 * i)
+            relu1(c, 2 * i + 1)
+
+        def second(c, i):
+            mx1(0, c, i)
+            diff0(c, 2 * i)
+            diff0(c, 2 * i + 1)
+
+        def weigh(c):
+            for t in range(4):
+                mul_a(c, t)
+
+        def turn_back(c):
+            for j in range(2):
+                o_tr(c, j)
+                o_cp(c, j)
+                o_st(c, j)
 
         load_x(1, 0)
-        x_tr(1, 0)
+        load_w("w1", 0, 64)
+        load_w("w1", 64, 128)
         load_x(0, 0)
-        x_cp(1, 0, "s")
-        load_x(0, 3)
-        x_tr(0, 0)
-        x_tr(0, 3)
-        load_w("w1")
-        x_q(1, 0)
-        load_w("w0")
+        load_w("w0", 0, 128)
         load_x(1, 1)
-        consts_pe()
-        w_cp("w1", 2, 4, "s")
-        load_x(1, 2)
+        load_w("a0", 0, 128)
         load_x(0, 1)
-        x_cp(0, 0, "s")
-        load_x(1, 3)
-        w_cp("w0", 0, 2, "s")
-        w_cp("w1", 0, 2, "v")
-        w_q("w1", 0, 2)
-        x_cp(0, 3, "v")
-        w_q("w1", 2, 4)
-        mx1(1, 0)
-        x_tr(1, 1)
-        x_tr(1, 2)
-        consts()
+        load_w("a1", 0, 128)
+        for c in range(2, NCH):
+            load_x(1, c)
+            load_x(0, c)
+
+        x_turn(1, 0)
+        w_cp("w1", 0, 0, 64, V)
+        w_cp("w1", 64, 64, 128, V)
+        x_q(1, 0)
+        w_q("w1")
+        x_turn(0, 0)
+        w_cp("w0", 0, 0, 96, V)
+        w_cp("w0", 0, 96, 128, S)
+        first(0, 0)
+        mx1(1, 0, 1)
+        x_turn(1, 1)
+        relu1(0, 2)
+        relu1(0, 3)
         x_q(0, 0)
-        w_cp("w0", 2, 4, "v")
-        w_q("w0", 0, 2)
-        w_q("w0", 2, 4)
-        relu(1, 0, "sssv")
-        x_cp(1, 1, "s")
-        mx1(0, 0)
-        load_w("a0")
-        x_q(0, 3)
+        w_q("w0")
+        w_cp("a0", 0, 0, 128, V)
         x_q(1, 1)
-        x_tr(0, 1)
-        relu(0, 0, "ssss")
-        x_cp(0, 1, "s")
-        x_cp(1, 2, "v")
-        w_cp("a0", 0, 4, "v")
-        load_x(0, 2)
-        diff(0)
-        mx1(1, 1)
-        x_q(0, 1)
-        sum_t(0, 0)
-        relu(1, 1, "ssss")
-        x_tr(0, 2)
-        x_q(1, 2)
-        load_w("a1")
-        w_cp("a1", 0, 4, "v")
-        x_tr(1, 3)
-        w_q("a0", 0, 4)
-        sum_cp(0, "s")
-        consts2()
-        x_cp(0, 2, "s")
-        w_q("a1", 0, 4)
-        mx1(0, 1)
-        relu(0, 1, "ssss")
-        x_cp(1, 3, "s")
-        x_q(0, 2)
-        sum_g(0)
-        mx1(1, 2)
-        sgate(0)
-        relu(1, 2, "ssss")
-        sum_t(1, 0)
-        x_q(1, 3)
-        sg_q(0)
-        mx1(0, 2)
-        sum_cp(1, "v")
-        relu(0, 2, "ssss")
-        mx2(0)
-        sigm(0)
-        diff(1)
-        sum_g(1)
-        sgate(1)
-        mx1(1, 3)
-        diff(2)
-        sum_t(2, 0)
-        sg_q(1)
-        mx2(1)
-        relu(1, 3, "ssss")
-        mul_a(0, 0)
-        sum_cp(2, "s")
-        mx1(0, 3)
-        mul_a(0, 1)
-        sigm(1)
-        o_add(0, 0)
-        relu(0, 3, "ssss")
-        sum_g(2)
-        o_add(0, 1)
-        mul_a(1, 1)
-        sum_t(3, 0)
-        sgate(2)
-        mul_a(1, 0)
-        obf(0, "s")
-        sg_q(2)
-        sum_cp(3, "s")
-        o_tr(0, 1)
-        o_tr(0, 0)
-        o_cp(0, 1, "s")
-        diff(3)
-        o_add(1, 1)
-        mx2(2)
-        sigm(2)
-        o_cp(0, 0, "s")
-        sum_g(3)
-        o_add(1, 0)
-        mul_a(2, 0)
-        o_st(0)
-        sgate(3)
-        obf(1, "s")
-        o_q(0)
-        o_tr(1, 0)
-        o_tr(1, 1)
-        o_cp(1, 0, "s")
-        sg_q(3)
-        mx2(3)
-        mul_a(2, 1)
-        o_cp(1, 1, "s")
-        o_st(1)
-        o_add(2, 0)
-        w_st(0)
-        o_add(2, 1)
-        sigm(3)
-        obf(2, "s")
-        o_q(1)
-        w_st(1)
-        mul_a(3, 0)
-        mul_a(3, 1)
-        o_add(3, 0)
-        o_tr(2, 0)
-        o_cp(2, 0, "s")
-        o_q(2)
-        o_add(3, 1)
-        o_tr(2, 1)
-        o_cp(2, 1, "s")
-        w_st(2)
-        obf(3, "v")
-        o_st(2)
-        o_tr(3, 0)
-        o_cp(3, 0, "s")
-        o_st1(3, 0)
-        o_q(3)
-        w_st(3)
-        o_tr(3, 1)
-        o_cp(3, 1, "s")
-        s_st(0, 4)
-        o_st1(3, 1)
+        x_turn(0, 1)
+
+        for c in range(NCH + 2):
+            gate = 1 <= c <= NCH
+            if c < NCH:
+                second(c, 0)
+                second(c, 1)
+            if c == 0:
+                x_q(0, 1)
+            if c + 1 < NCH:
+                first(c + 1, 0)
+                first(c + 1, 1)
+            if gate:
+                sum_g(c - 1)
+            if 3 <= c <= NCH:
+                o_bf(c - 3, S)
+            if c >= 2:
+                mul_a(c - 2, 0)
+                mul_a(c - 2, 1)
+            if gate:
+                sgate(c - 1)
+            if c == 0:
+                w_q("a0")
+                w_cp("a1", 0, 0, 128, V)
+            if c == 1:
+                w_q("a1")
+            if c >= 2:
+                mul_a(c - 2, 2)
+            if gate:
+                sg_q(c - 1)
+            if c == NCH:
+                turn_back(c - 3)
+                mx2(c - 1)
+                sigm(c - 1)
+            if c >= 2:
+                mul_a(c - 2, 3)
+            if c + 2 < NCH:
+                for r in (1, 0):
+                    x_turn(r, c + 2)
+                for r in (1, 0):
+                    x_q(r, c + 2)
+            if 3 <= c <= NCH:
+                o_q(c - 3)
+                w_st(c - 3)
+            if c >= 2:
+                o_add(c - 2, 0)
+                o_add(c - 2, 1)
+            if c < NCH:
+                for t in range(4):
+                    sum_t(c, t)
+                sum_cp(c)
+            if 1 <= c < NCH:
+                mx2(c - 1)
+                sigm(c - 1)
+            if c == NCH - 1:
+                turn_back(c - 3)
+            if c == NCH:
+                o_bf(c - 2, S)
+                turn_back(c - 2)
+        last = NCH - 1
+        o_q(last - 1)
+        w_st(last - 1)
+        o_bf(last, V)
+        turn_back(last)
+        o_q(last)
+        w_st(last)
+        s_st()

@@ -53,28 +53,25 @@ def tile_radixsplitattentionpointwise_x1_kernel(tc, x, w, bias, gs, wa, ba, out_
         nc.vector.scalar_tensor_tensor(out=fold[:], in0=identf[:, 64:128], scalar=2.0, in1=identf[:, 0:64], op0=MUL, op1=ADD)
         grp = big("grp", [128, CB], F32)
         nc.vector.reduce_sum(out=grp[:], in_=fold[:].rearrange("p (b i) -> p b i", i=2), axis=mybir.AxisListType.X)
-        sgc = {}
-        sgs = {}
-        for c in range(NCH):
-            sgc[c] = big("sgc%d" % c, [128, B], U32)
-            sgs[c] = big("sgs%d" % c, [128, B], U8)
-            nc.gpsimd.memset(sgc[c][:], 0)
-            nc.gpsimd.memset(sgs[c][:].bitcast(U32), 0)
+        sgc = big("sgc", [128, B], U32)
+        sgs = big("sgs", [128, B], U8)
+        nc.gpsimd.memset(sgc[:], 0)
+        nc.gpsimd.memset(sgs[:].bitcast(U32), 0)
 
         nb0 = big("nb0", [128, 4], F32)
-        pb0 = big("pb0", [128, 4], F32)
         b0x8 = big("b0x8", [128, 4, CB], BF16)
-        pb1 = big("pb1", [128, 4], F32)
         gs8 = big("gs8", [128, 4], F32)
         bd = big("bd", [128, 4], F32)
-        nc.gpsimd.tensor_scalar(out=pb1[:], in0=biasc[:, 1, 0:4], scalar1=1.0, scalar2=0.0, op0=MUL, op1=ADD)
-        nc.gpsimd.tensor_scalar(out=nb0[:], in0=biasc[:, 0, 0:4], scalar1=-1.0, scalar2=0.0, op0=MUL, op1=ADD)
-        nc.gpsimd.tensor_scalar(out=pb0[:], in0=biasc[:, 0, 0:4], scalar1=1.0, scalar2=0.0, op0=MUL, op1=ADD)
-        nc.gpsimd.tensor_scalar(
-            out=b0x8[:], in0=biasc[:, 0, 0:4].unsqueeze(2).to_broadcast([128, 4, CB]), scalar1=8.0, scalar2=0.0, op0=MUL, op1=ADD
-        )
-        nc.gpsimd.tensor_scalar(out=gs8[:], in0=gsc[:, 0:4], scalar1=half[:], scalar2=0.25, op0=MUL, op1=MUL)
-        nc.gpsimd.tensor_sub(out=bd[:], in0=bac[:, 0, 0:4], in1=bac[:, 1, 0:4])
+
+        def consts_s():
+            nc.scalar.activation(out=nb0[:], in_=biasc[:, 0, 0:4], func=AF.Copy, scale=-1.0)
+            nc.scalar.activation(
+                out=b0x8[:], in_=biasc[:, 0, 0:4].unsqueeze(2).to_broadcast([128, 4, CB]), func=AF.Copy, scale=8.0
+            )
+
+        def consts_v():
+            nc.vector.tensor_scalar(out=gs8[:], in0=gsc[:, 0:4], scalar1=half[:], scalar2=0.25, op0=MUL, op1=MUL)
+            nc.vector.tensor_sub(out=bd[:], in0=bac[:, 0, 0:4], in1=bac[:, 1, 0:4])
 
         xs = {}
         xg = {}
@@ -122,13 +119,17 @@ def tile_radixsplitattentionpointwise_x1_kernel(tc, x, w, bias, gs, wa, ba, out_
             nc.sync.dma_start(out=wr[nm, m0][:], in_=wsrc[nm].rearrange("(p j) c -> p j c", j=4)[:, :, 4 * m0 : 4 * m1])
 
         def w_cp(nm, base, m0, m1, eng):
-            dst = wg[nm][:].rearrange("p (t m j) -> p m j t", t=4, j=4)[:, m0:m1]
-            src = wr[nm, base][:].rearrange("p j (m t) -> p m j t", t=4)[:, m0 - base : m1 - base]
-            sign = -1.0 if nm == "a1" else 1.0
+            dst = wg[nm][:].rearrange("p (t m j) -> p t m j", t=4, j=4)[:, :, m0:m1]
+            src = wr[nm, base][:].rearrange("p j (m t) -> p t m j", t=4)[:, :, m0 - base : m1 - base]
+            if nm == "a1":
+                nc.vector.tensor_scalar(out=dst, in0=src, scalar1=-1.0, scalar2=None, op0=MUL)
+                return
+            dst = dst.rearrange("p t (n i) j -> p n t i j", i=2)
+            src = src.rearrange("p t (n i) j -> p n t i j", i=2)
             if eng is nc.vector:
-                nc.vector.tensor_scalar(out=dst, in0=src, scalar1=sign, scalar2=None, op0=MUL)
+                nc.vector.tensor_copy(out=dst, in_=src)
             else:
-                nc.scalar.activation(out=dst, in_=src, func=AF.Copy, scale=sign)
+                nc.scalar.copy(out=dst, in_=src)
 
         def w_q(nm):
             nc.vector.quantize_mx(out=wc[nm][:].bitcast(FP8X4), scales=ws[nm][:], in_=wg[nm][:])
@@ -155,7 +156,7 @@ def tile_radixsplitattentionpointwise_x1_kernel(tc, x, w, bias, gs, wa, ba, out_
                 )
 
         def relu1(c, t):
-            nc.scalar.activation(out=du[c][:, t, :, 1, :], in_=y[1, c, t // 2][:, t % 2], func=AF.Relu, bias=pb1[:, t : t + 1])
+            nc.scalar.activation(out=du[c][:, t, :, 1, :], in_=y[1, c, t // 2][:, t % 2], func=AF.Relu, bias=biasc[:, 1, t : t + 1])
 
         def diff0(c, t):
             nc.vector.scalar_tensor_tensor(
@@ -206,7 +207,7 @@ def tile_radixsplitattentionpointwise_x1_kernel(tc, x, w, bias, gs, wa, ba, out_
 
         def sg_q(c):
             nc.vector.quantize_mx(
-                out=sgc[c][:, 0:CB].bitcast(FP8X4), scales=sgs[c][:, 0:CB], in_=sgb[c][:].rearrange("p b t -> p (b t)")
+                out=sgc[:, 0:CB].bitcast(FP8X4), scales=sgs[:, 0:CB], in_=sgb[c][:].rearrange("p b t -> p (b t)")
             )
 
         def mx2(c):
@@ -217,8 +218,8 @@ def tile_radixsplitattentionpointwise_x1_kernel(tc, x, w, bias, gs, wa, ba, out_
                         out=lps[c][:, t, :],
                         lhsT=wc[nm][:, 128 * t : 128 * (t + 1)].bitcast(FP8X4),
                         lhsT_scale=ws[nm][:, 128 * t : 128 * (t + 1)],
-                        rhs=sgc[c][:].bitcast(FP8X4),
-                        rhs_scale=sgs[c][:],
+                        rhs=sgc[:].bitcast(FP8X4),
+                        rhs_scale=sgs[:],
                         start=(i == 0),
                         stop=(i == 1),
                     )
@@ -249,7 +250,7 @@ def tile_radixsplitattentionpointwise_x1_kernel(tc, x, w, bias, gs, wa, ba, out_
             nc.vector.scalar_tensor_tensor(
                 out=mm[c][:, t],
                 in0=du[c][:, t, :, 0, :],
-                scalar=pb0[:, t : t + 1],
+                scalar=biasc[:, 0, t : t + 1],
                 in1=a0[c][:, t].rearrange("p b i -> p (b i)").unsqueeze(1).to_broadcast([128, 4, 64]),
                 op0=ADD,
                 op1=MUL,
@@ -336,6 +337,7 @@ def tile_radixsplitattentionpointwise_x1_kernel(tc, x, w, bias, gs, wa, ba, out_
             load_x(0, c)
 
         x_turn(1, 0)
+        consts_s()
         w_cp("w1", 0, 0, 64, V)
         w_cp("w1", 64, 64, 128, V)
         x_q(1, 0)
@@ -349,6 +351,7 @@ def tile_radixsplitattentionpointwise_x1_kernel(tc, x, w, bias, gs, wa, ba, out_
         relu1(0, 2)
         relu1(0, 3)
         x_q(0, 0)
+        consts_v()
         w_q("w0")
         w_cp("a0", 0, 0, 128, V)
         x_q(1, 1)

@@ -19,7 +19,7 @@ R, B, N, C, E = 2, 128, 8, 512, 512
 T = B * N
 FLOPS = 2 * R * T * C * E + 2 * R * B * E * E
 
-CB = 32
+CB = 64
 CH = CB * N
 NCH = B // CB
 
@@ -30,6 +30,7 @@ def tile_radixsplitattentionpointwise_x1_kernel(tc, x, w, bias, gs, wa, ba, out_
         sb = ctx.enter_context(tc.tile_pool(name="sb", bufs=1))
         pp = ctx.enter_context(tc.psum_pool(name="pp", bufs=1))
         ctx.enter_context(tc.manual_schedule())
+        V, S = nc.vector, nc.scalar
 
         def big(name, shape, dtype):
             return sb.tile(shape, dtype, name=name, align_bytes=64)
@@ -38,21 +39,17 @@ def tile_radixsplitattentionpointwise_x1_kernel(tc, x, w, bias, gs, wa, ba, out_
         bac = big("bac", [128, 2, 16], BF16)
         gsc = big("gsc", [128, 16], BF16)
         nc.scalar.dma_start(out=biasc[:, :, 0:4], in_=bias.rearrange("r (p t) -> p r t", t=4))
-        nc.scalar.dma_start(out=gsc[:, 0:4], in_=gs.rearrange("(p t) -> p t", t=4))
-        nc.scalar.dma_start(out=bac[:, :, 0:4], in_=ba.rearrange("r (p t) -> p r t", t=4))
-        zero = big("zero", [128, 1], F32)
-        nc.vector.memset(zero[:], 0.0)
+        zeros = big("zeros", [128, 512], F32)
+        nc.vector.memset(zeros[:], 0.0)
         half = big("half", [128, 1], F32)
-        nc.scalar.activation(out=half[:], in_=zero[:], func=AF.Sigmoid)
+        nc.scalar.activation(out=half[:], in_=zeros[:, 0:1], func=AF.Sigmoid)
 
         identf = big("identf", [128, 128], F32)
         make_identity(nc, identf[:])
         identb = big("identb", [128, 128], BF16)
         nc.vector.tensor_copy(out=identb[:], in_=identf[:])
-        fold = big("fold", [128, 64], F32)
+        fold = big("fold", [128, CB], F32)
         nc.vector.scalar_tensor_tensor(out=fold[:], in0=identf[:, 64:128], scalar=2.0, in1=identf[:, 0:64], op0=MUL, op1=ADD)
-        grp = big("grp", [128, CB], F32)
-        nc.vector.reduce_sum(out=grp[:], in_=fold[:].rearrange("p (b i) -> p b i", i=2), axis=mybir.AxisListType.X)
         sgc = big("sgc", [128, B], U32)
         sgs = big("sgs", [128, B], U8)
         nc.gpsimd.memset(sgc[:], 0)
@@ -69,9 +66,19 @@ def tile_radixsplitattentionpointwise_x1_kernel(tc, x, w, bias, gs, wa, ba, out_
                 out=b0x8[:], in_=biasc[:, 0, 0:4].unsqueeze(2).to_broadcast([128, 4, CB]), func=AF.Copy, scale=8.0
             )
 
+        def load_gate_vectors():
+            nc.sync.dma_start(out=gsc[:, 0:4], in_=gs.rearrange("(p t) -> p t", t=4))
+            nc.sync.dma_start(out=bac[:, :, 0:4], in_=ba.rearrange("r (p t) -> p r t", t=4))
+
         def consts_v():
             nc.vector.tensor_scalar(out=gs8[:], in0=gsc[:, 0:4], scalar1=half[:], scalar2=0.25, op0=MUL, op1=MUL)
             nc.vector.tensor_sub(out=bd[:], in0=bac[:, 0, 0:4], in1=bac[:, 1, 0:4])
+
+        def copy(eng, dst, src):
+            if eng is nc.vector:
+                nc.vector.tensor_copy(out=dst, in_=src)
+            else:
+                nc.scalar.copy(out=dst, in_=src)
 
         xs = {}
         xg = {}
@@ -80,29 +87,33 @@ def tile_radixsplitattentionpointwise_x1_kernel(tc, x, w, bias, gs, wa, ba, out_
         xt = {}
         for c in range(NCH):
             for r in range(R):
-                xs[r, c] = big("xs%d%d" % (r, c), [128, 1024], BF16)
-                xg[r, c] = big("xg%d%d" % (r, c), [128, 1024], BF16)
+                xg[r, c] = big("xg%d%d" % (r, c), [128, 4 * CH], BF16)
                 xc[r, c] = big("xc%d%d" % (r, c), [128, CH], U32)
                 xsc[r, c] = big("xsc%d%d" % (r, c), [128, CH], U8)
+                for k in range(2):
+                    xs[r, c, k] = big("xs%d%d%d" % (r, c, k), [128, 1024], BF16)
 
-        def load_x(r, c):
-            rows = x[r, CB * c : CB * (c + 1)].rearrange("b n c -> (b n) c").rearrange("(q j) c -> q (j c)", j=2)
-            nc.sync.dma_start(out=xs[r, c][:], in_=rows)
+        def load_x(r, c, k):
+            rows = x[r, CB * c : CB * (c + 1)].rearrange("b n c -> (b n) c").rearrange("(q k j) c -> k q (j c)", k=2, j=2)
+            nc.sync.dma_start(out=xs[r, c, k][:], in_=rows[k])
 
-        def x_tr(r, c):
-            ps = pp.tile([128, 2, 2, 128], F32, name="xt%d%d" % (r, c), tag="tp", bufs=2)
-            xt[r, c] = ps
-            words = xs[r, c][:].bitcast(F32)
+        def x_tr(r, c, k):
+            ps = pp.tile([128, 2, 2, 128], F32, name="xt%d%d%d" % (r, c, k), tag="ps", bufs=8)
+            xt[r, c, k] = ps
+            words = xs[r, c, k][:].bitcast(F32)
             for j in range(2):
                 for u in range(2):
                     nc.tensor.transpose(ps[:, j, u, :], words[:, 256 * j + u : 256 * (j + 1) : 2], identf[:])
 
-        def x_cp(r, c):
-            dst = xg[r, c][:].bitcast(F32).rearrange("p (k j q u) -> p k j q u", k=2, j=2, u=2)
-            nc.scalar.copy(out=dst, in_=xt[r, c][:].rearrange("p j u (q k) -> p k j q u", k=2))
+        def x_cp(r, c, k, eng):
+            dst = xg[r, c][:, 1024 * k : 1024 * (k + 1)].bitcast(F32).rearrange("p (j h b u) -> p j h b u", j=2, h=2, u=2)
+            copy(eng, dst, xt[r, c, k][:].rearrange("p j u (b h) -> p j h b u", h=2))
 
-        def x_q(r, c):
-            nc.vector.quantize_mx(out=xc[r, c][:].bitcast(FP8X4), scales=xsc[r, c][:], in_=xg[r, c][:])
+        def x_q(r, c, k0, k1):
+            cols = slice(256 * k0, 256 * k1)
+            nc.vector.quantize_mx(
+                out=xc[r, c][:, cols].bitcast(FP8X4), scales=xsc[r, c][:, cols], in_=xg[r, c][:, 1024 * k0 : 1024 * k1]
+            )
 
         wsrc = {"w0": w[0], "w1": w[1], "a0": wa[0], "a1": wa[1]}
         wr = {}
@@ -122,14 +133,12 @@ def tile_radixsplitattentionpointwise_x1_kernel(tc, x, w, bias, gs, wa, ba, out_
             dst = wg[nm][:].rearrange("p (t m j) -> p t m j", t=4, j=4)[:, :, m0:m1]
             src = wr[nm, base][:].rearrange("p j (m t) -> p t m j", t=4)[:, :, m0 - base : m1 - base]
             if nm == "a1":
-                nc.vector.tensor_scalar(out=dst, in0=src, scalar1=-1.0, scalar2=None, op0=MUL)
+                if eng is nc.vector:
+                    nc.vector.tensor_scalar(out=dst, in0=src, scalar1=-1.0, scalar2=None, op0=MUL)
+                else:
+                    nc.scalar.activation(out=dst, in_=src, func=AF.Copy, scale=-1.0)
                 return
-            dst = dst.rearrange("p t (n i) j -> p n t i j", i=2)
-            src = src.rearrange("p t (n i) j -> p n t i j", i=2)
-            if eng is nc.vector:
-                nc.vector.tensor_copy(out=dst, in_=src)
-            else:
-                nc.scalar.copy(out=dst, in_=src)
+            copy(eng, dst.rearrange("p t (n i) j -> p n t i j", i=2), src.rearrange("p t (n i) j -> p n t i j", i=2))
 
         def w_q(nm):
             nc.vector.quantize_mx(out=wc[nm][:].bitcast(FP8X4), scales=ws[nm][:], in_=wg[nm][:])
@@ -138,30 +147,28 @@ def tile_radixsplitattentionpointwise_x1_kernel(tc, x, w, bias, gs, wa, ba, out_
         du = {}
         mm = {}
         for c in range(NCH):
-            du[c] = big("du%d" % c, [128, 4, 4, 2, 64], F32)
-            mm[c] = big("mm%d" % c, [128, 4, 4, 64], F32)
+            du[c] = big("du%d" % c, [128, 4, N, 2, CB], F32)
+            mm[c] = big("mm%d" % c, [128, 4, N, CB], F32)
 
-        def mx1(r, c, i):
-            y[r, c, i] = pp.tile([128, 2, 4, 64], F32, name="y%d%d%d" % (r, c, i), tag="y", bufs=4)
-            for k in range(2):
-                t = 2 * i + k
-                nc.tensor.matmul_mx(
-                    out=y[r, c, i][:, k].rearrange("p g q -> p (g q)"),
-                    lhsT=wc["w%d" % r][:, 128 * t : 128 * (t + 1)].bitcast(FP8X4),
-                    lhsT_scale=ws["w%d" % r][:, 128 * t : 128 * (t + 1)],
-                    rhs=xc[r, c][:].bitcast(FP8X4),
-                    rhs_scale=xsc[r, c][:],
-                    start=True,
-                    stop=True,
-                )
+        def mx1(r, c, t):
+            y[r, c, t] = pp.tile([128, N, CB], F32, name="y%d%d%d" % (r, c, t), tag="ps", bufs=8)
+            nc.tensor.matmul_mx(
+                out=y[r, c, t][:].rearrange("p g b -> p (g b)"),
+                lhsT=wc["w%d" % r][:, 128 * t : 128 * (t + 1)].bitcast(FP8X4),
+                lhsT_scale=ws["w%d" % r][:, 128 * t : 128 * (t + 1)],
+                rhs=xc[r, c][:].bitcast(FP8X4),
+                rhs_scale=xsc[r, c][:],
+                start=True,
+                stop=True,
+            )
 
         def relu1(c, t):
-            nc.scalar.activation(out=du[c][:, t, :, 1, :], in_=y[1, c, t // 2][:, t % 2], func=AF.Relu, bias=biasc[:, 1, t : t + 1])
+            nc.scalar.activation(out=du[c][:, t, :, 1, :], in_=y[1, c, t][:], func=AF.Relu, bias=biasc[:, 1, t : t + 1])
 
         def diff0(c, t):
             nc.vector.scalar_tensor_tensor(
                 out=du[c][:, t, :, 0, :],
-                in0=y[0, c, t // 2][:, t % 2],
+                in0=y[0, c, t][:],
                 scalar=nb0[:, t : t + 1],
                 in1=du[c][:, t, :, 1, :],
                 op0=MAX,
@@ -173,27 +180,27 @@ def tile_radixsplitattentionpointwise_x1_kernel(tc, x, w, bias, gs, wa, ba, out_
         pss = {}
 
         def sum_t(c, t):
-            if t == 0:
-                pst[c] = pp.tile([128, 4, 128], F32, name="pst%d" % c, tag="st", bufs=1)
-            for g in range(4):
+            if t % 2 == 0:
+                pst[c, t // 2] = pp.tile([128, 2, 128], F32, name="pst%d%d" % (c, t // 2), tag="ps", bufs=8)
+            for g in range(N):
                 nc.tensor.matmul(
-                    out=pst[c][:, t, :],
-                    lhsT=du[c][:, t, g].rearrange("p a q -> p (a q)"),
+                    out=pst[c, t // 2][:, t % 2, :],
+                    lhsT=du[c][:, t, g].rearrange("p a b -> p (a b)"),
                     rhs=identf[:],
                     start=(g == 0),
-                    stop=(g == 3),
+                    stop=(g == N - 1),
                     is_transpose=True,
                 )
 
-        def sum_cp(c):
-            ut[c] = big("ut%d" % c, [128, 4, 128], F32)
-            nc.scalar.copy(out=ut[c][:], in_=pst[c][:])
+        def sum_cp(c, i, eng):
+            ut[c, i] = big("ut%d%d" % (c, i), [128, 2, 128], F32)
+            copy(eng, ut[c, i][:], pst[c, i][:])
 
         def sum_g(c):
-            pss[c] = pp.tile([128, 4, CB], F32, name="pss%d" % c, tag="tp", bufs=2)
+            pss[c] = pp.tile([128, 4, CB], F32, name="pss%d" % c, tag="ps", bufs=8)
             for t in range(4):
                 nc.tensor.matmul(out=pss[c][:, t, :], lhsT=identb[:], rhs=b0x8[:, t, :], start=True, stop=False)
-                nc.tensor.matmul(out=pss[c][:, t, :], lhsT=ut[c][:, t, :], rhs=grp[:], start=False, stop=True)
+                nc.tensor.matmul(out=pss[c][:, t, :], lhsT=ut[c, t // 2][:, t % 2, :], rhs=fold[:], start=False, stop=True)
 
         sgb = {}
         lps = {}
@@ -206,12 +213,13 @@ def tile_radixsplitattentionpointwise_x1_kernel(tc, x, w, bias, gs, wa, ba, out_
             )
 
         def sg_q(c):
+            cols = slice(CB * c, CB * (c + 1))
             nc.vector.quantize_mx(
-                out=sgc[:, 0:CB].bitcast(FP8X4), scales=sgs[:, 0:CB], in_=sgb[c][:].rearrange("p b t -> p (b t)")
+                out=sgc[:, cols].bitcast(FP8X4), scales=sgs[:, cols], in_=sgb[c][:].rearrange("p b t -> p (b t)")
             )
 
         def mx2(c):
-            lps[c] = pp.tile([128, 4, B], F32, name="l%d" % c, tag="ch", bufs=1)
+            lps[c] = pp.tile([128, 4, B], F32, name="l%d" % c, tag="ps", bufs=8)
             for t in range(4):
                 for i, nm in enumerate(("a0", "a1")):
                     nc.tensor.matmul_mx(
@@ -225,13 +233,10 @@ def tile_radixsplitattentionpointwise_x1_kernel(tc, x, w, bias, gs, wa, ba, out_
                     )
 
         def sigm(c):
-            a0[c] = big("a0g%d" % c, [128, 4, CB, 2], F32)
+            a0[c] = big("a0g%d" % c, [128, 4, CB], F32)
             for t in range(4):
                 nc.scalar.activation(
-                    out=a0[c][:, t],
-                    in_=lps[c][:, t, 0:CB].unsqueeze(2).to_broadcast([128, CB, 2]),
-                    func=AF.Sigmoid,
-                    bias=bd[:, t : t + 1],
+                    out=a0[c][:, t], in_=lps[c][:, t, CB * c : CB * (c + 1)], func=AF.Sigmoid, bias=bd[:, t : t + 1]
                 )
 
         oo = {}
@@ -239,186 +244,225 @@ def tile_radixsplitattentionpointwise_x1_kernel(tc, x, w, bias, gs, wa, ba, out_
         oc = {}
         ot = {}
         ops = {}
-        for s in range(4):
-            oo[s] = big("oo%d" % s, [128, 2, 4, 128], F32)
-            ob[s] = big("ob%d" % s, [128, CH * 4], BF16)
-            oc[s] = big("oc%d" % s, [128, CH], U32)
-            ot[s] = big("ot%d" % s, [128, 2, 128, 4], F32)
+        for c in range(NCH):
+            oo[c] = big("oo%d" % c, [128, 4, 4, 128], F32)
+            ob[c] = big("ob%d" % c, [128, CH * 4], BF16)
+            oc[c] = big("oc%d" % c, [128, CH], U32)
+            ot[c] = big("ot%d" % c, [128, 4, 128, 4], F32)
         osc = big("osc", [128, T], U8)
 
-        def mul_a(c, t):
+        def mul_a(c, t, j0, j1):
             nc.vector.scalar_tensor_tensor(
-                out=mm[c][:, t],
-                in0=du[c][:, t, :, 0, :],
+                out=mm[c][:, t, 2 * j0 : 2 * j1],
+                in0=du[c][:, t, 2 * j0 : 2 * j1, 0, :],
                 scalar=biasc[:, 0, t : t + 1],
-                in1=a0[c][:, t].rearrange("p b i -> p (b i)").unsqueeze(1).to_broadcast([128, 4, 64]),
+                in1=a0[c][:, t].unsqueeze(1).to_broadcast([128, 2 * (j1 - j0), CB]),
                 op0=ADD,
                 op1=MUL,
             )
 
         def o_add(c, j):
             nc.vector.tensor_add(
-                out=oo[c][:, j].rearrange("p t (q k) -> p t q k", k=2),
-                in0=mm[c][:].rearrange("p t (k j) q -> p j t q k", j=2)[:, j],
-                in1=du[c][:, :, :, 1, :].rearrange("p t (k j) q -> p j t q k", j=2)[:, j],
+                out=oo[c][:, j].rearrange("p t (b h) -> p t b h", h=2),
+                in0=mm[c][:, :, 2 * j : 2 * j + 2].rearrange("p t h b -> p t b h"),
+                in1=du[c][:, :, 2 * j : 2 * j + 2, 1, :].rearrange("p t h b -> p t b h"),
             )
 
-        def o_bf(s, eng):
-            dst = ob[s][:].rearrange("p (q i k) -> p q k i", i=2, k=8)
-            src = oo[s][:].rearrange("p j t q -> p (j t) q").rearrange("p k (q i) -> p q k i", i=2)
-            if eng is nc.vector:
-                nc.vector.tensor_copy(out=dst, in_=src)
-            else:
-                nc.scalar.copy(out=dst, in_=src)
+        def o_bf(c, k, q0, q1, eng):
+            dst = ob[c][:].rearrange("p (g i k e) -> p k g e i", i=2, k=2, e=8)[:, k, 32 * q0 : 32 * q1]
+            src = oo[c][:, 2 * k : 2 * k + 2].rearrange("p j t (g i) -> p g (j t) i", i=2)[:, 32 * q0 : 32 * q1]
+            copy(eng, dst, src)
 
-        def o_q(s):
-            nc.vector.quantize_mx(out=oc[s][:].bitcast(FP8X4), scales=osc[:, CH * s : CH * (s + 1)], in_=ob[s][:])
+        def o_q(c, q0, q1):
+            nc.vector.quantize_mx(
+                out=oc[c][:, 256 * q0 : 256 * q1].bitcast(FP8X4),
+                scales=osc[:, CH * c + 256 * q0 : CH * c + 256 * q1],
+                in_=ob[c][:, 1024 * q0 : 1024 * q1],
+            )
 
-        def o_tr(s, j):
-            ps = pp.tile([128, 4, 128], F32, name="o%d%d" % (s, j), tag="y", bufs=4)
-            ops[s, j] = ps
+        def o_tr(c, j):
+            ps = pp.tile([128, 4, 128], F32, name="o%d%d" % (c, j), tag="ps", bufs=8)
+            ops[c, j] = ps
             for t in range(4):
-                nc.tensor.transpose(ps[:, t, :], oo[s][:, j, t, :], identf[:])
+                nc.tensor.transpose(ps[:, t, :], oo[c][:, j, t, :], identf[:])
 
-        def o_cp(s, j):
-            nc.scalar.copy(out=ot[s][:, j], in_=ops[s, j][:].rearrange("q t p -> q p t"))
+        def o_cp(c, j, eng):
+            copy(eng, ot[c][:, j], ops[c, j][:].rearrange("q t p -> q p t"))
 
-        rows = out_0.rearrange("b n e -> (b n) e").rearrange("(s q j) e -> s q j e", s=4, j=2)
+        rows = out_0.rearrange("b n e -> (b n) e").rearrange("(c q j) e -> c q j e", c=NCH, j=4)
         words = out_1.rearrange("g p m t -> (g p) (m t)").bitcast(I32)
         srows = out_2.rearrange("g q m -> (g q) m").bitcast(I32)
 
-        def o_st(s, j):
-            nc.sync.dma_start(out=rows[s, :, j, :], in_=ot[s][:, j].rearrange("q p t -> q (p t)"))
+        def o_st(c, j0, j1, queue):
+            queue.dma_start(
+                out=rows[c, :, j0:j1, :].rearrange("q j e -> q (j e)"), in_=ot[c][:, j0:j1].rearrange("q j p t -> q (j p t)")
+            )
 
-        def w_st(s):
-            nc.sync.dma_start(out=words[:, CH * s : CH * (s + 1)], in_=oc[s][:].bitcast(I32))
+        def w_st(c, q0, q1):
+            nc.sync.dma_start(
+                out=words[:, CH * c + 256 * q0 : CH * c + 256 * q1], in_=oc[c][:, 256 * q0 : 256 * q1].bitcast(I32)
+            )
 
-        def s_st():
+        def s_st(queue):
             for q in range(4):
-                nc.scalar.dma_start(out=srows[4 * q : 4 * q + 4, :], in_=osc[32 * q : 32 * q + 4, :].bitcast(I32))
+                queue.dma_start(out=srows[4 * q : 4 * q + 4, :], in_=osc[32 * q : 32 * q + 4, :].bitcast(I32))
 
-        V, S = nc.vector, nc.scalar
+        def x_turn(r, c, k, eng=S):
+            x_tr(r, c, k)
+            x_cp(r, c, k, eng)
 
-        def x_turn(r, c):
-            x_tr(r, c)
-            x_cp(r, c)
+        def warm(n):
+            wp = pp.tile([128, 512], F32, name="warm", tag="ps", bufs=8)
+            nc.tensor.matmul(out=wp[:, 0:n], lhsT=zeros[:, 0:128], rhs=zeros[:, 0:n], start=True, stop=True)
 
-        def first(c, i):
-            mx1(1, c, i)
-            relu1(c, 2 * i)
-            relu1(c, 2 * i + 1)
-
-        def second(c, i):
-            mx1(0, c, i)
-            diff0(c, 2 * i)
-            diff0(c, 2 * i + 1)
-
-        def weigh(c):
-            for t in range(4):
-                mul_a(c, t)
-
-        def turn_back(c):
-            for j in range(2):
-                o_tr(c, j)
-                o_cp(c, j)
-                o_st(c, j)
-
-        load_x(1, 0)
-        load_w("w1", 0, 64)
-        load_w("w1", 64, 128)
-        load_x(0, 0)
+        load_x(1, 0, 0)
+        load_x(1, 0, 1)
+        load_w("w1", 0, 128)
+        load_x(0, 0, 0)
         load_w("w0", 0, 128)
-        load_x(1, 1)
+        load_x(0, 0, 1)
+        load_x(1, 1, 0)
         load_w("a0", 0, 128)
-        load_x(0, 1)
+        load_x(1, 1, 1)
+        load_x(0, 1, 0)
         load_w("a1", 0, 128)
-        for c in range(2, NCH):
-            load_x(1, c)
-            load_x(0, c)
+        load_x(0, 1, 1)
+        load_gate_vectors()
 
-        x_turn(1, 0)
+        warm(512)
+        warm(256)
         consts_s()
-        w_cp("w1", 0, 0, 64, V)
-        w_cp("w1", 64, 64, 128, V)
-        x_q(1, 0)
+        x_turn(1, 0, 0)
+        x_turn(1, 0, 1)
+        warm(384)
+        w_cp("w1", 0, 0, 88, V)
+        w_cp("w1", 0, 88, 128, S)
+        x_turn(0, 0, 0, S)
+        warm(384)
+        x_q(1, 0, 0, 2)
         w_q("w1")
-        x_turn(0, 0)
         w_cp("w0", 0, 0, 96, V)
         w_cp("w0", 0, 96, 128, S)
-        first(0, 0)
+        x_tr(0, 0, 1)
+        mx1(1, 0, 0)
         mx1(1, 0, 1)
-        x_turn(1, 1)
-        relu1(0, 2)
-        relu1(0, 3)
-        x_q(0, 0)
-        consts_v()
+        x_cp(0, 0, 1, S)
+        relu1(0, 0)
+        relu1(0, 1)
         w_q("w0")
-        w_cp("a0", 0, 0, 128, V)
-        x_q(1, 1)
-        x_turn(0, 1)
+        x_q(0, 0, 0, 2)
+        for t in range(2, 4):
+            mx1(1, 0, t)
+            relu1(0, t)
+        x_tr(1, 1, 0)
+        w_cp("a0", 0, 0, 64, V)
+        mx1(0, 0, 0)
+        mx1(0, 0, 1)
+        x_cp(1, 1, 0, S)
+        x_turn(1, 1, 1, S)
+        mx1(0, 0, 2)
+        mx1(0, 0, 3)
+        x_turn(0, 1, 0, S)
+        diff0(0, 0)
+        diff0(0, 1)
+        diff0(0, 2)
+        x_q(1, 1, 0, 2)
+        diff0(0, 3)
+        w_cp("a0", 0, 64, 128, V)
+        sum_t(0, 0)
+        x_turn(0, 1, 1, S)
+        w_cp("a1", 0, 96, 128, S)
+        mx1(1, 1, 0)
+        mx1(1, 1, 1)
+        relu1(1, 0)
+        relu1(1, 1)
+        w_q("a0")
+        x_q(0, 1, 0, 2)
+        w_cp("a1", 0, 0, 96, V)
+        sum_t(0, 1)
+        sum_t(0, 2)
+        sum_cp(0, 0, S)
+        sum_t(0, 3)
+        sum_cp(0, 1, S)
+        mx1(1, 1, 2)
+        mx1(1, 1, 3)
+        relu1(1, 2)
+        relu1(1, 3)
+        consts_v()
+        w_q("a1")
+        mx1(0, 1, 0)
+        sum_g(0)
+        mx1(0, 1, 1)
+        mx1(0, 1, 2)
+        mx1(0, 1, 3)
+        diff0(1, 0)
+        sgate(0)
+        diff0(1, 1)
+        sg_q(0)
+        diff0(1, 2)
+        diff0(1, 3)
+        sum_t(1, 0)
+        mx2(0)
+        sigm(0)
+        sum_t(1, 1)
+        sum_cp(1, 0, S)
+        sum_t(1, 2)
+        sum_t(1, 3)
+        sum_cp(1, 1, S)
+        sum_g(1)
 
-        for c in range(NCH + 2):
-            gate = 1 <= c <= NCH
-            if c < NCH:
-                second(c, 0)
-                second(c, 1)
-            if c == 0:
-                x_q(0, 1)
-            if c + 1 < NCH:
-                first(c + 1, 0)
-                first(c + 1, 1)
-            if gate:
-                sum_g(c - 1)
-            if 3 <= c <= NCH:
-                o_bf(c - 3, S)
-            if c >= 2:
-                mul_a(c - 2, 0)
-                mul_a(c - 2, 1)
-            if gate:
-                sgate(c - 1)
-            if c == 0:
-                w_q("a0")
-                w_cp("a1", 0, 0, 128, V)
-            if c == 1:
-                w_q("a1")
-            if c >= 2:
-                mul_a(c - 2, 2)
-            if gate:
-                sg_q(c - 1)
-            if c == NCH:
-                turn_back(c - 3)
-                mx2(c - 1)
-                sigm(c - 1)
-            if c >= 2:
-                mul_a(c - 2, 3)
-            if c + 2 < NCH:
-                for r in (1, 0):
-                    x_turn(r, c + 2)
-                for r in (1, 0):
-                    x_q(r, c + 2)
-            if 3 <= c <= NCH:
-                o_q(c - 3)
-                w_st(c - 3)
-            if c >= 2:
-                o_add(c - 2, 0)
-                o_add(c - 2, 1)
-            if c < NCH:
-                for t in range(4):
-                    sum_t(c, t)
-                sum_cp(c)
-            if 1 <= c < NCH:
-                mx2(c - 1)
-                sigm(c - 1)
-            if c == NCH - 1:
-                turn_back(c - 3)
-            if c == NCH:
-                o_bf(c - 2, S)
-                turn_back(c - 2)
-        last = NCH - 1
-        o_q(last - 1)
-        w_st(last - 1)
-        o_bf(last, V)
-        turn_back(last)
-        o_q(last)
-        w_st(last)
-        s_st()
+        for t in range(4):
+            mul_a(0, t, 0, 2)
+        mul_a(0, 0, 2, 4)
+        o_add(0, 0)
+        o_add(0, 1)
+        sgate(1)
+        mul_a(0, 1, 2, 4)
+        sg_q(1)
+        mul_a(0, 2, 2, 4)
+        mul_a(0, 3, 2, 4)
+        o_tr(0, 0)
+        o_tr(0, 1)
+        mx2(1)
+        o_cp(0, 0, S)
+        o_cp(0, 1, S)
+        o_st(0, 0, 2, nc.sync)
+        sigm(1)
+        o_bf(0, 0, 0, 2, S)
+        o_add(0, 2)
+        o_add(0, 3)
+        warm(256)
+        o_tr(0, 2)
+        o_tr(0, 3)
+        warm(256)
+        o_cp(0, 2, S)
+        o_cp(0, 3, S)
+        o_st(0, 2, 4, nc.sync)
+        o_bf(0, 1, 0, 2, S)
+        for t in range(4):
+            mul_a(1, t, 0, 2)
+        mul_a(1, 0, 2, 4)
+        o_add(1, 0)
+        o_add(1, 1)
+        o_tr(1, 0)
+        o_tr(1, 1)
+        warm(256)
+        for t in range(1, 4):
+            mul_a(1, t, 2, 4)
+        o_q(0, 0, 2)
+        w_st(0, 0, 2)
+        o_cp(1, 0, S)
+        o_cp(1, 1, S)
+        o_st(1, 0, 2, nc.sync)
+        o_bf(1, 0, 0, 1, S)
+        for j in (2, 3):
+            o_add(1, j)
+        o_bf(1, 0, 1, 2, V)
+        o_bf(1, 1, 0, 2, V)
+        o_q(1, 0, 2)
+        for j in (2, 3):
+            o_tr(1, j)
+            o_cp(1, j, S)
+            o_st(1, j, j + 1, nc.sync)
+        w_st(1, 0, 2)
+        s_st(nc.scalar)

@@ -140,8 +140,14 @@ def tile_radixsplitattentionpointwise_x1_kernel(tc, x, w, bias, gs, wa, ba, out_
                 return
             copy(eng, dst.rearrange("p t (n i) j -> p n t i j", i=2), src.rearrange("p t (n i) j -> p n t i j", i=2))
 
-        def w_q(nm):
-            nc.vector.quantize_mx(out=wc[nm][:].bitcast(FP8X4), scales=ws[nm][:], in_=wg[nm][:])
+        def w_cpt(nm, t0, t1, eng):
+            dst = wg[nm][:].rearrange("p (t n i j) -> p n t i j", t=4, i=2, j=4)[:, :, t0:t1]
+            src = wr[nm, 0][:].rearrange("p j (n i t) -> p n t i j", i=2, t=4)[:, :, t0:t1]
+            copy(eng, dst, src)
+
+        def w_q(nm, t0=0, t1=4):
+            cols = slice(128 * t0, 128 * t1)
+            nc.vector.quantize_mx(out=wc[nm][:, cols].bitcast(FP8X4), scales=ws[nm][:, cols], in_=wg[nm][:, 512 * t0 : 512 * t1])
 
         y = {}
         du = {}
@@ -162,8 +168,13 @@ def tile_radixsplitattentionpointwise_x1_kernel(tc, x, w, bias, gs, wa, ba, out_
                 stop=True,
             )
 
-        def relu1(c, t):
-            nc.scalar.activation(out=du[c][:, t, :, 1, :], in_=y[1, c, t][:], func=AF.Relu, bias=biasc[:, 1, t : t + 1])
+        def relu1(c, t, eng=S):
+            if eng is nc.vector:
+                nc.vector.tensor_scalar(
+                    out=du[c][:, t, :, 1, :], in0=y[1, c, t][:], scalar1=biasc[:, 1, t : t + 1], scalar2=0.0, op0=ADD, op1=MAX
+                )
+            else:
+                nc.scalar.activation(out=du[c][:, t, :, 1, :], in_=y[1, c, t][:], func=AF.Relu, bias=biasc[:, 1, t : t + 1])
 
         def diff0(c, t):
             nc.vector.scalar_tensor_tensor(
@@ -179,28 +190,32 @@ def tile_radixsplitattentionpointwise_x1_kernel(tc, x, w, bias, gs, wa, ba, out_
         ut = {}
         pss = {}
 
-        def sum_t(c, t):
-            if t % 2 == 0:
-                pst[c, t // 2] = pp.tile([128, 2, 128], F32, name="pst%d%d" % (c, t // 2), tag="ps", bufs=8)
+        def sum_bank(c, t0, t1):
+            bank = pp.tile([128, t1 - t0, 128], F32, name="pst%d%d" % (c, t0), tag="ps", bufs=8)
+            rows_sb = big("ut%d%d" % (c, t0), [128, t1 - t0, 128], F32)
+            pst[c, t0] = (bank, rows_sb)
+            for t in range(t0, t1):
+                ut[c, t] = (bank[:, t - t0, :], rows_sb[:, t - t0, :])
+
+        def sum_t(c, t, plain=0):
             for g in range(N):
                 nc.tensor.matmul(
-                    out=pst[c, t // 2][:, t % 2, :],
+                    out=ut[c, t][0],
                     lhsT=du[c][:, t, g].rearrange("p a b -> p (a b)"),
                     rhs=identf[:],
                     start=(g == 0),
                     stop=(g == N - 1),
-                    is_transpose=True,
+                    is_transpose=(g >= plain),
                 )
 
-        def sum_cp(c, i, eng):
-            ut[c, i] = big("ut%d%d" % (c, i), [128, 2, 128], F32)
-            copy(eng, ut[c, i][:], pst[c, i][:])
+        def sum_cp(c, t0):
+            nc.scalar.copy(out=pst[c, t0][1][:], in_=pst[c, t0][0][:])
 
         def sum_g(c):
             pss[c] = pp.tile([128, 4, CB], F32, name="pss%d" % c, tag="ps", bufs=8)
             for t in range(4):
                 nc.tensor.matmul(out=pss[c][:, t, :], lhsT=identb[:], rhs=b0x8[:, t, :], start=True, stop=False)
-                nc.tensor.matmul(out=pss[c][:, t, :], lhsT=ut[c, t // 2][:, t % 2, :], rhs=fold[:], start=False, stop=True)
+                nc.tensor.matmul(out=pss[c][:, t, :], lhsT=ut[c, t][1], rhs=fold[:], start=False, stop=True)
 
         sgb = {}
         lps = {}
@@ -219,11 +234,12 @@ def tile_radixsplitattentionpointwise_x1_kernel(tc, x, w, bias, gs, wa, ba, out_
             )
 
         def mx2(c):
-            lps[c] = pp.tile([128, 4, B], F32, name="l%d" % c, tag="ps", bufs=8)
             for t in range(4):
+                if t % 2 == 0:
+                    lps[c, t // 2] = pp.tile([128, 2, B], F32, name="l%d%d" % (c, t // 2), tag="ps", bufs=8)
                 for i, nm in enumerate(("a0", "a1")):
                     nc.tensor.matmul_mx(
-                        out=lps[c][:, t, :],
+                        out=lps[c, t // 2][:, t % 2, :],
                         lhsT=wc[nm][:, 128 * t : 128 * (t + 1)].bitcast(FP8X4),
                         lhsT_scale=ws[nm][:, 128 * t : 128 * (t + 1)],
                         rhs=sgc[:].bitcast(FP8X4),
@@ -236,7 +252,10 @@ def tile_radixsplitattentionpointwise_x1_kernel(tc, x, w, bias, gs, wa, ba, out_
             a0[c] = big("a0g%d" % c, [128, 4, CB], F32)
             for t in range(4):
                 nc.scalar.activation(
-                    out=a0[c][:, t], in_=lps[c][:, t, CB * c : CB * (c + 1)], func=AF.Sigmoid, bias=bd[:, t : t + 1]
+                    out=a0[c][:, t],
+                    in_=lps[c, t // 2][:, t % 2, CB * c : CB * (c + 1)],
+                    func=AF.Sigmoid,
+                    bias=bd[:, t : t + 1],
                 )
 
         oo = {}
@@ -319,96 +338,96 @@ def tile_radixsplitattentionpointwise_x1_kernel(tc, x, w, bias, gs, wa, ba, out_
         load_x(1, 0, 1)
         load_w("w1", 0, 128)
         load_x(0, 0, 0)
-        load_w("w0", 0, 128)
         load_x(0, 0, 1)
+        load_w("w0", 0, 128)
         load_x(1, 1, 0)
-        load_w("a0", 0, 128)
         load_x(1, 1, 1)
+        load_w("a0", 0, 128)
         load_x(0, 1, 0)
-        load_w("a1", 0, 128)
         load_x(0, 1, 1)
+        load_w("a1", 0, 128)
         load_gate_vectors()
 
         warm(512)
-        warm(256)
         consts_s()
         x_turn(1, 0, 0)
         x_turn(1, 0, 1)
-        warm(384)
-        w_cp("w1", 0, 0, 88, V)
-        w_cp("w1", 0, 88, 128, S)
+        warm(256)
+
+        w_cpt("w1", 0, 2, V)
+        w_cpt("w1", 3, 4, S)
         x_turn(0, 0, 0, S)
-        warm(384)
+        x_turn(0, 0, 1, S)
+        warm(256)
+        w_cpt("w1", 2, 3, V)
+        w_q("w1", 0, 2)
         x_q(1, 0, 0, 2)
-        w_q("w1")
-        w_cp("w0", 0, 0, 96, V)
-        w_cp("w0", 0, 96, 128, S)
-        x_tr(0, 0, 1)
-        mx1(1, 0, 0)
-        mx1(1, 0, 1)
-        x_cp(0, 0, 1, S)
-        relu1(0, 0)
-        relu1(0, 1)
-        w_q("w0")
-        x_q(0, 0, 0, 2)
-        for t in range(2, 4):
+        w_q("w1", 2, 4)
+        w_cpt("w0", 0, 2, V)
+        w_cpt("w0", 3, 4, S)
+        for t in range(4):
             mx1(1, 0, t)
             relu1(0, t)
-        x_tr(1, 1, 0)
+        w_cpt("w0", 2, 3, V)
+        w_q("w0", 0, 2)
+        x_q(0, 0, 0, 2)
+        w_q("w0", 2, 4)
         w_cp("a0", 0, 0, 64, V)
-        mx1(0, 0, 0)
-        mx1(0, 0, 1)
-        x_cp(1, 1, 0, S)
+        x_turn(1, 1, 0, S)
         x_turn(1, 1, 1, S)
-        mx1(0, 0, 2)
-        mx1(0, 0, 3)
+        for t in range(4):
+            mx1(0, 0, t)
         x_turn(0, 1, 0, S)
-        diff0(0, 0)
-        diff0(0, 1)
-        diff0(0, 2)
-        x_q(1, 1, 0, 2)
-        diff0(0, 3)
-        w_cp("a0", 0, 64, 128, V)
-        sum_t(0, 0)
         x_turn(0, 1, 1, S)
-        w_cp("a1", 0, 96, 128, S)
-        mx1(1, 1, 0)
-        mx1(1, 1, 1)
-        relu1(1, 0)
-        relu1(1, 1)
-        w_q("a0")
-        x_q(0, 1, 0, 2)
-        w_cp("a1", 0, 0, 96, V)
+        for t in range(4):
+            diff0(0, t)
+        x_q(1, 1, 0, 2)
+        w_cp("a0", 0, 64, 128, V)
+        sum_bank(0, 0, 2)
+        sum_t(0, 0, 1)
         sum_t(0, 1)
-        sum_t(0, 2)
-        sum_cp(0, 0, S)
+        w_cp("a1", 0, 32, 128, S)
+        sum_cp(0, 0)
+        sum_bank(0, 2, 4)
+        sum_t(0, 2, 1)
         sum_t(0, 3)
-        sum_cp(0, 1, S)
-        mx1(1, 1, 2)
-        mx1(1, 1, 3)
-        relu1(1, 2)
-        relu1(1, 3)
+        sum_cp(0, 2)
+        x_q(0, 1, 0, 2)
+        w_q("a0")
+        w_cp("a1", 0, 0, 32, V)
         consts_v()
         w_q("a1")
+
+
+        mx1(1, 1, 0)
+        mx1(1, 1, 1)
         mx1(0, 1, 0)
+        mx1(1, 1, 2)
+        relu1(1, 0)
+        relu1(1, 1)
         sum_g(0)
         mx1(0, 1, 1)
+        mx1(1, 1, 3)
         mx1(0, 1, 2)
         mx1(0, 1, 3)
+        relu1(1, 2)
+        relu1(1, 3)
         diff0(1, 0)
         sgate(0)
         diff0(1, 1)
         sg_q(0)
         diff0(1, 2)
         diff0(1, 3)
+        sum_bank(1, 0, 2)
         sum_t(1, 0)
         mx2(0)
         sigm(0)
         sum_t(1, 1)
-        sum_cp(1, 0, S)
+        sum_cp(1, 0)
+        sum_bank(1, 2, 4)
         sum_t(1, 2)
         sum_t(1, 3)
-        sum_cp(1, 1, S)
+        sum_cp(1, 2)
         sum_g(1)
 
         for t in range(4):
@@ -416,22 +435,22 @@ def tile_radixsplitattentionpointwise_x1_kernel(tc, x, w, bias, gs, wa, ba, out_
         mul_a(0, 0, 2, 4)
         o_add(0, 0)
         o_add(0, 1)
-        sgate(1)
         mul_a(0, 1, 2, 4)
-        sg_q(1)
         mul_a(0, 2, 2, 4)
+        sgate(1)
         mul_a(0, 3, 2, 4)
+        sg_q(1)
+        o_add(0, 2)
+        o_add(0, 3)
         o_tr(0, 0)
         o_tr(0, 1)
+        warm(256)
         mx2(1)
         o_cp(0, 0, S)
         o_cp(0, 1, S)
         o_st(0, 0, 2, nc.sync)
         sigm(1)
-        o_bf(0, 0, 0, 2, S)
-        o_add(0, 2)
-        o_add(0, 3)
-        warm(256)
+        o_bf(0, 0, 0, 2, V)
         o_tr(0, 2)
         o_tr(0, 3)
         warm(256)
@@ -451,18 +470,24 @@ def tile_radixsplitattentionpointwise_x1_kernel(tc, x, w, bias, gs, wa, ba, out_
             mul_a(1, t, 2, 4)
         o_q(0, 0, 2)
         w_st(0, 0, 2)
-        o_cp(1, 0, S)
-        o_cp(1, 1, S)
-        o_st(1, 0, 2, nc.sync)
         o_bf(1, 0, 0, 1, S)
+        o_cp(1, 0, S)
+        o_st(1, 0, 1, nc.sync)
+        o_cp(1, 1, S)
+        o_st(1, 1, 2, nc.sync)
+        o_bf(1, 0, 1, 2, S)
         for j in (2, 3):
             o_add(1, j)
-        o_bf(1, 0, 1, 2, V)
-        o_bf(1, 1, 0, 2, V)
-        o_q(1, 0, 2)
-        for j in (2, 3):
-            o_tr(1, j)
-            o_cp(1, j, S)
-            o_st(1, j, j + 1, nc.sync)
-        w_st(1, 0, 2)
-        s_st(nc.scalar)
+        o_bf(1, 1, 0, 1, V)
+        o_bf(1, 1, 1, 2, V)
+        o_q(1, 0, 1)
+        o_q(1, 1, 2)
+        o_tr(1, 2)
+        o_cp(1, 2, S)
+        w_st(1, 0, 1)
+        o_st(1, 2, 3, nc.sync)
+        w_st(1, 1, 2)
+        o_tr(1, 3)
+        o_cp(1, 3, S)
+        o_st(1, 3, 4, nc.scalar)
+        s_st(nc.sync)

@@ -22,6 +22,8 @@ FLOPS = 2 * R * T * C * E + 2 * R * B * E * E
 CB = 64
 CH = CB * N
 NCH = B // CB
+BANKS = 8
+WARM = 256
 
 
 def tile_radixsplitattentionpointwise_x1_kernel(tc, x, w, bias, gs, wa, ba, out_0, out_1, out_2):
@@ -32,462 +34,458 @@ def tile_radixsplitattentionpointwise_x1_kernel(tc, x, w, bias, gs, wa, ba, out_
         ctx.enter_context(tc.manual_schedule())
         V, S = nc.vector, nc.scalar
 
-        def big(name, shape, dtype):
+        def sbuf(name, shape, dtype):
             return sb.tile(shape, dtype, name=name, align_bytes=64)
 
-        biasc = big("biasc", [128, 2, 16], BF16)
-        bac = big("bac", [128, 2, 16], BF16)
-        gsc = big("gsc", [128, 16], BF16)
-        nc.scalar.dma_start(out=biasc[:, :, 0:4], in_=bias.rearrange("r (p t) -> p r t", t=4))
-        zeros = big("zeros", [128, 512], F32)
-        nc.vector.memset(zeros[:], 0.0)
-        half = big("half", [128, 1], F32)
-        nc.scalar.activation(out=half[:], in_=zeros[:, 0:1], func=AF.Sigmoid)
-
-        identf = big("identf", [128, 128], F32)
-        make_identity(nc, identf[:])
-        identb = big("identb", [128, 128], BF16)
-        nc.vector.tensor_copy(out=identb[:], in_=identf[:])
-        fold = big("fold", [128, CB], F32)
-        nc.vector.scalar_tensor_tensor(out=fold[:], in0=identf[:, 64:128], scalar=2.0, in1=identf[:, 0:64], op0=MUL, op1=ADD)
-        sgc = big("sgc", [128, B], U32)
-        sgs = big("sgs", [128, B], U8)
-        nc.gpsimd.memset(sgc[:], 0)
-        nc.gpsimd.memset(sgs[:].bitcast(U32), 0)
-
-        nb0 = big("nb0", [128, 4], F32)
-        b0x8 = big("b0x8", [128, 4, CB], BF16)
-        gs8 = big("gs8", [128, 4], F32)
-        bd = big("bd", [128, 4], F32)
-
-        def consts_s():
-            nc.scalar.activation(out=nb0[:], in_=biasc[:, 0, 0:4], func=AF.Copy, scale=-1.0)
-            nc.scalar.activation(
-                out=b0x8[:], in_=biasc[:, 0, 0:4].unsqueeze(2).to_broadcast([128, 4, CB]), func=AF.Copy, scale=8.0
-            )
-
-        def load_gate_vectors():
-            nc.sync.dma_start(out=gsc[:, 0:4], in_=gs.rearrange("(p t) -> p t", t=4))
-            nc.sync.dma_start(out=bac[:, :, 0:4], in_=ba.rearrange("r (p t) -> p r t", t=4))
-
-        def consts_v():
-            nc.vector.tensor_scalar(out=gs8[:], in0=gsc[:, 0:4], scalar1=half[:], scalar2=0.25, op0=MUL, op1=MUL)
-            nc.vector.tensor_sub(out=bd[:], in0=bac[:, 0, 0:4], in1=bac[:, 1, 0:4])
+        def bank(name, shape):
+            return pp.tile(shape, F32, name=name, tag="bank", bufs=BANKS)
 
         def copy(eng, dst, src):
-            if eng is nc.vector:
+            if eng is V:
                 nc.vector.tensor_copy(out=dst, in_=src)
             else:
                 nc.scalar.copy(out=dst, in_=src)
 
-        xs = {}
-        xg = {}
-        xc = {}
-        xsc = {}
-        xt = {}
-        for c in range(NCH):
-            for r in range(R):
-                xg[r, c] = big("xg%d%d" % (r, c), [128, 4 * CH], BF16)
-                xc[r, c] = big("xc%d%d" % (r, c), [128, CH], U32)
-                xsc[r, c] = big("xsc%d%d" % (r, c), [128, CH], U8)
-                for k in range(2):
-                    xs[r, c, k] = big("xs%d%d%d" % (r, c, k), [128, 1024], BF16)
+        bias_c = sbuf("bias_c", [128, 2, 16], BF16)
+        ba_c = sbuf("ba_c", [128, 2, 16], BF16)
+        gs_c = sbuf("gs_c", [128, 16], BF16)
+        nc.scalar.dma_start(out=bias_c[:, :, 0:4], in_=bias.rearrange("r (p t) -> p r t", t=4))
+        zeros = sbuf("zeros", [128, 2 * WARM], F32)
+        nc.vector.memset(zeros[:], 0.0)
+        half = sbuf("half", [128, 1], F32)
+        nc.scalar.activation(out=half[:], in_=zeros[:, 0:1], func=AF.Sigmoid)
 
-        def load_x(r, c, k):
-            rows = x[r, CB * c : CB * (c + 1)].rearrange("b n c -> (b n) c").rearrange("(q k j) c -> k q (j c)", k=2, j=2)
-            nc.sync.dma_start(out=xs[r, c, k][:], in_=rows[k])
+        ident = sbuf("ident", [128, 128], F32)
+        make_identity(nc, ident[:])
+        ident_bf = sbuf("ident_bf", [128, 128], BF16)
+        nc.vector.tensor_copy(out=ident_bf[:], in_=ident[:])
+        fold_du = sbuf("fold_du", [128, CB], F32)
+        nc.vector.scalar_tensor_tensor(out=fold_du[:], in0=ident[:, CB:128], scalar=2.0, in1=ident[:, 0:CB], op0=MUL, op1=ADD)
+        fold_pair = sbuf("fold_pair", [128, CB], F32)
+        nc.vector.tensor_add(out=fold_pair[:], in0=ident[:, CB:128], in1=ident[:, 0:CB])
+        sg_codes = sbuf("sg_codes", [128, B], U32)
+        sg_scales = sbuf("sg_scales", [128, B], U8)
+        nc.gpsimd.memset(sg_codes[:], 0)
+        nc.gpsimd.memset(sg_scales[:].bitcast(U32), 0)
 
-        def x_tr(r, c, k):
-            ps = pp.tile([128, 2, 2, 128], F32, name="xt%d%d%d" % (r, c, k), tag="ps", bufs=8)
-            xt[r, c, k] = ps
-            words = xs[r, c, k][:].bitcast(F32)
-            for j in range(2):
-                for u in range(2):
-                    nc.tensor.transpose(ps[:, j, u, :], words[:, 256 * j + u : 256 * (j + 1) : 2], identf[:])
+        neg_bias0 = sbuf("neg_bias0", [128, 4], F32)
+        bias0_sum = sbuf("bias0_sum", [128, 4, CB], BF16)
+        gain = sbuf("gain", [128, 4], F32)
+        ba_diff = sbuf("ba_diff", [128, 4], F32)
 
-        def x_cp(r, c, k, eng):
-            dst = xg[r, c][:, 1024 * k : 1024 * (k + 1)].bitcast(F32).rearrange("p (j h b u) -> p j h b u", j=2, h=2, u=2)
-            copy(eng, dst, xt[r, c, k][:].rearrange("p j u (b h) -> p j h b u", h=2))
-
-        def x_q(r, c, k0, k1):
-            cols = slice(256 * k0, 256 * k1)
-            nc.vector.quantize_mx(
-                out=xc[r, c][:, cols].bitcast(FP8X4), scales=xsc[r, c][:, cols], in_=xg[r, c][:, 1024 * k0 : 1024 * k1]
+        def bias_constants():
+            nc.scalar.activation(out=neg_bias0[:], in_=bias_c[:, 0, 0:4], func=AF.Copy, scale=-1.0)
+            nc.scalar.activation(
+                out=bias0_sum[:], in_=bias_c[:, 0, 0:4].unsqueeze(2).to_broadcast([128, 4, CB]), func=AF.Copy, scale=float(N)
             )
 
-        wsrc = {"w0": w[0], "w1": w[1], "a0": wa[0], "a1": wa[1]}
-        wr = {}
-        wg = {}
-        wc = {}
-        ws = {}
-        for nm in wsrc:
-            wg[nm] = big("wg" + nm, [128, 2048], BF16)
-            wc[nm] = big("wc" + nm, [128, 512], U32)
-            ws[nm] = big("ws" + nm, [128, 512], U8)
+        def load_gate_vectors():
+            nc.sync.dma_start(out=gs_c[:, 0:4], in_=gs.rearrange("(p t) -> p t", t=4))
+            nc.sync.dma_start(out=ba_c[:, :, 0:4], in_=ba.rearrange("r (p t) -> p r t", t=4))
 
-        def load_w(nm, m0, m1):
-            wr[nm, m0] = big("wr%s%d" % (nm, m0), [128, 4, 4 * (m1 - m0)], BF16)
-            nc.sync.dma_start(out=wr[nm, m0][:], in_=wsrc[nm].rearrange("(p j) c -> p j c", j=4)[:, :, 4 * m0 : 4 * m1])
+        def gate_constants():
+            nc.vector.tensor_scalar(out=gain[:], in0=gs_c[:, 0:4], scalar1=half[:], scalar2=2.0 / N, op0=MUL, op1=MUL)
+            nc.vector.tensor_sub(out=ba_diff[:], in0=ba_c[:, 0, 0:4], in1=ba_c[:, 1, 0:4])
 
-        def w_cp(nm, base, m0, m1, eng):
-            dst = wg[nm][:].rearrange("p (t m j) -> p t m j", t=4, j=4)[:, :, m0:m1]
-            src = wr[nm, base][:].rearrange("p j (m t) -> p t m j", t=4)[:, :, m0 - base : m1 - base]
-            if nm == "a1":
-                if eng is nc.vector:
-                    nc.vector.tensor_scalar(out=dst, in0=src, scalar1=-1.0, scalar2=None, op0=MUL)
-                else:
-                    nc.scalar.activation(out=dst, in_=src, func=AF.Copy, scale=-1.0)
-                return
-            copy(eng, dst.rearrange("p t (n i) j -> p n t i j", i=2), src.rearrange("p t (n i) j -> p n t i j", i=2))
+        def warm(columns):
+            scrap = bank("warm", [128, 2 * WARM])
+            nc.tensor.matmul(out=scrap[:, 0:columns], lhsT=zeros[:, 0:128], rhs=zeros[:, 0:columns], start=True, stop=True)
 
-        def w_cpt(nm, t0, t1, eng):
-            dst = wg[nm][:].rearrange("p (t n i j) -> p n t i j", t=4, i=2, j=4)[:, :, t0:t1]
-            src = wr[nm, 0][:].rearrange("p j (n i t) -> p n t i j", i=2, t=4)[:, :, t0:t1]
-            copy(eng, dst, src)
+        x_rows = {}
+        x_bf = {}
+        x_codes = {}
+        x_scales = {}
+        for c in range(NCH):
+            for r in range(R):
+                x_bf[r, c] = sbuf("x_bf%d%d" % (r, c), [128, 4 * CH], BF16)
+                x_codes[r, c] = sbuf("x_codes%d%d" % (r, c), [128, CH], U32)
+                x_scales[r, c] = sbuf("x_scales%d%d" % (r, c), [128, CH], U8)
 
-        def w_q(nm, t0=0, t1=4):
+        def load_x(r, c, k0, k1):
+            src = x[r, CB * c : CB * (c + 1)].rearrange("b n c -> (b n) c").rearrange("(q j) c -> q (j c)", j=4)
+            part = sbuf("x_rows%d%d%d" % (r, c, k0), [128, 2 * C * (k1 - k0)], BF16)
+            nc.sync.dma_start(out=part[:], in_=src[:, 2 * C * k0 : 2 * C * k1])
+            for k in range(k0, k1):
+                x_rows[r, c, k] = part[:, 2 * C * (k - k0) : 2 * C * (k - k0 + 1)]
+
+        def x_turn(r, c):
+            for k in range(2):
+                ps = bank("x_ps%d%d%d" % (r, c, k), [128, 2, 2, 128])
+                pairs = x_rows[r, c, k].bitcast(F32)
+                for j in range(2):
+                    for i in range(2):
+                        nc.tensor.transpose(ps[:, j, i, :], pairs[:, 256 * j + i : 256 * (j + 1) : 2], ident[:])
+                dst = x_bf[r, c][:, 2 * C * k : 2 * C * (k + 1)].bitcast(F32)
+                nc.scalar.copy(
+                    out=dst.rearrange("p (j h b i) -> p j h b i", j=2, h=2, i=2),
+                    in_=ps[:].rearrange("p j i (b h) -> p j h b i", h=2),
+                )
+
+        def x_quantise(r, c):
+            nc.vector.quantize_mx(out=x_codes[r, c][:].bitcast(FP8X4), scales=x_scales[r, c][:], in_=x_bf[r, c][:])
+
+        w_src = {"w0": w[0], "w1": w[1], "wa0": wa[0], "wa1": wa[1]}
+        w_rows = {}
+        w_bf = {}
+        w_codes = {}
+        w_scales = {}
+        for nm in w_src:
+            w_rows[nm] = sbuf("w_rows_" + nm, [128, 4, E], BF16)
+            w_bf[nm] = sbuf("w_bf_" + nm, [128, 4 * E], BF16)
+            w_codes[nm] = sbuf("w_codes_" + nm, [128, E], U32)
+            w_scales[nm] = sbuf("w_scales_" + nm, [128, E], U8)
+
+        def load_w(nm):
+            nc.sync.dma_start(out=w_rows[nm][:], in_=w_src[nm].rearrange("(p s) e -> p s e", s=4))
+
+        def w_views(nm):
+            dst = w_bf[nm][:].rearrange("p (t a i s) -> p a t i s", t=4, i=2, s=4)
+            src = w_rows[nm][:].rearrange("p s (a i t) -> p a t i s", i=2, t=4)
+            return dst, src
+
+        def w_lay_slices(nm, t0, t1, eng):
+            dst, src = w_views(nm)
+            copy(eng, dst[:, :, t0:t1], src[:, :, t0:t1])
+
+        def wa0_lay_half(i, eng):
+            dst, src = w_views("wa0")
+            copy(eng, dst[:, 32 * i : 32 * (i + 1)], src[:, 32 * i : 32 * (i + 1)])
+
+        def wa1_lay_half_negated(i, eng):
+            dst = w_bf["wa1"][:].rearrange("p (t m s) -> p t m s", t=4, s=4)[:, :, 64 * i : 64 * (i + 1)]
+            src = w_rows["wa1"][:].rearrange("p s (m t) -> p t m s", t=4)[:, :, 64 * i : 64 * (i + 1)]
+            if eng is V:
+                nc.vector.tensor_scalar(out=dst, in0=src, scalar1=-1.0, scalar2=None, op0=MUL)
+            else:
+                nc.scalar.activation(out=dst, in_=src, func=AF.Copy, scale=-1.0)
+
+        def w_quantise(nm, t0, t1):
             cols = slice(128 * t0, 128 * t1)
-            nc.vector.quantize_mx(out=wc[nm][:, cols].bitcast(FP8X4), scales=ws[nm][:, cols], in_=wg[nm][:, 512 * t0 : 512 * t1])
+            nc.vector.quantize_mx(
+                out=w_codes[nm][:, cols].bitcast(FP8X4), scales=w_scales[nm][:, cols], in_=w_bf[nm][:, 512 * t0 : 512 * t1]
+            )
+
+        def mx_pass(out, nm, t, codes, scales, start, stop):
+            cols = slice(128 * t, 128 * (t + 1))
+            nc.tensor.matmul_mx(
+                out=out,
+                lhsT=w_codes[nm][:, cols].bitcast(FP8X4),
+                lhsT_scale=w_scales[nm][:, cols],
+                rhs=codes[:].bitcast(FP8X4),
+                rhs_scale=scales[:],
+                start=start,
+                stop=stop,
+            )
 
         y = {}
         du = {}
-        mm = {}
         for c in range(NCH):
-            du[c] = big("du%d" % c, [128, 4, N, 2, CB], F32)
-            mm[c] = big("mm%d" % c, [128, 4, N, CB], F32)
+            du[c] = sbuf("du%d" % c, [128, 4, N, 2, CB], F32)
 
-        def mx1(r, c, t):
-            y[r, c, t] = pp.tile([128, N, CB], F32, name="y%d%d%d" % (r, c, t), tag="ps", bufs=8)
-            nc.tensor.matmul_mx(
-                out=y[r, c, t][:].rearrange("p g b -> p (g b)"),
-                lhsT=wc["w%d" % r][:, 128 * t : 128 * (t + 1)].bitcast(FP8X4),
-                lhsT_scale=ws["w%d" % r][:, 128 * t : 128 * (t + 1)],
-                rhs=xc[r, c][:].bitcast(FP8X4),
-                rhs_scale=xsc[r, c][:],
-                start=True,
-                stop=True,
-            )
+        def product(r, c, t):
+            y[r, c, t] = bank("y%d%d%d" % (r, c, t), [128, N, CB])
+            mx_pass(y[r, c, t][:].rearrange("p g b -> p (g b)"), "w%d" % r, t, x_codes[r, c], x_scales[r, c], True, True)
 
-        def relu1(c, t, eng=S):
-            if eng is nc.vector:
-                nc.vector.tensor_scalar(
-                    out=du[c][:, t, :, 1, :], in0=y[1, c, t][:], scalar1=biasc[:, 1, t : t + 1], scalar2=0.0, op0=ADD, op1=MAX
-                )
-            else:
-                nc.scalar.activation(out=du[c][:, t, :, 1, :], in_=y[1, c, t][:], func=AF.Relu, bias=biasc[:, 1, t : t + 1])
+        def relu1(c, t):
+            nc.scalar.activation(out=du[c][:, t, :, 1, :], in_=y[1, c, t][:], func=AF.Relu, bias=bias_c[:, 1, t : t + 1])
 
         def diff0(c, t):
             nc.vector.scalar_tensor_tensor(
                 out=du[c][:, t, :, 0, :],
                 in0=y[0, c, t][:],
-                scalar=nb0[:, t : t + 1],
+                scalar=neg_bias0[:, t : t + 1],
                 in1=du[c][:, t, :, 1, :],
                 op0=MAX,
                 op1=SUB,
             )
 
-        pst = {}
-        ut = {}
-        pss = {}
+        LAST = 3
+        sum_ps = {}
+        sum_sb = {}
+        last_sum = {}
+        s_ps = {}
 
-        def sum_bank(c, t0, t1):
-            bank = pp.tile([128, t1 - t0, 128], F32, name="pst%d%d" % (c, t0), tag="ps", bufs=8)
-            rows_sb = big("ut%d%d" % (c, t0), [128, t1 - t0, 128], F32)
-            pst[c, t0] = (bank, rows_sb)
-            for t in range(t0, t1):
-                ut[c, t] = (bank[:, t - t0, :], rows_sb[:, t - t0, :])
-
-        def sum_t(c, t, plain=0):
-            for g in range(N):
+        def add_up(out, blocks, first_plain):
+            for g, block in enumerate(blocks):
                 nc.tensor.matmul(
-                    out=ut[c, t][0],
-                    lhsT=du[c][:, t, g].rearrange("p a b -> p (a b)"),
-                    rhs=identf[:],
+                    out=out,
+                    lhsT=block,
+                    rhs=ident[:],
                     start=(g == 0),
-                    stop=(g == N - 1),
-                    is_transpose=(g >= plain),
+                    stop=(g == len(blocks) - 1),
+                    is_transpose=not (first_plain and g == 0),
                 )
 
-        def sum_cp(c, t0):
-            nc.scalar.copy(out=pst[c, t0][1][:], in_=pst[c, t0][0][:])
+        def pre_add_last(c):
+            last_sum[c] = sbuf("last_sum%d" % c, [128, N, CB], F32)
+            nc.vector.scalar_tensor_tensor(
+                out=last_sum[c][:], in0=du[c][:, LAST, :, 1, :], scalar=2.0, in1=du[c][:, LAST, :, 0, :], op0=MUL, op1=ADD
+            )
 
-        def sum_g(c):
-            pss[c] = pp.tile([128, 4, CB], F32, name="pss%d" % c, tag="ps", bufs=8)
+        def sum_slice(c, t, first_plain=False):
+            if t % 2 == 0:
+                sum_ps[c, t // 2] = bank("sum_ps%d%d" % (c, t // 2), [128, 2, 128])
+            if t == LAST:
+                blocks = [last_sum[c][:, g : g + 2].rearrange("p g b -> p (g b)") for g in range(0, N, 2)]
+            else:
+                blocks = [du[c][:, t, g].rearrange("p a b -> p (a b)") for g in range(N)]
+            add_up(sum_ps[c, t // 2][:, t % 2, :], blocks, first_plain)
+
+        def sum_out(c, i):
+            sum_sb[c, i] = sbuf("sum_sb%d%d" % (c, i), [128, 2, 128], F32)
+            nc.scalar.copy(out=sum_sb[c, i][:], in_=sum_ps[c, i][:])
+
+        def sum_fold(c):
+            s_ps[c] = bank("s_ps%d" % c, [128, 4, CB])
             for t in range(4):
-                nc.tensor.matmul(out=pss[c][:, t, :], lhsT=identb[:], rhs=b0x8[:, t, :], start=True, stop=False)
-                nc.tensor.matmul(out=pss[c][:, t, :], lhsT=ut[c, t][1], rhs=fold[:], start=False, stop=True)
+                fold = fold_pair if t == LAST else fold_du
+                nc.tensor.matmul(out=s_ps[c][:, t, :], lhsT=ident_bf[:], rhs=bias0_sum[:, t, :], start=True, stop=False)
+                nc.tensor.matmul(out=s_ps[c][:, t, :], lhsT=sum_sb[c, t // 2][:, t % 2, :], rhs=fold[:], start=False, stop=True)
 
-        sgb = {}
-        lps = {}
+        sg_bf = {}
+        l_ps = {}
         a0 = {}
 
-        def sgate(c):
-            sgb[c] = big("sgb%d" % c, [128, CB, 4], BF16)
+        def sg_round(c):
+            sg_bf[c] = sbuf("sg_bf%d" % c, [128, CB, 4], BF16)
             nc.vector.tensor_mul(
-                out=sgb[c][:], in0=pss[c][:].rearrange("p t b -> p b t"), in1=gs8[:].unsqueeze(1).to_broadcast([128, CB, 4])
+                out=sg_bf[c][:], in0=s_ps[c][:].rearrange("p t b -> p b t"), in1=gain[:].unsqueeze(1).to_broadcast([128, CB, 4])
             )
 
-        def sg_q(c):
+        def sg_quantise(c):
             cols = slice(CB * c, CB * (c + 1))
             nc.vector.quantize_mx(
-                out=sgc[:, cols].bitcast(FP8X4), scales=sgs[:, cols], in_=sgb[c][:].rearrange("p b t -> p (b t)")
+                out=sg_codes[:, cols].bitcast(FP8X4), scales=sg_scales[:, cols], in_=sg_bf[c][:].rearrange("p b t -> p (b t)")
             )
 
-        def mx2(c):
+        def logits(c):
             for t in range(4):
                 if t % 2 == 0:
-                    lps[c, t // 2] = pp.tile([128, 2, B], F32, name="l%d%d" % (c, t // 2), tag="ps", bufs=8)
-                for i, nm in enumerate(("a0", "a1")):
-                    nc.tensor.matmul_mx(
-                        out=lps[c, t // 2][:, t % 2, :],
-                        lhsT=wc[nm][:, 128 * t : 128 * (t + 1)].bitcast(FP8X4),
-                        lhsT_scale=ws[nm][:, 128 * t : 128 * (t + 1)],
-                        rhs=sgc[:].bitcast(FP8X4),
-                        rhs_scale=sgs[:],
-                        start=(i == 0),
-                        stop=(i == 1),
-                    )
+                    l_ps[c, t // 2] = bank("l_ps%d%d" % (c, t // 2), [128, 2, B])
+                mx_pass(l_ps[c, t // 2][:, t % 2, :], "wa0", t, sg_codes, sg_scales, True, False)
+                mx_pass(l_ps[c, t // 2][:, t % 2, :], "wa1", t, sg_codes, sg_scales, False, True)
 
-        def sigm(c):
-            a0[c] = big("a0g%d" % c, [128, 4, CB], F32)
+        def softmax(c):
+            a0[c] = sbuf("a0_%d" % c, [128, 4, CB], F32)
             for t in range(4):
                 nc.scalar.activation(
                     out=a0[c][:, t],
-                    in_=lps[c, t // 2][:, t % 2, CB * c : CB * (c + 1)],
+                    in_=l_ps[c, t // 2][:, t % 2, CB * c : CB * (c + 1)],
                     func=AF.Sigmoid,
-                    bias=bd[:, t : t + 1],
+                    bias=ba_diff[:, t : t + 1],
                 )
 
-        oo = {}
-        ob = {}
-        oc = {}
-        ot = {}
-        ops = {}
+        weighted = {}
+        res = {}
+        res_bf = {}
+        res_codes = {}
+        res_rows = {}
+        res_ps = {}
         for c in range(NCH):
-            oo[c] = big("oo%d" % c, [128, 4, 4, 128], F32)
-            ob[c] = big("ob%d" % c, [128, CH * 4], BF16)
-            oc[c] = big("oc%d" % c, [128, CH], U32)
-            ot[c] = big("ot%d" % c, [128, 4, 128, 4], F32)
-        osc = big("osc", [128, T], U8)
+            weighted[c] = sbuf("weighted%d" % c, [128, 4, N, CB], F32)
+            res[c] = sbuf("res%d" % c, [128, 4, 4, 128], F32)
+            res_bf[c] = sbuf("res_bf%d" % c, [128, CH * 4], BF16)
+            res_codes[c] = sbuf("res_codes%d" % c, [128, CH], U32)
+            res_rows[c] = sbuf("res_rows%d" % c, [128, 4, 128, 4], F32)
+        res_scales = sbuf("res_scales", [128, T], U8)
 
-        def mul_a(c, t, j0, j1):
+        def weigh(c, k, t):
+            groups = slice(4 * k, 4 * (k + 1))
             nc.vector.scalar_tensor_tensor(
-                out=mm[c][:, t, 2 * j0 : 2 * j1],
-                in0=du[c][:, t, 2 * j0 : 2 * j1, 0, :],
-                scalar=biasc[:, 0, t : t + 1],
-                in1=a0[c][:, t].unsqueeze(1).to_broadcast([128, 2 * (j1 - j0), CB]),
+                out=weighted[c][:, t, groups],
+                in0=du[c][:, t, groups, 0, :],
+                scalar=bias_c[:, 0, t : t + 1],
+                in1=a0[c][:, t].unsqueeze(1).to_broadcast([128, 4, CB]),
                 op0=ADD,
                 op1=MUL,
             )
 
-        def o_add(c, j):
+        def add_u1(c, j):
             nc.vector.tensor_add(
-                out=oo[c][:, j].rearrange("p t (b h) -> p t b h", h=2),
-                in0=mm[c][:, :, 2 * j : 2 * j + 2].rearrange("p t h b -> p t b h"),
+                out=res[c][:, j].rearrange("p t (b h) -> p t b h", h=2),
+                in0=weighted[c][:, :, 2 * j : 2 * j + 2].rearrange("p t h b -> p t b h"),
                 in1=du[c][:, :, 2 * j : 2 * j + 2, 1, :].rearrange("p t h b -> p t b h"),
             )
 
-        def o_bf(c, k, q0, q1, eng):
-            dst = ob[c][:].rearrange("p (g i k e) -> p k g e i", i=2, k=2, e=8)[:, k, 32 * q0 : 32 * q1]
-            src = oo[c][:, 2 * k : 2 * k + 2].rearrange("p j t (g i) -> p g (j t) i", i=2)[:, 32 * q0 : 32 * q1]
+        rows_out = out_0.rearrange("b n e -> (b n) e").rearrange("(c q j) e -> c q j e", c=NCH, j=4)
+
+        def res_turn(c, j):
+            res_ps[c, j] = bank("res_ps%d%d" % (c, j), [128, 4, 128])
+            for t in range(4):
+                nc.tensor.transpose(res_ps[c, j][:, t, :], res[c][:, j, t, :], ident[:])
+
+        def res_out(c, j):
+            nc.scalar.copy(out=res_rows[c][:, j], in_=res_ps[c, j][:].rearrange("q t p -> q p t"))
+
+        def store_rows(c, j0, j1, queue):
+            queue.dma_start(
+                out=rows_out[c, :, j0:j1, :].rearrange("q j e -> q (j e)"),
+                in_=res_rows[c][:, j0:j1].rearrange("q j p t -> q (j p t)"),
+            )
+
+        words_out = out_1.rearrange("g p m t -> (g p) (m t)").bitcast(I32)
+        scales_out = out_2.rearrange("g q m -> (g q) m").bitcast(I32)
+
+        def res_round(c, k, h0, h1, eng):
+            dst = res_bf[c][:].rearrange("p (a i k e) -> p k a e i", i=2, k=2, e=8)[:, k, 32 * h0 : 32 * h1]
+            src = res[c][:, 2 * k : 2 * k + 2].rearrange("p j t (a i) -> p a (j t) i", i=2)[:, 32 * h0 : 32 * h1]
             copy(eng, dst, src)
 
-        def o_q(c, q0, q1):
+        def res_quantise(c, h0, h1):
             nc.vector.quantize_mx(
-                out=oc[c][:, 256 * q0 : 256 * q1].bitcast(FP8X4),
-                scales=osc[:, CH * c + 256 * q0 : CH * c + 256 * q1],
-                in_=ob[c][:, 1024 * q0 : 1024 * q1],
+                out=res_codes[c][:, 256 * h0 : 256 * h1].bitcast(FP8X4),
+                scales=res_scales[:, CH * c + 256 * h0 : CH * c + 256 * h1],
+                in_=res_bf[c][:, 1024 * h0 : 1024 * h1],
             )
 
-        def o_tr(c, j):
-            ps = pp.tile([128, 4, 128], F32, name="o%d%d" % (c, j), tag="ps", bufs=8)
-            ops[c, j] = ps
-            for t in range(4):
-                nc.tensor.transpose(ps[:, t, :], oo[c][:, j, t, :], identf[:])
+        def store_words(c):
+            nc.sync.dma_start(out=words_out[:, CH * c : CH * (c + 1)], in_=res_codes[c][:].bitcast(I32))
 
-        def o_cp(c, j, eng):
-            copy(eng, ot[c][:, j], ops[c, j][:].rearrange("q t p -> q p t"))
+        def store_scales():
+            for i in range(4):
+                queue = nc.sync if i < 2 else nc.scalar
+                queue.dma_start(out=scales_out[4 * i : 4 * i + 4, :], in_=res_scales[32 * i : 32 * i + 4, :].bitcast(I32))
 
-        rows = out_0.rearrange("b n e -> (b n) e").rearrange("(c q j) e -> c q j e", c=NCH, j=4)
-        words = out_1.rearrange("g p m t -> (g p) (m t)").bitcast(I32)
-        srows = out_2.rearrange("g q m -> (g q) m").bitcast(I32)
 
-        def o_st(c, j0, j1, queue):
-            queue.dma_start(
-                out=rows[c, :, j0:j1, :].rearrange("q j e -> q (j e)"), in_=ot[c][:, j0:j1].rearrange("q j p t -> q (j p t)")
-            )
-
-        def w_st(c, q0, q1):
-            nc.sync.dma_start(
-                out=words[:, CH * c + 256 * q0 : CH * c + 256 * q1], in_=oc[c][:, 256 * q0 : 256 * q1].bitcast(I32)
-            )
-
-        def s_st(queue):
-            for q in range(4):
-                queue.dma_start(out=srows[4 * q : 4 * q + 4, :], in_=osc[32 * q : 32 * q + 4, :].bitcast(I32))
-
-        def x_turn(r, c, k, eng=S):
-            x_tr(r, c, k)
-            x_cp(r, c, k, eng)
-
-        def warm(n):
-            wp = pp.tile([128, 512], F32, name="warm", tag="ps", bufs=8)
-            nc.tensor.matmul(out=wp[:, 0:n], lhsT=zeros[:, 0:128], rhs=zeros[:, 0:n], start=True, stop=True)
-
-        load_x(1, 0, 0)
-        load_x(1, 0, 1)
-        load_w("w1", 0, 128)
-        load_x(0, 0, 0)
-        load_x(0, 0, 1)
-        load_w("w0", 0, 128)
-        load_x(1, 1, 0)
-        load_x(1, 1, 1)
-        load_w("a0", 0, 128)
-        load_x(0, 1, 0)
-        load_x(0, 1, 1)
-        load_w("a1", 0, 128)
+        for r in (1, 0):
+            load_x(r, 0, 0, 1)
+            load_x(r, 0, 1, 2)
+            load_w("w%d" % r)
+        for r in (1, 0):
+            load_x(r, 1, 0, 2)
+            load_w("wa%d" % (1 - r))
         load_gate_vectors()
 
-        warm(512)
-        consts_s()
-        x_turn(1, 0, 0)
-        x_turn(1, 0, 1)
-        warm(256)
+        warm(2 * WARM)
+        warm(WARM)
+        bias_constants()
+        x_turn(1, 0)
+        warm(WARM)
+        w_lay_slices("w1", 0, 2, V)
+        w_lay_slices("w1", 3, 4, S)
+        x_turn(0, 0)
+        warm(WARM)
+        for r in (1, 0):
+            w_lay_slices("w%d" % r, 2, 3, V)
+            w_quantise("w%d" % r, 0, 2)
+            x_quantise(r, 0)
+            w_quantise("w%d" % r, 2, 4)
+            if r == 1:
+                w_lay_slices("w0", 0, 2, V)
+                w_lay_slices("w0", 3, 4, S)
+                for t in range(4):
+                    product(1, 0, t)
+                    relu1(0, t)
 
-        w_cpt("w1", 0, 2, V)
-        w_cpt("w1", 3, 4, S)
-        x_turn(0, 0, 0, S)
-        x_turn(0, 0, 1, S)
-        warm(256)
-        w_cpt("w1", 2, 3, V)
-        w_q("w1", 0, 2)
-        x_q(1, 0, 0, 2)
-        w_q("w1", 2, 4)
-        w_cpt("w0", 0, 2, V)
-        w_cpt("w0", 3, 4, S)
+        wa0_lay_half(0, V)
+        x_turn(1, 1)
         for t in range(4):
-            mx1(1, 0, t)
-            relu1(0, t)
-        w_cpt("w0", 2, 3, V)
-        w_q("w0", 0, 2)
-        x_q(0, 0, 0, 2)
-        w_q("w0", 2, 4)
-        w_cp("a0", 0, 0, 64, V)
-        x_turn(1, 1, 0, S)
-        x_turn(1, 1, 1, S)
-        for t in range(4):
-            mx1(0, 0, t)
-        x_turn(0, 1, 0, S)
-        x_turn(0, 1, 1, S)
+            product(0, 0, t)
+        wa0_lay_half(1, S)
+        x_turn(0, 1)
         for t in range(4):
             diff0(0, t)
-        x_q(1, 1, 0, 2)
-        w_cp("a0", 0, 64, 128, V)
-        sum_bank(0, 0, 2)
-        sum_t(0, 0, 1)
-        sum_t(0, 1)
-        w_cp("a1", 0, 32, 128, S)
-        sum_cp(0, 0)
-        sum_bank(0, 2, 4)
-        sum_t(0, 2, 1)
-        sum_t(0, 3)
-        sum_cp(0, 2)
-        x_q(0, 1, 0, 2)
-        w_q("a0")
-        w_cp("a1", 0, 0, 32, V)
-        consts_v()
-        w_q("a1")
+        x_quantise(1, 1)
+        pre_add_last(0)
 
+        wa1_lay_half_negated(1, S)
+        for t in range(4):
+            sum_slice(0, t, first_plain=(t % 2 == 0))
+            if t % 2 == 1:
+                sum_out(0, t // 2)
+        x_quantise(0, 1)
+        w_quantise("wa0", 0, 4)
+        wa1_lay_half_negated(0, V)
+        gate_constants()
+        w_quantise("wa1", 0, 4)
 
-        mx1(1, 1, 0)
-        mx1(1, 1, 1)
-        mx1(0, 1, 0)
-        mx1(1, 1, 2)
+        product(1, 1, 0)
+        product(1, 1, 1)
+        product(0, 1, 0)
+        product(1, 1, 2)
         relu1(1, 0)
         relu1(1, 1)
-        sum_g(0)
-        mx1(0, 1, 1)
-        mx1(1, 1, 3)
-        mx1(0, 1, 2)
-        mx1(0, 1, 3)
+        sum_fold(0)
+        product(0, 1, 1)
+        product(1, 1, 3)
+        product(0, 1, 2)
+        product(0, 1, 3)
         relu1(1, 2)
         relu1(1, 3)
+
         diff0(1, 0)
-        sgate(0)
+        sg_round(0)
         diff0(1, 1)
-        sg_q(0)
+        sg_quantise(0)
         diff0(1, 2)
         diff0(1, 3)
-        sum_bank(1, 0, 2)
-        sum_t(1, 0)
-        mx2(0)
-        sigm(0)
-        sum_t(1, 1)
-        sum_cp(1, 0)
-        sum_bank(1, 2, 4)
-        sum_t(1, 2)
-        sum_t(1, 3)
-        sum_cp(1, 2)
-        sum_g(1)
+        pre_add_last(1)
+        sum_slice(1, 0)
+        logits(0)
+        softmax(0)
+        sum_slice(1, 1)
+        sum_out(1, 0)
+        sum_slice(1, 2, first_plain=True)
+        sum_slice(1, 3)
+        sum_out(1, 1)
+        sum_fold(1)
 
-        for t in range(4):
-            mul_a(0, t, 0, 2)
-        mul_a(0, 0, 2, 4)
-        o_add(0, 0)
-        o_add(0, 1)
-        mul_a(0, 1, 2, 4)
-        mul_a(0, 2, 2, 4)
-        sgate(1)
-        mul_a(0, 3, 2, 4)
-        sg_q(1)
-        o_add(0, 2)
-        o_add(0, 3)
-        o_tr(0, 0)
-        o_tr(0, 1)
-        warm(256)
-        mx2(1)
-        o_cp(0, 0, S)
-        o_cp(0, 1, S)
-        o_st(0, 0, 2, nc.sync)
-        sigm(1)
-        o_bf(0, 0, 0, 2, V)
-        o_tr(0, 2)
-        o_tr(0, 3)
-        warm(256)
-        o_cp(0, 2, S)
-        o_cp(0, 3, S)
-        o_st(0, 2, 4, nc.sync)
-        o_bf(0, 1, 0, 2, S)
-        for t in range(4):
-            mul_a(1, t, 0, 2)
-        mul_a(1, 0, 2, 4)
-        o_add(1, 0)
-        o_add(1, 1)
-        o_tr(1, 0)
-        o_tr(1, 1)
-        warm(256)
+        def weigh_first_piece(c):
+            for t in range(4):
+                weigh(c, 0, t)
+            weigh(c, 1, 0)
+            add_u1(c, 0)
+            add_u1(c, 1)
+
+        weigh_first_piece(0)
+        weigh(0, 1, 1)
+        weigh(0, 1, 2)
+        sg_round(1)
+        weigh(0, 1, 3)
+        sg_quantise(1)
+        add_u1(0, 2)
+        add_u1(0, 3)
+        res_turn(0, 0)
+        res_turn(0, 1)
+        warm(WARM)
+        logits(1)
+        res_round(0, 0, 0, 2, S)
+        res_out(0, 0)
+        softmax(1)
+        res_out(0, 1)
+        store_rows(0, 0, 2, nc.sync)
+        res_turn(0, 2)
+        res_turn(0, 3)
+        warm(WARM)
+        res_out(0, 2)
+        res_out(0, 3)
+        store_rows(0, 2, 4, nc.sync)
+        res_round(0, 1, 0, 2, S)
+
+        weigh_first_piece(1)
+        res_turn(1, 0)
+        res_turn(1, 1)
+        warm(WARM)
         for t in range(1, 4):
-            mul_a(1, t, 2, 4)
-        o_q(0, 0, 2)
-        w_st(0, 0, 2)
-        o_bf(1, 0, 0, 1, S)
-        o_cp(1, 0, S)
-        o_st(1, 0, 1, nc.sync)
-        o_cp(1, 1, S)
-        o_st(1, 1, 2, nc.sync)
-        o_bf(1, 0, 1, 2, S)
-        for j in (2, 3):
-            o_add(1, j)
-        o_bf(1, 1, 0, 1, V)
-        o_bf(1, 1, 1, 2, V)
-        o_q(1, 0, 1)
-        o_q(1, 1, 2)
-        o_tr(1, 2)
-        o_cp(1, 2, S)
-        w_st(1, 0, 1)
-        o_st(1, 2, 3, nc.sync)
-        w_st(1, 1, 2)
-        o_tr(1, 3)
-        o_cp(1, 3, S)
-        o_st(1, 3, 4, nc.scalar)
-        s_st(nc.sync)
+            weigh(1, 1, t)
+        res_quantise(0, 0, 2)
+        store_words(0)
+        res_round(1, 0, 0, 1, S)
+        res_out(1, 0)
+        res_out(1, 1)
+        store_rows(1, 0, 2, nc.sync)
+        res_round(1, 0, 1, 2, S)
+        add_u1(1, 2)
+        add_u1(1, 3)
+        for h in range(2):
+            res_round(1, 1, h, h + 1, V)
+        for h in range(2):
+            res_quantise(1, h, h + 1)
+        res_turn(1, 2)
+        res_out(1, 2)
+        store_rows(1, 2, 3, nc.sync)
+        store_words(1)
+        res_turn(1, 3)
+        res_out(1, 3)
+        store_rows(1, 3, 4, nc.scalar)
+        store_scales()

@@ -50,7 +50,7 @@ def tile_radixsplitattentionpointwise_x1_kernel(tc, x, w, bias, gs, wa, ba, out_
         ba_c = sbuf("ba_c", [128, 2, 16], BF16)
         gs_c = sbuf("gs_c", [128, 16], BF16)
         nc.scalar.dma_start(out=bias_c[:, :, 0:4], in_=bias.rearrange("r (p t) -> p r t", t=4))
-        zeros = sbuf("zeros", [128, 2 * WARM], F32)
+        zeros = sbuf("zeros", [128, WARM], F32)
         nc.vector.memset(zeros[:], 0.0)
         half = sbuf("half", [128, 1], F32)
         nc.scalar.activation(out=half[:], in_=zeros[:, 0:1], func=AF.Sigmoid)
@@ -61,8 +61,6 @@ def tile_radixsplitattentionpointwise_x1_kernel(tc, x, w, bias, gs, wa, ba, out_
         nc.vector.tensor_copy(out=ident_bf[:], in_=ident[:])
         fold_du = sbuf("fold_du", [128, CB], F32)
         nc.vector.scalar_tensor_tensor(out=fold_du[:], in0=ident[:, CB:128], scalar=2.0, in1=ident[:, 0:CB], op0=MUL, op1=ADD)
-        fold_pair = sbuf("fold_pair", [128, CB], F32)
-        nc.vector.tensor_add(out=fold_pair[:], in0=ident[:, CB:128], in1=ident[:, 0:CB])
         sg_codes = sbuf("sg_codes", [128, B], U32)
         sg_scales = sbuf("sg_scales", [128, B], U8)
         nc.gpsimd.memset(sg_codes[:], 0)
@@ -87,9 +85,9 @@ def tile_radixsplitattentionpointwise_x1_kernel(tc, x, w, bias, gs, wa, ba, out_
             nc.vector.tensor_scalar(out=gain[:], in0=gs_c[:, 0:4], scalar1=half[:], scalar2=2.0 / N, op0=MUL, op1=MUL)
             nc.vector.tensor_sub(out=ba_diff[:], in0=ba_c[:, 0, 0:4], in1=ba_c[:, 1, 0:4])
 
-        def warm(columns):
-            scrap = bank("warm", [128, 2 * WARM])
-            nc.tensor.matmul(out=scrap[:, 0:columns], lhsT=zeros[:, 0:128], rhs=zeros[:, 0:columns], start=True, stop=True)
+        def warm(columns, moving=None):
+            scrap = bank("warm", [128, WARM])
+            nc.tensor.matmul(out=scrap[:, 0:columns], lhsT=zeros[:, 0:128], rhs=zeros[:, 0:columns] if moving is None else moving, start=True, stop=True)
 
         x_rows = {}
         x_bf = {}
@@ -147,13 +145,13 @@ def tile_radixsplitattentionpointwise_x1_kernel(tc, x, w, bias, gs, wa, ba, out_
             dst, src = w_views(nm)
             copy(eng, dst[:, :, t0:t1], src[:, :, t0:t1])
 
-        def wa0_lay_half(i, eng):
+        def wa0_lay(i0, i1, eng):
             dst, src = w_views("wa0")
-            copy(eng, dst[:, 32 * i : 32 * (i + 1)], src[:, 32 * i : 32 * (i + 1)])
+            copy(eng, dst[:, 16 * i0 : 16 * i1], src[:, 16 * i0 : 16 * i1])
 
-        def wa1_lay_half_negated(i, eng):
-            dst = w_bf["wa1"][:].rearrange("p (t m s) -> p t m s", t=4, s=4)[:, :, 64 * i : 64 * (i + 1)]
-            src = w_rows["wa1"][:].rearrange("p s (m t) -> p t m s", t=4)[:, :, 64 * i : 64 * (i + 1)]
+        def wa1_lay_negated(i0, i1, eng):
+            dst = w_bf["wa1"][:].rearrange("p (t m s) -> p t m s", t=4, s=4)[:, :, 32 * i0 : 32 * i1]
+            src = w_rows["wa1"][:].rearrange("p s (m t) -> p t m s", t=4)[:, :, 32 * i0 : 32 * i1]
             if eng is V:
                 nc.vector.tensor_scalar(out=dst, in0=src, scalar1=-1.0, scalar2=None, op0=MUL)
             else:
@@ -199,10 +197,8 @@ def tile_radixsplitattentionpointwise_x1_kernel(tc, x, w, bias, gs, wa, ba, out_
                 op1=SUB,
             )
 
-        LAST = 3
         sum_ps = {}
         sum_sb = {}
-        last_sum = {}
         s_ps = {}
 
         def add_up(out, blocks, first_plain):
@@ -216,31 +212,21 @@ def tile_radixsplitattentionpointwise_x1_kernel(tc, x, w, bias, gs, wa, ba, out_
                     is_transpose=not (first_plain and g == 0),
                 )
 
-        def pre_add_last(c):
-            last_sum[c] = sbuf("last_sum%d" % c, [128, N, CB], F32)
-            nc.vector.scalar_tensor_tensor(
-                out=last_sum[c][:], in0=du[c][:, LAST, :, 1, :], scalar=2.0, in1=du[c][:, LAST, :, 0, :], op0=MUL, op1=ADD
-            )
-
         def sum_slice(c, t, first_plain=False):
-            if t % 2 == 0:
-                sum_ps[c, t // 2] = bank("sum_ps%d%d" % (c, t // 2), [128, 2, 128])
-            if t == LAST:
-                blocks = [last_sum[c][:, g : g + 2].rearrange("p g b -> p (g b)") for g in range(0, N, 2)]
-            else:
-                blocks = [du[c][:, t, g].rearrange("p a b -> p (a b)") for g in range(N)]
-            add_up(sum_ps[c, t // 2][:, t % 2, :], blocks, first_plain)
+            if t != 1:
+                sum_ps[c, t] = bank("sum_ps%d%d" % (c, t), [128, 2 if t == 0 else 1, 128])
+            blocks = [du[c][:, t, g].rearrange("p a b -> p (a b)") for g in range(N)]
+            add_up(sum_ps[c, 0][:, 1, :] if t == 1 else sum_ps[c, t][:, 0, :], blocks, first_plain)
 
         def sum_out(c, i):
-            sum_sb[c, i] = sbuf("sum_sb%d%d" % (c, i), [128, 2, 128], F32)
+            sum_sb[c, i] = sbuf("sum_sb%d%d" % (c, i), [128, 2 if i == 0 else 1, 128], F32)
             nc.scalar.copy(out=sum_sb[c, i][:], in_=sum_ps[c, i][:])
 
         def sum_fold(c):
             s_ps[c] = bank("s_ps%d" % c, [128, 4, CB])
             for t in range(4):
-                fold = fold_pair if t == LAST else fold_du
                 nc.tensor.matmul(out=s_ps[c][:, t, :], lhsT=ident_bf[:], rhs=bias0_sum[:, t, :], start=True, stop=False)
-                nc.tensor.matmul(out=s_ps[c][:, t, :], lhsT=sum_sb[c, t // 2][:, t % 2, :], rhs=fold[:], start=False, stop=True)
+                nc.tensor.matmul(out=s_ps[c][:, t, :], lhsT=sum_sb[c, 0][:, 1, :] if t == 1 else sum_sb[c, t][:, 0, :], rhs=fold_du[:], start=False, stop=True)
 
         sg_bf = {}
         l_ps = {}
@@ -300,11 +286,12 @@ def tile_radixsplitattentionpointwise_x1_kernel(tc, x, w, bias, gs, wa, ba, out_
                 op1=MUL,
             )
 
-        def add_u1(c, j):
+        def add_u1(c, j, h0=0, h1=2):
+            items = slice(32 * h0, 32 * h1)
             nc.vector.tensor_add(
-                out=res[c][:, j].rearrange("p t (b h) -> p t b h", h=2),
-                in0=weighted[c][:, :, 2 * j : 2 * j + 2].rearrange("p t h b -> p t b h"),
-                in1=du[c][:, :, 2 * j : 2 * j + 2, 1, :].rearrange("p t h b -> p t b h"),
+                out=res[c][:, j].rearrange("p t (b h) -> p t b h", h=2)[:, :, items],
+                in0=weighted[c][:, :, 2 * j : 2 * j + 2, items].rearrange("p t h b -> p t b h"),
+                in1=du[c][:, :, 2 * j : 2 * j + 2, 1, items].rearrange("p t h b -> p t b h"),
             )
 
         rows_out = out_0.rearrange("b n e -> (b n) e").rearrange("(c q j) e -> c q j e", c=NCH, j=4)
@@ -338,13 +325,14 @@ def tile_radixsplitattentionpointwise_x1_kernel(tc, x, w, bias, gs, wa, ba, out_
                 in_=res_bf[c][:, 1024 * h0 : 1024 * h1],
             )
 
-        def store_words(c):
-            nc.sync.dma_start(out=words_out[:, CH * c : CH * (c + 1)], in_=res_codes[c][:].bitcast(I32))
+        def store_words(c, h0, h1):
+            nc.sync.dma_start(
+                out=words_out[:, CH * c + 256 * h0 : CH * c + 256 * h1], in_=res_codes[c][:, 256 * h0 : 256 * h1].bitcast(I32)
+            )
 
         def store_scales():
             for i in range(4):
-                queue = nc.sync if i < 2 else nc.scalar
-                queue.dma_start(out=scales_out[4 * i : 4 * i + 4, :], in_=res_scales[32 * i : 32 * i + 4, :].bitcast(I32))
+                nc.sync.dma_start(out=scales_out[4 * i : 4 * i + 4, :], in_=res_scales[32 * i : 32 * i + 4, :].bitcast(I32))
 
 
         for r in (1, 0):
@@ -356,7 +344,7 @@ def tile_radixsplitattentionpointwise_x1_kernel(tc, x, w, bias, gs, wa, ba, out_
             load_w("wa%d" % (1 - r))
         load_gate_vectors()
 
-        warm(2 * WARM)
+        warm(WARM)
         warm(WARM)
         bias_constants()
         x_turn(1, 0)
@@ -364,70 +352,60 @@ def tile_radixsplitattentionpointwise_x1_kernel(tc, x, w, bias, gs, wa, ba, out_
         w_lay_slices("w1", 0, 2, V)
         w_lay_slices("w1", 3, 4, S)
         x_turn(0, 0)
-        warm(WARM)
-        for r in (1, 0):
-            w_lay_slices("w%d" % r, 2, 3, V)
-            w_quantise("w%d" % r, 0, 2)
-            x_quantise(r, 0)
-            w_quantise("w%d" % r, 2, 4)
-            if r == 1:
-                w_lay_slices("w0", 0, 2, V)
-                w_lay_slices("w0", 3, 4, S)
-                for t in range(4):
-                    product(1, 0, t)
-                    relu1(0, t)
-
-        wa0_lay_half(0, V)
+        warm(WARM // 2)
+        w_lay_slices("w1", 2, 3, V)
+        w_quantise("w1", 0, 2)
+        x_quantise(1, 0)
+        w_quantise("w1", 2, 4)
+        for t in range(4):
+            product(1, 0, t)
+            relu1(0, t)
+        w_lay_slices("w0", 0, 2, V)
+        w_lay_slices("w0", 2, 4, V)
+        w_quantise("w0", 0, 2)
+        x_quantise(0, 0)
+        w_quantise("w0", 2, 4)
         x_turn(1, 1)
+        wa0_lay(0, 2, V)
         for t in range(4):
             product(0, 0, t)
-        wa0_lay_half(1, S)
-        x_turn(0, 1)
-        for t in range(4):
             diff0(0, t)
+        wa0_lay(2, 4, S)
+        x_turn(0, 1)
         x_quantise(1, 1)
-        pre_add_last(0)
-
-        wa1_lay_half_negated(1, S)
-        for t in range(4):
-            sum_slice(0, t, first_plain=(t % 2 == 0))
-            if t % 2 == 1:
-                sum_out(0, t // 2)
+        wa1_lay_negated(0, 3, V)
         x_quantise(0, 1)
+        wa1_lay_negated(3, 4, S)
+        for t in range(4):
+            sum_slice(0, t)
+            if t >= 1:
+                sum_out(0, t if t > 1 else 0)
         w_quantise("wa0", 0, 4)
-        wa1_lay_half_negated(0, V)
         gate_constants()
         w_quantise("wa1", 0, 4)
-
-        product(1, 1, 0)
-        product(1, 1, 1)
+        for t in range(2):
+            product(1, 1, t)
+            relu1(1, t)
+        sum_fold(0)
+        sg_round(0)
         product(0, 1, 0)
         product(1, 1, 2)
-        relu1(1, 0)
-        relu1(1, 1)
-        sum_fold(0)
-        product(0, 1, 1)
+        relu1(1, 2)
         product(1, 1, 3)
+        relu1(1, 3)
+        diff0(1, 0)
+        sg_quantise(0)
+        product(0, 1, 1)
         product(0, 1, 2)
         product(0, 1, 3)
-        relu1(1, 2)
-        relu1(1, 3)
-
-        diff0(1, 0)
-        sg_round(0)
-        diff0(1, 1)
-        sg_quantise(0)
-        diff0(1, 2)
-        diff0(1, 3)
-        pre_add_last(1)
-        sum_slice(1, 0)
         logits(0)
         softmax(0)
-        sum_slice(1, 1)
-        sum_out(1, 0)
-        sum_slice(1, 2, first_plain=True)
-        sum_slice(1, 3)
-        sum_out(1, 1)
+        for t in range(1, 4):
+            diff0(1, t)
+        for t in range(4):
+            sum_slice(1, t)
+            if t >= 1:
+                sum_out(1, t if t > 1 else 0)
         sum_fold(1)
 
         def weigh_first_piece(c):
@@ -438,6 +416,10 @@ def tile_radixsplitattentionpointwise_x1_kernel(tc, x, w, bias, gs, wa, ba, out_
             add_u1(c, 1)
 
         weigh_first_piece(0)
+        res_turn(0, 0)
+        res_turn(0, 1)
+        warm(WARM)
+        res_round(0, 0, 0, 2, S)
         weigh(0, 1, 1)
         weigh(0, 1, 2)
         sg_round(1)
@@ -445,15 +427,11 @@ def tile_radixsplitattentionpointwise_x1_kernel(tc, x, w, bias, gs, wa, ba, out_
         sg_quantise(1)
         add_u1(0, 2)
         add_u1(0, 3)
-        res_turn(0, 0)
-        res_turn(0, 1)
-        warm(WARM)
         logits(1)
-        res_round(0, 0, 0, 2, S)
         res_out(0, 0)
-        softmax(1)
         res_out(0, 1)
         store_rows(0, 0, 2, nc.sync)
+        softmax(1)
         res_turn(0, 2)
         res_turn(0, 3)
         warm(WARM)
@@ -463,29 +441,32 @@ def tile_radixsplitattentionpointwise_x1_kernel(tc, x, w, bias, gs, wa, ba, out_
         res_round(0, 1, 0, 2, S)
 
         weigh_first_piece(1)
+        warm(WARM, weighted[1][:, 3, 0:4].rearrange("p g b -> p (g b)"))
         res_turn(1, 0)
         res_turn(1, 1)
-        warm(WARM)
-        for t in range(1, 4):
-            weigh(1, 1, t)
-        res_quantise(0, 0, 2)
-        store_words(0)
-        res_round(1, 0, 0, 1, S)
+        weigh(1, 1, 1)
+        warm(WARM, weighted[1][:, 1, 4:8].rearrange("p g b -> p (g b)"))
+        weigh(1, 1, 2)
+        weigh(1, 1, 3)
         res_out(1, 0)
         res_out(1, 1)
         store_rows(1, 0, 2, nc.sync)
-        res_round(1, 0, 1, 2, S)
+        res_quantise(0, 0, 1)
+        res_round(1, 0, 0, 2, S)
         add_u1(1, 2)
-        add_u1(1, 3)
+        res_turn(1, 2)
+        res_quantise(0, 1, 2)
+        store_words(0, 0, 2)
+        add_u1(1, 3, 0, 1)
+        add_u1(1, 3, 1, 2)
+        res_turn(1, 3)
         for h in range(2):
             res_round(1, 1, h, h + 1, V)
-        for h in range(2):
-            res_quantise(1, h, h + 1)
-        res_turn(1, 2)
         res_out(1, 2)
         store_rows(1, 2, 3, nc.sync)
-        store_words(1)
-        res_turn(1, 3)
+        for h in range(2):
+            res_quantise(1, h, h + 1)
         res_out(1, 3)
+        store_words(1, 0, 2)
         store_rows(1, 3, 4, nc.scalar)
         store_scales()

@@ -61,6 +61,8 @@ def tile_radixsplitattentionpointwise_x1_kernel(tc, x, w, bias, gs, wa, ba, out_
         nc.vector.tensor_copy(out=ident_bf[:], in_=ident[:])
         fold_du = sbuf("fold_du", [128, CB], F32)
         nc.vector.scalar_tensor_tensor(out=fold_du[:], in0=ident[:, CB:128], scalar=2.0, in1=ident[:, 0:CB], op0=MUL, op1=ADD)
+        fold_pair = sbuf("fold_pair", [128, CB], F32)
+        nc.vector.tensor_add(out=fold_pair[:], in0=ident[:, CB:128], in1=ident[:, 0:CB])
         sg_codes = sbuf("sg_codes", [128, B], U32)
         sg_scales = sbuf("sg_scales", [128, B], U8)
         nc.gpsimd.memset(sg_codes[:], 0)
@@ -199,6 +201,7 @@ def tile_radixsplitattentionpointwise_x1_kernel(tc, x, w, bias, gs, wa, ba, out_
 
         sum_ps = {}
         sum_sb = {}
+        pre_sum = {}
         s_ps = {}
 
         def add_up(out, blocks, first_plain):
@@ -212,10 +215,19 @@ def tile_radixsplitattentionpointwise_x1_kernel(tc, x, w, bias, gs, wa, ba, out_
                     is_transpose=not (first_plain and g == 0),
                 )
 
+        def pre_add(c, t):
+            pre_sum[c, t] = sbuf("pre_sum%d%d" % (c, t), [128, N, CB], F32)
+            nc.vector.scalar_tensor_tensor(
+                out=pre_sum[c, t][:], in0=du[c][:, t, :, 1, :], scalar=2.0, in1=du[c][:, t, :, 0, :], op0=MUL, op1=ADD
+            )
+
         def sum_slice(c, t, first_plain=False):
             if t != 1:
                 sum_ps[c, t] = bank("sum_ps%d%d" % (c, t), [128, 2 if t == 0 else 1, 128])
-            blocks = [du[c][:, t, g].rearrange("p a b -> p (a b)") for g in range(N)]
+            if (c, t) in pre_sum:
+                blocks = [pre_sum[c, t][:, g : g + 2].rearrange("p g b -> p (g b)") for g in range(0, N, 2)]
+            else:
+                blocks = [du[c][:, t, g].rearrange("p a b -> p (a b)") for g in range(N)]
             add_up(sum_ps[c, 0][:, 1, :] if t == 1 else sum_ps[c, t][:, 0, :], blocks, first_plain)
 
         def sum_out(c, i):
@@ -226,7 +238,7 @@ def tile_radixsplitattentionpointwise_x1_kernel(tc, x, w, bias, gs, wa, ba, out_
             s_ps[c] = bank("s_ps%d" % c, [128, 4, CB])
             for t in range(4):
                 nc.tensor.matmul(out=s_ps[c][:, t, :], lhsT=ident_bf[:], rhs=bias0_sum[:, t, :], start=True, stop=False)
-                nc.tensor.matmul(out=s_ps[c][:, t, :], lhsT=sum_sb[c, 0][:, 1, :] if t == 1 else sum_sb[c, t][:, 0, :], rhs=fold_du[:], start=False, stop=True)
+                nc.tensor.matmul(out=s_ps[c][:, t, :], lhsT=sum_sb[c, 0][:, 1, :] if t == 1 else sum_sb[c, t][:, 0, :], rhs=(fold_pair if (c, t) in pre_sum else fold_du)[:], start=False, stop=True)
 
         sg_bf = {}
         l_ps = {}
@@ -336,8 +348,7 @@ def tile_radixsplitattentionpointwise_x1_kernel(tc, x, w, bias, gs, wa, ba, out_
 
 
         for r in (1, 0):
-            load_x(r, 0, 0, 1)
-            load_x(r, 0, 1, 2)
+            load_x(r, 0, 0, 2)
             load_w("w%d" % r)
         for r in (1, 0):
             load_x(r, 1, 0, 2)
@@ -346,13 +357,13 @@ def tile_radixsplitattentionpointwise_x1_kernel(tc, x, w, bias, gs, wa, ba, out_
 
         warm(WARM)
         warm(WARM)
+        warm(WARM)
         bias_constants()
         x_turn(1, 0)
         warm(WARM)
         w_lay_slices("w1", 0, 2, V)
         w_lay_slices("w1", 3, 4, S)
         x_turn(0, 0)
-        warm(WARM // 2)
         w_lay_slices("w1", 2, 3, V)
         w_quantise("w1", 0, 2)
         x_quantise(1, 0)
@@ -373,6 +384,7 @@ def tile_radixsplitattentionpointwise_x1_kernel(tc, x, w, bias, gs, wa, ba, out_
         wa0_lay(2, 4, S)
         x_turn(0, 1)
         x_quantise(1, 1)
+        pre_add(0, 3)
         wa1_lay_negated(0, 3, V)
         x_quantise(0, 1)
         wa1_lay_negated(3, 4, S)
@@ -449,8 +461,9 @@ def tile_radixsplitattentionpointwise_x1_kernel(tc, x, w, bias, gs, wa, ba, out_
         weigh(1, 1, 2)
         weigh(1, 1, 3)
         res_out(1, 0)
+        store_rows(1, 0, 1, nc.sync)
         res_out(1, 1)
-        store_rows(1, 0, 2, nc.sync)
+        store_rows(1, 1, 2, nc.sync)
         res_quantise(0, 0, 1)
         res_round(1, 0, 0, 2, S)
         add_u1(1, 2)

@@ -68,6 +68,9 @@ def tile_radixsplitattentionpointwise_x1_kernel(tc, x, w, bias, gs, wa, ba, out_
         nc.gpsimd.memset(sg_codes[:], 0)
         nc.gpsimd.memset(sg_scales[:].bitcast(U32), 0)
 
+        sign = sbuf("sign", [128, 1], F32)
+        nc.gpsimd.memset(sign[0:64], 1.0)
+        nc.gpsimd.memset(sign[64:128], -1.0)
         neg_bias0 = sbuf("neg_bias0", [128, 4], F32)
         bias0_sum = sbuf("bias0_sum", [128, 4, CB], BF16)
         gain = sbuf("gain", [128, 4], F32)
@@ -143,21 +146,14 @@ def tile_radixsplitattentionpointwise_x1_kernel(tc, x, w, bias, gs, wa, ba, out_
             src = w_rows[nm][:].rearrange("p s (a i t) -> p a t i s", i=2, t=4)
             return dst, src
 
-        def w_lay_slices(nm, t0, t1, eng):
+        def w_lay(nm, i0, i1, eng):
             dst, src = w_views(nm)
-            copy(eng, dst[:, :, t0:t1], src[:, :, t0:t1])
-
-        def wa0_lay(i0, i1, eng):
-            dst, src = w_views("wa0")
             copy(eng, dst[:, 16 * i0 : 16 * i1], src[:, 16 * i0 : 16 * i1])
 
-        def wa1_lay_negated(i0, i1, eng):
-            dst = w_bf["wa1"][:].rearrange("p (t m s) -> p t m s", t=4, s=4)[:, :, 32 * i0 : 32 * i1]
-            src = w_rows["wa1"][:].rearrange("p s (m t) -> p t m s", t=4)[:, :, 32 * i0 : 32 * i1]
-            if eng is V:
-                nc.vector.tensor_scalar(out=dst, in0=src, scalar1=-1.0, scalar2=None, op0=MUL)
-            else:
-                nc.scalar.activation(out=dst, in_=src, func=AF.Copy, scale=-1.0)
+        def w_lay_negated(nm, i0, i1):
+            dst = w_bf[nm][:].rearrange("p (t m s) -> p t m s", t=4, s=4)[:, :, 32 * i0 : 32 * i1]
+            src = w_rows[nm][:].rearrange("p s (m t) -> p t m s", t=4)[:, :, 32 * i0 : 32 * i1]
+            nc.scalar.activation(out=dst, in_=src, func=AF.Copy, scale=-1.0)
 
         def w_quantise(nm, t0, t1):
             cols = slice(128 * t0, 128 * t1)
@@ -271,6 +267,7 @@ def tile_radixsplitattentionpointwise_x1_kernel(tc, x, w, bias, gs, wa, ba, out_
                     in_=l_ps[c, t // 2][:, t % 2, CB * c : CB * (c + 1)],
                     func=AF.Sigmoid,
                     bias=ba_diff[:, t : t + 1],
+                    scale=sign[:],
                 )
 
         weighted = {}
@@ -348,7 +345,11 @@ def tile_radixsplitattentionpointwise_x1_kernel(tc, x, w, bias, gs, wa, ba, out_
 
 
         for r in (1, 0):
-            load_x(r, 0, 0, 2)
+            if r == 1:
+                load_x(r, 0, 0, 1)
+                load_x(r, 0, 1, 2)
+            else:
+                load_x(r, 0, 0, 2)
             load_w("w%d" % r)
         for r in (1, 0):
             load_x(r, 1, 0, 2)
@@ -357,56 +358,57 @@ def tile_radixsplitattentionpointwise_x1_kernel(tc, x, w, bias, gs, wa, ba, out_
 
         warm(WARM)
         warm(WARM)
-        warm(WARM)
         bias_constants()
         x_turn(1, 0)
         warm(WARM)
-        w_lay_slices("w1", 0, 2, V)
-        w_lay_slices("w1", 3, 4, S)
+        warm(WARM)
+        w_lay("w1", 0, 3, V)
+        w_lay("w1", 3, 4, S)
         x_turn(0, 0)
-        w_lay_slices("w1", 2, 3, V)
-        w_quantise("w1", 0, 2)
         x_quantise(1, 0)
+        w_quantise("w1", 0, 2)
         w_quantise("w1", 2, 4)
         for t in range(4):
             product(1, 0, t)
             relu1(0, t)
-        w_lay_slices("w0", 0, 2, V)
-        w_lay_slices("w0", 2, 4, V)
-        w_quantise("w0", 0, 2)
+        w_lay("w0", 0, 4, V)
         x_quantise(0, 0)
+        w_quantise("w0", 0, 2)
         w_quantise("w0", 2, 4)
         x_turn(1, 1)
-        wa0_lay(0, 2, V)
+        w_lay("wa0", 0, 2, V)
         for t in range(4):
             product(0, 0, t)
             diff0(0, t)
-        wa0_lay(2, 4, S)
+        w_lay_negated("wa0", 2, 4)
         x_turn(0, 1)
         x_quantise(1, 1)
         pre_add(0, 3)
-        wa1_lay_negated(0, 3, V)
+        w_lay("wa1", 2, 4, V)
         x_quantise(0, 1)
-        wa1_lay_negated(3, 4, S)
+        w_lay_negated("wa1", 0, 1)
         for t in range(4):
             sum_slice(0, t)
             if t >= 1:
                 sum_out(0, t if t > 1 else 0)
+            if t == 1:
+                w_lay_negated("wa1", 1, 2)
         w_quantise("wa0", 0, 4)
         gate_constants()
-        w_quantise("wa1", 0, 4)
+        w_quantise("wa1", 2, 4)
         for t in range(2):
             product(1, 1, t)
             relu1(1, t)
         sum_fold(0)
         sg_round(0)
+        w_quantise("wa1", 0, 2)
+        sg_quantise(0)
         product(0, 1, 0)
         product(1, 1, 2)
         relu1(1, 2)
         product(1, 1, 3)
         relu1(1, 3)
         diff0(1, 0)
-        sg_quantise(0)
         product(0, 1, 1)
         product(0, 1, 2)
         product(0, 1, 3)
@@ -441,9 +443,9 @@ def tile_radixsplitattentionpointwise_x1_kernel(tc, x, w, bias, gs, wa, ba, out_
         add_u1(0, 3)
         logits(1)
         res_out(0, 0)
+        softmax(1)
         res_out(0, 1)
         store_rows(0, 0, 2, nc.sync)
-        softmax(1)
         res_turn(0, 2)
         res_turn(0, 3)
         warm(WARM)

@@ -200,41 +200,42 @@ def tile_radixsplitattentionpointwise_x1_kernel(tc, x, w, bias, gs, wa, ba, out_
         pre_sum = {}
         s_ps = {}
 
-        def add_up(out, blocks, first_plain):
-            for g, block in enumerate(blocks):
-                nc.tensor.matmul(
-                    out=out,
-                    lhsT=block,
-                    rhs=ident[:],
-                    start=(g == 0),
-                    stop=(g == len(blocks) - 1),
-                    is_transpose=not (first_plain and g == 0),
-                )
-
         def pre_add(c, t):
             pre_sum[c, t] = sbuf("pre_sum%d%d" % (c, t), [128, N, CB], F32)
             nc.vector.scalar_tensor_tensor(
                 out=pre_sum[c, t][:], in0=du[c][:, t, :, 1, :], scalar=2.0, in1=du[c][:, t, :, 0, :], op0=MUL, op1=ADD
             )
 
-        def sum_slice(c, t, first_plain=False):
-            if t != 1:
-                sum_ps[c, t] = bank("sum_ps%d%d" % (c, t), [128, 2 if t == 0 else 1, 128])
-            if (c, t) in pre_sum:
-                blocks = [pre_sum[c, t][:, g : g + 2].rearrange("p g b -> p (g b)") for g in range(0, N, 2)]
-            else:
-                blocks = [du[c][:, t, g].rearrange("p a b -> p (a b)") for g in range(N)]
-            add_up(sum_ps[c, 0][:, 1, :] if t == 1 else sum_ps[c, t][:, 0, :], blocks, first_plain)
+        def sum_pair(c, t0):
+            blocks = {}
+            for t in (t0, t0 + 1):
+                sum_ps[c, t] = bank("sum_ps%d%d" % (c, t), [128, 128])
+                if (c, t) in pre_sum:
+                    blocks[t] = [pre_sum[c, t][:, g : g + 2].rearrange("p g b -> p (g b)") for g in range(0, N, 2)]
+                else:
+                    blocks[t] = [du[c][:, t, g].rearrange("p a b -> p (a b)") for g in range(N)]
+            for step in range(N):
+                for t in (t0, t0 + 1):
+                    g = step - (N - len(blocks[t]))
+                    if g >= 0:
+                        nc.tensor.matmul(
+                            out=sum_ps[c, t][:],
+                            lhsT=blocks[t][g],
+                            rhs=ident[:],
+                            start=(g == 0),
+                            stop=(step == N - 1),
+                            is_transpose=True,
+                        )
 
-        def sum_out(c, i):
-            sum_sb[c, i] = sbuf("sum_sb%d%d" % (c, i), [128, 2 if i == 0 else 1, 128], F32)
-            nc.scalar.copy(out=sum_sb[c, i][:], in_=sum_ps[c, i][:])
+        def sum_out(c, t):
+            sum_sb[c, t] = sbuf("sum_sb%d%d" % (c, t), [128, 128], F32)
+            nc.scalar.copy(out=sum_sb[c, t][:], in_=sum_ps[c, t][:])
 
         def sum_fold(c):
             s_ps[c] = bank("s_ps%d" % c, [128, 4, CB])
             for t in range(4):
                 nc.tensor.matmul(out=s_ps[c][:, t, :], lhsT=ident_bf[:], rhs=bias0_sum[:, t, :], start=True, stop=False)
-                nc.tensor.matmul(out=s_ps[c][:, t, :], lhsT=sum_sb[c, 0][:, 1, :] if t == 1 else sum_sb[c, t][:, 0, :], rhs=(fold_pair if (c, t) in pre_sum else fold_du)[:], start=False, stop=True)
+                nc.tensor.matmul(out=s_ps[c][:, t, :], lhsT=sum_sb[c, t][:], rhs=(fold_pair if (c, t) in pre_sum else fold_du)[:], start=False, stop=True)
 
         sg_bf = {}
         l_ps = {}
@@ -383,16 +384,16 @@ def tile_radixsplitattentionpointwise_x1_kernel(tc, x, w, bias, gs, wa, ba, out_
         w_lay_negated("wa0", 2, 4)
         x_turn(0, 1)
         x_quantise(1, 1)
-        pre_add(0, 3)
         w_lay("wa1", 2, 4, V)
         x_quantise(0, 1)
         w_lay_negated("wa1", 0, 1)
-        for t in range(4):
-            sum_slice(0, t)
-            if t >= 1:
-                sum_out(0, t if t > 1 else 0)
-            if t == 1:
-                w_lay_negated("wa1", 1, 2)
+        sum_pair(0, 0)
+        sum_out(0, 0)
+        sum_out(0, 1)
+        w_lay_negated("wa1", 1, 2)
+        sum_pair(0, 2)
+        sum_out(0, 2)
+        sum_out(0, 3)
         w_quantise("wa0", 0, 4)
         gate_constants()
         w_quantise("wa1", 2, 4)
@@ -416,10 +417,10 @@ def tile_radixsplitattentionpointwise_x1_kernel(tc, x, w, bias, gs, wa, ba, out_
         softmax(0)
         for t in range(1, 4):
             diff0(1, t)
-        for t in range(4):
-            sum_slice(1, t)
-            if t >= 1:
-                sum_out(1, t if t > 1 else 0)
+        for t in (0, 2):
+            sum_pair(1, t)
+            sum_out(1, t)
+            sum_out(1, t + 1)
         sum_fold(1)
 
         def weigh_first_piece(c):

@@ -52,8 +52,8 @@ def tile_radixsplitattentionpointwise_x1_kernel(tc, x, w, bias, gs, wa, ba, out_
         nc.scalar.dma_start(out=bias_c[:, :, 0:4], in_=bias.rearrange("r (p t) -> p r t", t=4))
         zeros = sbuf("zeros", [128, WARM], F32)
         nc.vector.memset(zeros[:], 0.0)
-        half = sbuf("half", [128, 1], F32)
-        nc.scalar.activation(out=half[:], in_=zeros[:, 0:1], func=AF.Sigmoid)
+        one_half = sbuf("one_half", [128, 1], F32)
+        nc.scalar.activation(out=one_half[:], in_=zeros[:, 0:1], func=AF.Sigmoid)
 
         ident = sbuf("ident", [128, 128], F32)
         make_identity(nc, ident[:])
@@ -61,16 +61,14 @@ def tile_radixsplitattentionpointwise_x1_kernel(tc, x, w, bias, gs, wa, ba, out_
         nc.vector.tensor_copy(out=ident_bf[:], in_=ident[:])
         fold_du = sbuf("fold_du", [128, CB], F32)
         nc.vector.scalar_tensor_tensor(out=fold_du[:], in0=ident[:, CB:128], scalar=2.0, in1=ident[:, 0:CB], op0=MUL, op1=ADD)
-        fold_pair = sbuf("fold_pair", [128, CB], F32)
-        nc.vector.tensor_add(out=fold_pair[:], in0=ident[:, CB:128], in1=ident[:, 0:CB])
         sg_codes = sbuf("sg_codes", [128, B], U32)
         sg_scales = sbuf("sg_scales", [128, B], U8)
         nc.gpsimd.memset(sg_codes[:], 0)
         nc.gpsimd.memset(sg_scales[:].bitcast(U32), 0)
-
         sign = sbuf("sign", [128, 1], F32)
         nc.gpsimd.memset(sign[0:64], 1.0)
         nc.gpsimd.memset(sign[64:128], -1.0)
+
         neg_bias0 = sbuf("neg_bias0", [128, 4], F32)
         bias0_sum = sbuf("bias0_sum", [128, 4, CB], BF16)
         gain = sbuf("gain", [128, 4], F32)
@@ -87,12 +85,12 @@ def tile_radixsplitattentionpointwise_x1_kernel(tc, x, w, bias, gs, wa, ba, out_
             nc.sync.dma_start(out=ba_c[:, :, 0:4], in_=ba.rearrange("r (p t) -> p r t", t=4))
 
         def gate_constants():
-            nc.vector.tensor_scalar(out=gain[:], in0=gs_c[:, 0:4], scalar1=half[:], scalar2=2.0 / N, op0=MUL, op1=MUL)
+            nc.vector.tensor_scalar(out=gain[:], in0=gs_c[:, 0:4], scalar1=one_half[:], scalar2=2.0 / N, op0=MUL, op1=MUL)
             nc.vector.tensor_sub(out=ba_diff[:], in0=ba_c[:, 0, 0:4], in1=ba_c[:, 1, 0:4])
 
-        def warm(columns, moving=None):
+        def warm(moving):
             scrap = bank("warm", [128, WARM])
-            nc.tensor.matmul(out=scrap[:, 0:columns], lhsT=zeros[:, 0:128], rhs=zeros[:, 0:columns] if moving is None else moving, start=True, stop=True)
+            nc.tensor.matmul(out=scrap[:], lhsT=zeros[:, 0:128], rhs=moving, start=True, stop=True)
 
         x_rows = {}
         x_bf = {}
@@ -105,7 +103,7 @@ def tile_radixsplitattentionpointwise_x1_kernel(tc, x, w, bias, gs, wa, ba, out_
                 x_scales[r, c] = sbuf("x_scales%d%d" % (r, c), [128, CH], U8)
 
         def load_x(r, c, k0, k1):
-            src = x[r, CB * c : CB * (c + 1)].rearrange("b n c -> (b n) c").rearrange("(q j) c -> q (j c)", j=4)
+            src = x[r, CB * c : CB * (c + 1)].rearrange("b n e -> (b n) e").rearrange("(q j) e -> q (j e)", j=4)
             part = sbuf("x_rows%d%d%d" % (r, c, k0), [128, 2 * C * (k1 - k0)], BF16)
             nc.sync.dma_start(out=part[:], in_=src[:, 2 * C * k0 : 2 * C * k1])
             for k in range(k0, k1):
@@ -141,19 +139,18 @@ def tile_radixsplitattentionpointwise_x1_kernel(tc, x, w, bias, gs, wa, ba, out_
         def load_w(nm):
             nc.sync.dma_start(out=w_rows[nm][:], in_=w_src[nm].rearrange("(p s) e -> p s e", s=4))
 
-        def w_views(nm):
-            dst = w_bf[nm][:].rearrange("p (t a i s) -> p a t i s", t=4, i=2, s=4)
-            src = w_rows[nm][:].rearrange("p s (a i t) -> p a t i s", i=2, t=4)
-            return dst, src
+        def w_lay(nm, m0, m1, eng):
+            dst = w_bf[nm][:].rearrange("p (t a o s) -> p a t o s", t=4, o=2, s=4)
+            src = w_rows[nm][:].rearrange("p s (a o t) -> p a t o s", o=2, t=4)
+            copy(eng, dst[:, m0 // 2 : m1 // 2], src[:, m0 // 2 : m1 // 2])
 
-        def w_lay(nm, i0, i1, eng):
-            dst, src = w_views(nm)
-            copy(eng, dst[:, 16 * i0 : 16 * i1], src[:, 16 * i0 : 16 * i1])
-
-        def w_lay_negated(nm, i0, i1):
-            dst = w_bf[nm][:].rearrange("p (t m s) -> p t m s", t=4, s=4)[:, :, 32 * i0 : 32 * i1]
-            src = w_rows[nm][:].rearrange("p s (m t) -> p t m s", t=4)[:, :, 32 * i0 : 32 * i1]
-            nc.scalar.activation(out=dst, in_=src, func=AF.Copy, scale=-1.0)
+        def w_lay_negated(nm, m0, m1, eng):
+            dst = w_bf[nm][:].rearrange("p (t m s) -> p t m s", t=4, s=4)[:, :, m0:m1]
+            src = w_rows[nm][:].rearrange("p s (m t) -> p t m s", t=4)[:, :, m0:m1]
+            if eng is V:
+                nc.vector.tensor_scalar(out=dst, in0=src, scalar1=-1.0, scalar2=None, op0=MUL)
+            else:
+                nc.scalar.activation(out=dst, in_=src, func=AF.Copy, scale=-1.0)
 
         def w_quantise(nm, t0, t1):
             cols = slice(128 * t0, 128 * t1)
@@ -197,35 +194,21 @@ def tile_radixsplitattentionpointwise_x1_kernel(tc, x, w, bias, gs, wa, ba, out_
 
         sum_ps = {}
         sum_sb = {}
-        pre_sum = {}
         s_ps = {}
 
-        def pre_add(c, t):
-            pre_sum[c, t] = sbuf("pre_sum%d%d" % (c, t), [128, N, CB], F32)
-            nc.vector.scalar_tensor_tensor(
-                out=pre_sum[c, t][:], in0=du[c][:, t, :, 1, :], scalar=2.0, in1=du[c][:, t, :, 0, :], op0=MUL, op1=ADD
-            )
-
         def sum_pair(c, t0):
-            blocks = {}
             for t in (t0, t0 + 1):
                 sum_ps[c, t] = bank("sum_ps%d%d" % (c, t), [128, 128])
-                if (c, t) in pre_sum:
-                    blocks[t] = [pre_sum[c, t][:, g : g + 2].rearrange("p g b -> p (g b)") for g in range(0, N, 2)]
-                else:
-                    blocks[t] = [du[c][:, t, g].rearrange("p a b -> p (a b)") for g in range(N)]
-            for step in range(N):
+            for g in range(N):
                 for t in (t0, t0 + 1):
-                    g = step - (N - len(blocks[t]))
-                    if g >= 0:
-                        nc.tensor.matmul(
-                            out=sum_ps[c, t][:],
-                            lhsT=blocks[t][g],
-                            rhs=ident[:],
-                            start=(g == 0),
-                            stop=(step == N - 1),
-                            is_transpose=True,
-                        )
+                    nc.tensor.matmul(
+                        out=sum_ps[c, t][:],
+                        lhsT=du[c][:, t, g].rearrange("p a b -> p (a b)"),
+                        rhs=ident[:],
+                        start=(g == 0),
+                        stop=(g == N - 1),
+                        is_transpose=True,
+                    )
 
         def sum_out(c, t):
             sum_sb[c, t] = sbuf("sum_sb%d%d" % (c, t), [128, 128], F32)
@@ -233,9 +216,15 @@ def tile_radixsplitattentionpointwise_x1_kernel(tc, x, w, bias, gs, wa, ba, out_
 
         def sum_fold(c):
             s_ps[c] = bank("s_ps%d" % c, [128, 4, CB])
+            nc.tensor.matmul(
+                out=s_ps[c][:].rearrange("p t b -> p (t b)"),
+                lhsT=ident_bf[:],
+                rhs=bias0_sum[:].rearrange("p t b -> p (t b)"),
+                start=True,
+                stop=False,
+            )
             for t in range(4):
-                nc.tensor.matmul(out=s_ps[c][:, t, :], lhsT=ident_bf[:], rhs=bias0_sum[:, t, :], start=True, stop=False)
-                nc.tensor.matmul(out=s_ps[c][:, t, :], lhsT=sum_sb[c, t][:], rhs=(fold_pair if (c, t) in pre_sum else fold_du)[:], start=False, stop=True)
+                nc.tensor.matmul(out=s_ps[c][:, t, :], lhsT=sum_sb[c, t][:], rhs=fold_du[:], start=False, stop=(t == 3))
 
         sg_bf = {}
         l_ps = {}
@@ -254,18 +243,19 @@ def tile_radixsplitattentionpointwise_x1_kernel(tc, x, w, bias, gs, wa, ba, out_
             )
 
         def logits(c):
-            for t in range(4):
-                if t % 2 == 0:
-                    l_ps[c, t // 2] = bank("l_ps%d%d" % (c, t // 2), [128, 2, B])
-                mx_pass(l_ps[c, t // 2][:, t % 2, :], "wa0", t, sg_codes, sg_scales, True, False)
-                mx_pass(l_ps[c, t // 2][:, t % 2, :], "wa1", t, sg_codes, sg_scales, False, True)
+            for t0 in (0, 2):
+                l_ps[c, t0] = bank("l_ps%d%d" % (c, t0), [128, 2, B])
+                for r in range(R):
+                    for t in (t0, t0 + 1):
+                        first, last = (r == 0 and t == t0), (r == R - 1 and t == t0 + 1)
+                        mx_pass(l_ps[c, t0][:, t - t0, :], "wa%d" % r, t, sg_codes, sg_scales, first, last)
 
         def softmax(c):
             a0[c] = sbuf("a0_%d" % c, [128, 4, CB], F32)
             for t in range(4):
                 nc.scalar.activation(
                     out=a0[c][:, t],
-                    in_=l_ps[c, t // 2][:, t % 2, CB * c : CB * (c + 1)],
+                    in_=l_ps[c, t - t % 2][:, t % 2, CB * c : CB * (c + 1)],
                     func=AF.Sigmoid,
                     bias=ba_diff[:, t : t + 1],
                     scale=sign[:],
@@ -296,8 +286,8 @@ def tile_radixsplitattentionpointwise_x1_kernel(tc, x, w, bias, gs, wa, ba, out_
                 op1=MUL,
             )
 
-        def add_u1(c, j, h0=0, h1=2):
-            items = slice(32 * h0, 32 * h1)
+        def add_u1(c, j, f0=0, f1=2):
+            items = slice(32 * f0, 32 * f1)
             nc.vector.tensor_add(
                 out=res[c][:, j].rearrange("p t (b h) -> p t b h", h=2)[:, :, items],
                 in0=weighted[c][:, :, 2 * j : 2 * j + 2, items].rearrange("p t h b -> p t b h"),
@@ -320,51 +310,49 @@ def tile_radixsplitattentionpointwise_x1_kernel(tc, x, w, bias, gs, wa, ba, out_
                 in_=res_rows[c][:, j0:j1].rearrange("q j p t -> q (j p t)"),
             )
 
-        words_out = out_1.rearrange("g p m t -> (g p) (m t)").bitcast(I32)
-        scales_out = out_2.rearrange("g q m -> (g q) m").bitcast(I32)
+        words_out = out_1.rearrange("one p token t -> (one p) (token t)").bitcast(I32)
+        scales_out = out_2.rearrange("one block token -> (one block) token").bitcast(I32)
 
-        def res_round(c, k, h0, h1, eng):
-            dst = res_bf[c][:].rearrange("p (a i k e) -> p k a e i", i=2, k=2, e=8)[:, k, 32 * h0 : 32 * h1]
-            src = res[c][:, 2 * k : 2 * k + 2].rearrange("p j t (a i) -> p a (j t) i", i=2)[:, 32 * h0 : 32 * h1]
+        def res_round(c, k, f0, f1, eng):
+            dst = res_bf[c][:].rearrange("p (a o k jt) -> p k a jt o", o=2, k=2, jt=8)[:, k, 32 * f0 : 32 * f1]
+            src = res[c][:, 2 * k : 2 * k + 2].rearrange("p j t (a o) -> p a (j t) o", o=2)[:, 32 * f0 : 32 * f1]
             copy(eng, dst, src)
 
-        def res_quantise(c, h0, h1):
+        def res_quantise(c, f):
             nc.vector.quantize_mx(
-                out=res_codes[c][:, 256 * h0 : 256 * h1].bitcast(FP8X4),
-                scales=res_scales[:, CH * c + 256 * h0 : CH * c + 256 * h1],
-                in_=res_bf[c][:, 1024 * h0 : 1024 * h1],
+                out=res_codes[c][:, 256 * f : 256 * (f + 1)].bitcast(FP8X4),
+                scales=res_scales[:, CH * c + 256 * f : CH * c + 256 * (f + 1)],
+                in_=res_bf[c][:, 1024 * f : 1024 * (f + 1)],
             )
 
-        def store_words(c, h0, h1):
-            nc.sync.dma_start(
-                out=words_out[:, CH * c + 256 * h0 : CH * c + 256 * h1], in_=res_codes[c][:, 256 * h0 : 256 * h1].bitcast(I32)
-            )
+        def store_words(c):
+            nc.sync.dma_start(out=words_out[:, CH * c : CH * (c + 1)], in_=res_codes[c][:].bitcast(I32))
 
         def store_scales():
-            for i in range(4):
-                nc.sync.dma_start(out=scales_out[4 * i : 4 * i + 4, :], in_=res_scales[32 * i : 32 * i + 4, :].bitcast(I32))
+            for quad in range(4):
+                nc.sync.dma_start(
+                    out=scales_out[4 * quad : 4 * quad + 4, :], in_=res_scales[32 * quad : 32 * quad + 4, :].bitcast(I32)
+                )
 
 
-        for r in (1, 0):
-            if r == 1:
-                load_x(r, 0, 0, 1)
-                load_x(r, 0, 1, 2)
-            else:
-                load_x(r, 0, 0, 2)
-            load_w("w%d" % r)
+        load_x(1, 0, 0, 1)
+        load_x(1, 0, 1, 2)
+        load_w("w1")
+        load_x(0, 0, 0, 2)
+        load_w("w0")
         for r in (1, 0):
             load_x(r, 1, 0, 2)
             load_w("wa%d" % (1 - r))
         load_gate_vectors()
 
-        warm(WARM)
-        warm(WARM)
+        warm(zeros[:])
+        warm(zeros[:])
         bias_constants()
         x_turn(1, 0)
-        warm(WARM)
-        warm(WARM)
-        w_lay("w1", 0, 3, V)
-        w_lay("w1", 3, 4, S)
+        warm(zeros[:])
+        warm(zeros[:])
+        w_lay("w1", 0, 96, V)
+        w_lay("w1", 96, 128, S)
         x_turn(0, 0)
         x_quantise(1, 0)
         w_quantise("w1", 0, 2)
@@ -372,28 +360,28 @@ def tile_radixsplitattentionpointwise_x1_kernel(tc, x, w, bias, gs, wa, ba, out_
         for t in range(4):
             product(1, 0, t)
             relu1(0, t)
-        w_lay("w0", 0, 4, V)
+
+        w_lay("w0", 0, 128, V)
         x_quantise(0, 0)
         w_quantise("w0", 0, 2)
         w_quantise("w0", 2, 4)
         x_turn(1, 1)
-        w_lay("wa0", 0, 2, V)
+        w_lay("wa0", 0, 64, V)
         for t in range(4):
             product(0, 0, t)
             diff0(0, t)
-        w_lay_negated("wa0", 2, 4)
+        w_lay_negated("wa0", 64, 128, S)
         x_turn(0, 1)
         x_quantise(1, 1)
-        w_lay("wa1", 2, 4, V)
+        w_lay("wa1", 64, 128, V)
+        w_lay_negated("wa1", 32, 64, V)
         x_quantise(0, 1)
-        w_lay_negated("wa1", 0, 1)
-        sum_pair(0, 0)
-        sum_out(0, 0)
-        sum_out(0, 1)
-        w_lay_negated("wa1", 1, 2)
-        sum_pair(0, 2)
-        sum_out(0, 2)
-        sum_out(0, 3)
+        w_lay_negated("wa1", 0, 32, S)
+
+        for t0 in (0, 2):
+            sum_pair(0, t0)
+            sum_out(0, t0)
+            sum_out(0, t0 + 1)
         w_quantise("wa0", 0, 4)
         gate_constants()
         w_quantise("wa1", 2, 4)
@@ -405,22 +393,20 @@ def tile_radixsplitattentionpointwise_x1_kernel(tc, x, w, bias, gs, wa, ba, out_
         w_quantise("wa1", 0, 2)
         sg_quantise(0)
         product(0, 1, 0)
-        product(1, 1, 2)
-        relu1(1, 2)
-        product(1, 1, 3)
-        relu1(1, 3)
+        for t in range(2, 4):
+            product(1, 1, t)
+            relu1(1, t)
         diff0(1, 0)
-        product(0, 1, 1)
-        product(0, 1, 2)
-        product(0, 1, 3)
+        for t in range(1, 4):
+            product(0, 1, t)
         logits(0)
         softmax(0)
         for t in range(1, 4):
             diff0(1, t)
-        for t in (0, 2):
-            sum_pair(1, t)
-            sum_out(1, t)
-            sum_out(1, t + 1)
+        for t0 in (0, 2):
+            sum_pair(1, t0)
+            sum_out(1, t0)
+            sum_out(1, t0 + 1)
         sum_fold(1)
 
         def weigh_first_piece(c):
@@ -433,7 +419,7 @@ def tile_radixsplitattentionpointwise_x1_kernel(tc, x, w, bias, gs, wa, ba, out_
         weigh_first_piece(0)
         res_turn(0, 0)
         res_turn(0, 1)
-        warm(WARM)
+        warm(zeros[:])
         res_round(0, 0, 0, 2, S)
         weigh(0, 1, 1)
         weigh(0, 1, 2)
@@ -449,40 +435,39 @@ def tile_radixsplitattentionpointwise_x1_kernel(tc, x, w, bias, gs, wa, ba, out_
         store_rows(0, 0, 2, nc.sync)
         res_turn(0, 2)
         res_turn(0, 3)
-        warm(WARM)
+        warm(zeros[:])
         res_out(0, 2)
         res_out(0, 3)
         store_rows(0, 2, 4, nc.sync)
         res_round(0, 1, 0, 2, S)
 
         weigh_first_piece(1)
-        warm(WARM, weighted[1][:, 3, 0:4].rearrange("p g b -> p (g b)"))
+        warm(weighted[1][:, 3, 0:4].rearrange("p g b -> p (g b)"))
         res_turn(1, 0)
         res_turn(1, 1)
         weigh(1, 1, 1)
-        warm(WARM, weighted[1][:, 1, 4:8].rearrange("p g b -> p (g b)"))
+        warm(weighted[1][:, 1, 4:8].rearrange("p g b -> p (g b)"))
         weigh(1, 1, 2)
         weigh(1, 1, 3)
-        res_out(1, 0)
-        store_rows(1, 0, 1, nc.sync)
-        res_out(1, 1)
-        store_rows(1, 1, 2, nc.sync)
-        res_quantise(0, 0, 1)
+        for j in range(2):
+            res_out(1, j)
+            store_rows(1, j, j + 1, nc.sync)
+        res_quantise(0, 0)
         res_round(1, 0, 0, 2, S)
         add_u1(1, 2)
         res_turn(1, 2)
-        res_quantise(0, 1, 2)
-        store_words(0, 0, 2)
-        add_u1(1, 3, 0, 1)
-        add_u1(1, 3, 1, 2)
+        res_quantise(0, 1)
+        store_words(0)
+        for f in range(2):
+            add_u1(1, 3, f, f + 1)
         res_turn(1, 3)
-        for h in range(2):
-            res_round(1, 1, h, h + 1, V)
+        for f in range(2):
+            res_round(1, 1, f, f + 1, V)
         res_out(1, 2)
         store_rows(1, 2, 3, nc.sync)
-        for h in range(2):
-            res_quantise(1, h, h + 1)
+        for f in range(2):
+            res_quantise(1, f)
         res_out(1, 3)
-        store_words(1, 0, 2)
+        store_words(1)
         store_rows(1, 3, 4, nc.scalar)
         store_scales()

@@ -140,8 +140,9 @@ def tile_radixsplitattentionpointwise_x1_kernel(tc, x, w, bias, gs, wa, ba, out_
             nc.sync.dma_start(out=w_rows[nm][:], in_=w_src[nm].rearrange("(p s) e -> p s e", s=4))
 
         def w_lay(nm, m0, m1, eng):
-            dst = w_bf[nm][:].rearrange("p (t a o s) -> p a t o s", t=4, o=2, s=4)
-            src = w_rows[nm][:].rearrange("p s (a o t) -> p a t o s", o=2, t=4)
+            walk = "p a s o t" if eng is V else "p a t o s"
+            dst = w_bf[nm][:].rearrange("p (t a o s) -> " + walk, t=4, o=2, s=4)
+            src = w_rows[nm][:].rearrange("p s (a o t) -> " + walk, o=2, t=4)
             copy(eng, dst[:, m0 // 2 : m1 // 2], src[:, m0 // 2 : m1 // 2])
 
         def w_lay_negated(nm, m0, m1, eng):

@@ -59,6 +59,9 @@ def tile_radixsplitattentionpointwise_x1_kernel(tc, x, w, bias, gs, wa, ba, out_
         make_identity(nc, ident[:])
         ident_bf = sbuf("ident_bf", [128, 128], BF16)
         nc.vector.tensor_copy(out=ident_bf[:], in_=ident[:])
+        fold = sbuf("fold", [128, 2, CB], F32)
+        nc.vector.tensor_add(out=fold[:, 0], in0=ident[:, 0:128:2], in1=ident[:, 1:128:2])
+        nc.vector.tensor_scalar(out=fold[:, 1], in0=fold[:, 0], scalar1=2.0, scalar2=None, op0=MUL)
         fold_du = sbuf("fold_du", [128, CB], F32)
         nc.vector.scalar_tensor_tensor(out=fold_du[:], in0=ident[:, CB:128], scalar=2.0, in1=ident[:, 0:CB], op0=MUL, op1=ADD)
         sg_codes = sbuf("sg_codes", [128, B], U32)
@@ -117,10 +120,13 @@ def tile_radixsplitattentionpointwise_x1_kernel(tc, x, w, bias, gs, wa, ba, out_
                     for i in range(2):
                         nc.tensor.transpose(ps[:, j, i, :], pairs[:, 256 * j + i : 256 * (j + 1) : 2], ident[:])
                 dst = x_bf[r, c][:, 2 * C * k : 2 * C * (k + 1)].bitcast(F32)
-                nc.scalar.copy(
-                    out=dst.rearrange("p (j h b i) -> p j h b i", j=2, h=2, i=2),
-                    in_=ps[:].rearrange("p j i (b h) -> p j h b i", h=2),
-                )
+                if c == 0:
+                    nc.scalar.copy(
+                        out=dst.rearrange("p (j h b i) -> p j h b i", j=2, h=2, i=2),
+                        in_=ps[:].rearrange("p j i (b h) -> p j h b i", h=2),
+                    )
+                else:
+                    nc.scalar.copy(out=dst.rearrange("p (j q i) -> p j q i", j=2, i=2), in_=ps[:].rearrange("p j i q -> p j q i"))
 
         def x_quantise(r, c):
             nc.vector.quantize_mx(out=x_codes[r, c][:].bitcast(FP8X4), scales=x_scales[r, c][:], in_=x_bf[r, c][:])
@@ -172,50 +178,53 @@ def tile_radixsplitattentionpointwise_x1_kernel(tc, x, w, bias, gs, wa, ba, out_
             )
 
         y = {}
-        du = {}
-        for c in range(NCH):
-            du[c] = sbuf("du%d" % c, [128, 4, N, 2, CB], F32)
+        du = sbuf("du", [128, 4, N, 2, CB], F32)
+        d = sbuf("d", [128, 4, 4, 128], F32)
+        u1 = sbuf("u1", [128, 4, 4, 128], F32)
 
         def product(r, c, t):
-            y[r, c, t] = bank("y%d%d%d" % (r, c, t), [128, N, CB])
+            y[r, c, t] = bank("y%d%d%d" % (r, c, t), [128, N, CB] if c == 0 else [128, 4, 128])
             mx_pass(y[r, c, t][:].rearrange("p g b -> p (g b)"), "w%d" % r, t, x_codes[r, c], x_scales[r, c], True, True)
 
+        def d_of(c, t):
+            return du[:, t, :, 0, :] if c == 0 else d[:, :, t, :]
+
+        def u1_of(c, t):
+            return du[:, t, :, 1, :] if c == 0 else u1[:, :, t, :]
+
         def relu1(c, t):
-            nc.scalar.activation(out=du[c][:, t, :, 1, :], in_=y[1, c, t][:], func=AF.Relu, bias=bias_c[:, 1, t : t + 1])
+            nc.scalar.activation(out=u1_of(c, t), in_=y[1, c, t][:], func=AF.Relu, bias=bias_c[:, 1, t : t + 1])
 
         def diff0(c, t):
             nc.vector.scalar_tensor_tensor(
-                out=du[c][:, t, :, 0, :],
-                in0=y[0, c, t][:],
-                scalar=neg_bias0[:, t : t + 1],
-                in1=du[c][:, t, :, 1, :],
-                op0=MAX,
-                op1=SUB,
+                out=d_of(c, t), in0=y[0, c, t][:], scalar=neg_bias0[:, t : t + 1], in1=u1_of(c, t), op0=MAX, op1=SUB
             )
+
+        def turn_add(out, src, start, stop):
+            nc.tensor.matmul(out=out, lhsT=src, rhs=ident[:], start=start, stop=stop, is_transpose=True)
 
         sum_ps = {}
         sum_sb = {}
         s_ps = {}
 
-        def sum_pair(c, t0):
+        def sum_rows(src, key, t0, t1):
+            sum_ps[key] = bank("sum_ps_" + key, [128, t1 - t0, 128])
+            for j in range(4):
+                for t in range(t0, t1):
+                    turn_add(sum_ps[key][:, t - t0, :], src[:, j, t, :], j == 0 and t == t0, j == 3 and t == t1 - 1)
+
+        def sum_pair(t0):
             for t in (t0, t0 + 1):
-                sum_ps[c, t] = bank("sum_ps%d%d" % (c, t), [128, 128])
+                sum_ps["du%d" % t] = bank("sum_ps_du%d" % t, [128, 1, 128])
             for g in range(N):
                 for t in (t0, t0 + 1):
-                    nc.tensor.matmul(
-                        out=sum_ps[c, t][:],
-                        lhsT=du[c][:, t, g].rearrange("p a b -> p (a b)"),
-                        rhs=ident[:],
-                        start=(g == 0),
-                        stop=(g == N - 1),
-                        is_transpose=True,
-                    )
+                    turn_add(sum_ps["du%d" % t][:, 0, :], du[:, t, g].rearrange("p a b -> p (a b)"), g == 0, g == N - 1)
 
-        def sum_out(c, t):
-            sum_sb[c, t] = sbuf("sum_sb%d%d" % (c, t), [128, 128], F32)
-            nc.scalar.copy(out=sum_sb[c, t][:], in_=sum_ps[c, t][:])
+        def sum_out(key, n):
+            sum_sb[key] = sbuf("sum_sb_" + key, [128, n, 128], F32)
+            nc.scalar.copy(out=sum_sb[key][:], in_=sum_ps[key][:])
 
-        def sum_fold(c):
+        def fold_open(c):
             s_ps[c] = bank("s_ps%d" % c, [128, 4, CB])
             nc.tensor.matmul(
                 out=s_ps[c][:].rearrange("p t b -> p (t b)"),
@@ -224,8 +233,9 @@ def tile_radixsplitattentionpointwise_x1_kernel(tc, x, w, bias, gs, wa, ba, out_
                 start=True,
                 stop=False,
             )
-            for t in range(4):
-                nc.tensor.matmul(out=s_ps[c][:, t, :], lhsT=sum_sb[c, t][:], rhs=fold_du[:], start=False, stop=(t == 3))
+
+        def fold_in(c, t, rows, matrix, stop):
+            nc.tensor.matmul(out=s_ps[c][:, t, :], lhsT=rows, rhs=matrix, start=False, stop=stop)
 
         sg_bf = {}
         l_ps = {}
@@ -252,55 +262,67 @@ def tile_radixsplitattentionpointwise_x1_kernel(tc, x, w, bias, gs, wa, ba, out_
                         mx_pass(l_ps[c, t0][:, t - t0, :], "wa%d" % r, t, sg_codes, sg_scales, first, last)
 
         def softmax(c):
-            a0[c] = sbuf("a0_%d" % c, [128, 4, CB], F32)
+            copies = 1 + c
+            a0[c] = sbuf("a0_%d" % c, [128, 4, CB, copies], F32)
             for t in range(4):
                 nc.scalar.activation(
                     out=a0[c][:, t],
-                    in_=l_ps[c, t - t % 2][:, t % 2, CB * c : CB * (c + 1)],
+                    in_=l_ps[c, t - t % 2][:, t % 2, CB * c : CB * (c + 1)].unsqueeze(2).to_broadcast([128, CB, copies]),
                     func=AF.Sigmoid,
                     bias=ba_diff[:, t : t + 1],
                     scale=sign[:],
                 )
 
-        weighted = {}
-        res = {}
+        weighted0 = sbuf("weighted0", [128, 4, N, CB], F32)
+        weighted1 = sbuf("weighted1", [128, 4, 4, 128], F32)
+        res = sbuf("res", [128, 4, 4, 128], F32)
         res_bf = {}
         res_codes = {}
         res_rows = {}
         res_ps = {}
         for c in range(NCH):
-            weighted[c] = sbuf("weighted%d" % c, [128, 4, N, CB], F32)
-            res[c] = sbuf("res%d" % c, [128, 4, 4, 128], F32)
             res_bf[c] = sbuf("res_bf%d" % c, [128, CH * 4], BF16)
             res_codes[c] = sbuf("res_codes%d" % c, [128, CH], U32)
             res_rows[c] = sbuf("res_rows%d" % c, [128, 4, 128, 4], F32)
         res_scales = sbuf("res_scales", [128, T], U8)
 
         def weigh(c, k, t):
-            groups = slice(4 * k, 4 * (k + 1))
+            if c == 0:
+                out, src, reps = weighted0[:, t, 4 * k : 4 * k + 4], du[:, t, 4 * k : 4 * k + 4, 0, :], 4
+            else:
+                out, src, reps = weighted1[:, 2 * k : 2 * k + 2, t, :], d[:, 2 * k : 2 * k + 2, t, :], 2
             nc.vector.scalar_tensor_tensor(
-                out=weighted[c][:, t, groups],
-                in0=du[c][:, t, groups, 0, :],
+                out=out,
+                in0=src,
                 scalar=bias_c[:, 0, t : t + 1],
-                in1=a0[c][:, t].unsqueeze(1).to_broadcast([128, 4, CB]),
+                in1=a0[c][:, t].rearrange("p b h -> p (b h)").unsqueeze(1).to_broadcast([128, reps, 256 // reps]),
                 op0=ADD,
                 op1=MUL,
             )
 
-        def add_u1(c, j, f0=0, f1=2):
+        def add_u1(j, f0=0, f1=2):
             items = slice(32 * f0, 32 * f1)
             nc.vector.tensor_add(
-                out=res[c][:, j].rearrange("p t (b h) -> p t b h", h=2)[:, :, items],
-                in0=weighted[c][:, :, 2 * j : 2 * j + 2, items].rearrange("p t h b -> p t b h"),
-                in1=du[c][:, :, 2 * j : 2 * j + 2, 1, items].rearrange("p t h b -> p t b h"),
+                out=res[:, j].rearrange("p t (b h) -> p t b h", h=2)[:, :, items],
+                in0=weighted0[:, :, 2 * j : 2 * j + 2, items].rearrange("p t h b -> p t b h"),
+                in1=du[:, :, 2 * j : 2 * j + 2, 1, items].rearrange("p t h b -> p t b h"),
             )
 
         rows_out = out_0.rearrange("b n e -> (b n) e").rearrange("(c q j) e -> c q j e", c=NCH, j=4)
 
-        def res_turn(c, j):
-            res_ps[c, j] = bank("res_ps%d%d" % (c, j), [128, 4, 128])
+        def res_turn(j):
+            res_ps[0, j] = bank("res_ps0%d" % j, [128, 4, 128])
             for t in range(4):
-                nc.tensor.transpose(res_ps[c, j][:, t, :], res[c][:, j, t, :], ident[:])
+                nc.tensor.transpose(res_ps[0, j][:, t, :], res[:, j, t, :], ident[:])
+
+        def turn_u1(j):
+            res_ps[1, j] = bank("res_ps1%d" % j, [128, 4, 128])
+            for t in range(4):
+                turn_add(res_ps[1, j][:, t, :], u1[:, j, t, :], t == 0, False)
+
+        def turn_weighted(j):
+            for t in range(4):
+                turn_add(res_ps[1, j][:, t, :], weighted1[:, j, t, :], False, t == 3)
 
         def res_out(c, j):
             nc.scalar.copy(out=res_rows[c][:, j], in_=res_ps[c, j][:].rearrange("q t p -> q p t"))
@@ -314,10 +336,17 @@ def tile_radixsplitattentionpointwise_x1_kernel(tc, x, w, bias, gs, wa, ba, out_
         words_out = out_1.rearrange("one p token t -> (one p) (token t)").bitcast(I32)
         scales_out = out_2.rearrange("one block token -> (one block) token").bitcast(I32)
 
-        def res_round(c, k, f0, f1, eng):
-            dst = res_bf[c][:].rearrange("p (a o k jt) -> p k a jt o", o=2, k=2, jt=8)[:, k, 32 * f0 : 32 * f1]
-            src = res[c][:, 2 * k : 2 * k + 2].rearrange("p j t (a o) -> p a (j t) o", o=2)[:, 32 * f0 : 32 * f1]
-            copy(eng, dst, src)
+        def pairs_of(tile, k, f0, f1):
+            return tile[:, 2 * k : 2 * k + 2].rearrange("p j t (a o) -> p a (j t) o", o=2)[:, 32 * f0 : 32 * f1]
+
+        def rounded(c, k, f0, f1):
+            return res_bf[c][:].rearrange("p (a o k jt) -> p k a jt o", o=2, k=2, jt=8)[:, k, 32 * f0 : 32 * f1]
+
+        def res_round(k, f0, f1, eng):
+            copy(eng, rounded(0, k, f0, f1), pairs_of(res, k, f0, f1))
+
+        def add_round(k, f):
+            nc.vector.tensor_add(out=rounded(1, k, f, f + 1), in0=pairs_of(weighted1, k, f, f + 1), in1=pairs_of(u1, k, f, f + 1))
 
         def res_quantise(c, f):
             nc.vector.quantize_mx(
@@ -326,12 +355,15 @@ def tile_radixsplitattentionpointwise_x1_kernel(tc, x, w, bias, gs, wa, ba, out_
                 in_=res_bf[c][:, 1024 * f : 1024 * (f + 1)],
             )
 
-        def store_words(c):
-            nc.sync.dma_start(out=words_out[:, CH * c : CH * (c + 1)], in_=res_codes[c][:].bitcast(I32))
+        def store_words(c, f0, f1):
+            nc.sync.dma_start(
+                out=words_out[:, CH * c + 256 * f0 : CH * c + 256 * f1], in_=res_codes[c][:, 256 * f0 : 256 * f1].bitcast(I32)
+            )
 
         def store_scales():
             for quad in range(4):
-                nc.sync.dma_start(
+                queue = nc.scalar if quad % 2 else nc.sync
+                queue.dma_start(
                     out=scales_out[4 * quad : 4 * quad + 4, :], in_=res_scales[32 * quad : 32 * quad + 4, :].bitcast(I32)
                 )
 
@@ -380,16 +412,18 @@ def tile_radixsplitattentionpointwise_x1_kernel(tc, x, w, bias, gs, wa, ba, out_
         w_lay_negated("wa1", 0, 32, S)
 
         for t0 in (0, 2):
-            sum_pair(0, t0)
-            sum_out(0, t0)
-            sum_out(0, t0 + 1)
+            sum_pair(t0)
+            sum_out("du%d" % t0, 1)
+            sum_out("du%d" % (t0 + 1), 1)
         w_quantise("wa0", 0, 4)
         gate_constants()
         w_quantise("wa1", 2, 4)
         for t in range(2):
             product(1, 1, t)
             relu1(1, t)
-        sum_fold(0)
+        fold_open(0)
+        for t in range(4):
+            fold_in(0, t, sum_sb["du%d" % t][:, 0], fold_du[:], t == 3)
         sg_round(0)
         w_quantise("wa1", 0, 2)
         sg_quantise(0)
@@ -404,71 +438,64 @@ def tile_radixsplitattentionpointwise_x1_kernel(tc, x, w, bias, gs, wa, ba, out_
         softmax(0)
         for t in range(1, 4):
             diff0(1, t)
+        sum_rows(u1, "u", 0, 4)
+        sum_out("u", 4)
         for t0 in (0, 2):
-            sum_pair(1, t0)
-            sum_out(1, t0)
-            sum_out(1, t0 + 1)
-        sum_fold(1)
+            sum_rows(d, "d%d" % t0, t0, t0 + 2)
+            sum_out("d%d" % t0, 2)
+        fold_open(1)
+        for t in range(4):
+            fold_in(1, t, sum_sb["u"][:, t], fold[:, 1], False)
+        for t in range(4):
+            fold_in(1, t, sum_sb["d%d" % (t - t % 2)][:, t % 2], fold[:, 0], t == 3)
 
-        def weigh_first_piece(c):
-            for t in range(4):
-                weigh(c, 0, t)
-            weigh(c, 1, 0)
-            add_u1(c, 0)
-            add_u1(c, 1)
-
-        weigh_first_piece(0)
-        res_turn(0, 0)
-        res_turn(0, 1)
-        warm(zeros[:])
-        res_round(0, 0, 0, 2, S)
-        weigh(0, 1, 1)
-        weigh(0, 1, 2)
-        sg_round(1)
-        weigh(0, 1, 3)
-        sg_quantise(1)
-        add_u1(0, 2)
-        add_u1(0, 3)
-        logits(1)
-        res_out(0, 0)
-        softmax(1)
-        res_out(0, 1)
-        store_rows(0, 0, 2, nc.sync)
-        res_turn(0, 2)
-        res_turn(0, 3)
-        warm(zeros[:])
-        res_out(0, 2)
-        res_out(0, 3)
-        store_rows(0, 2, 4, nc.sync)
-        res_round(0, 1, 0, 2, S)
-
-        weigh_first_piece(1)
-        warm(weighted[1][:, 3, 0:4].rearrange("p g b -> p (g b)"))
-        res_turn(1, 0)
-        res_turn(1, 1)
-        weigh(1, 1, 1)
-        warm(weighted[1][:, 1, 4:8].rearrange("p g b -> p (g b)"))
-        weigh(1, 1, 2)
-        weigh(1, 1, 3)
+        for t in range(4):
+            weigh(0, 0, t)
+        weigh(0, 1, 0)
+        add_u1(0)
+        add_u1(1)
+        res_round(0, 0, 2, S)
         for j in range(2):
-            res_out(1, j)
-            store_rows(1, j, j + 1, nc.sync)
-        res_quantise(0, 0)
-        res_round(1, 0, 0, 2, S)
-        add_u1(1, 2)
-        res_turn(1, 2)
-        res_quantise(0, 1)
-        store_words(0)
+            res_turn(j)
+            res_out(0, j)
+            store_rows(0, j, j + 1, nc.sync)
+        for t in range(1, 4):
+            weigh(0, 1, t)
+        sg_round(1)
+        add_u1(2, 0, 1)
+        sg_quantise(1)
+        add_u1(2, 1, 2)
+        add_u1(3, 0, 1)
+        add_u1(3, 1, 2)
+        turn_u1(0)
+        turn_u1(1)
+        logits(1)
+        softmax(1)
         for f in range(2):
-            add_u1(1, 3, f, f + 1)
-        res_turn(1, 3)
+            res_round(1, f, f + 1, V)
         for f in range(2):
-            res_round(1, 1, f, f + 1, V)
-        res_out(1, 2)
-        store_rows(1, 2, 3, nc.sync)
+            res_quantise(0, f)
+        store_words(0, 0, 2)
+        for j in range(2, 4):
+            res_turn(j)
+            res_out(0, j)
+            store_rows(0, j, j + 1, nc.sync)
+
+        for j in range(2, 4):
+            turn_u1(j)
+        warm(zeros[:])
+        for k in range(2):
+            for t in range(4):
+                weigh(1, k, t)
+            for j in (2 * k, 2 * k + 1):
+                turn_weighted(j)
+                res_out(1, j)
+                store_rows(1, j, j + 1, nc.sync)
+        add_round(0, 0)
+        add_round(1, 0)
+        add_round(0, 1)
+        add_round(1, 1)
         for f in range(2):
             res_quantise(1, f)
-        res_out(1, 3)
-        store_words(1)
-        store_rows(1, 3, 4, nc.scalar)
+            store_words(1, f, f + 1)
         store_scales()

@@ -126,7 +126,10 @@ def tile_radixsplitattentionpointwise_x1_kernel(tc, x, w, bias, gs, wa, ba, out_
                         in_=ps[:].rearrange("p j i (b h) -> p j h b i", h=2),
                     )
                 else:
-                    nc.scalar.copy(out=dst.rearrange("p (j q i) -> p j q i", j=2, i=2), in_=ps[:].rearrange("p j i q -> p j q i"))
+                    nc.scalar.copy(
+                        out=x_bf[r, c][:].bitcast(F32).rearrange("p (h k b o i) -> p k h b o i", h=2, k=2, o=2, i=2)[:, k],
+                        in_=ps[:].rearrange("p o i (b h) -> p h b o i", h=2),
+                    )
 
         def x_quantise(r, c):
             nc.vector.quantize_mx(out=x_codes[r, c][:].bitcast(FP8X4), scales=x_scales[r, c][:], in_=x_bf[r, c][:])
@@ -327,6 +330,12 @@ def tile_radixsplitattentionpointwise_x1_kernel(tc, x, w, bias, gs, wa, ba, out_
         def res_out(c, j):
             nc.scalar.copy(out=res_rows[c][:, j], in_=res_ps[c, j][:].rearrange("q t p -> q p t"))
 
+        def store_rows1(j):
+            nc.sync.dma_start(
+                out=out_0[CB:B, 2 * j : 2 * j + 2, :].rearrange("b o e -> b (o e)"),
+                in_=res_rows[1][:, j].rearrange("q p t -> q (p t)"),
+            )
+
         def store_rows(c, j0, j1, queue):
             queue.dma_start(
                 out=rows_out[c, :, j0:j1, :].rearrange("q j e -> q (j e)"),
@@ -345,8 +354,14 @@ def tile_radixsplitattentionpointwise_x1_kernel(tc, x, w, bias, gs, wa, ba, out_
         def res_round(k, f0, f1, eng):
             copy(eng, rounded(0, k, f0, f1), pairs_of(res, k, f0, f1))
 
-        def add_round(k, f):
-            nc.vector.tensor_add(out=rounded(1, k, f, f + 1), in0=pairs_of(weighted1, k, f, f + 1), in1=pairs_of(u1, k, f, f + 1))
+        def add_round(j, f0, f1):
+            items = slice(32 * f0, 32 * f1)
+            walk = "p t (b o) -> p b t o"
+            nc.vector.tensor_add(
+                out=res_bf[1][:].rearrange("p (b j o t) -> p j b t o", j=4, o=2, t=4)[:, j, items],
+                in0=weighted1[:, j].rearrange(walk, o=2)[:, items],
+                in1=u1[:, j].rearrange(walk, o=2)[:, items],
+            )
 
         def res_quantise(c, f):
             nc.vector.quantize_mx(
@@ -490,11 +505,11 @@ def tile_radixsplitattentionpointwise_x1_kernel(tc, x, w, bias, gs, wa, ba, out_
             for j in (2 * k, 2 * k + 1):
                 turn_weighted(j)
                 res_out(1, j)
-                store_rows(1, j, j + 1, nc.sync)
-        add_round(0, 0)
-        add_round(1, 0)
-        add_round(0, 1)
-        add_round(1, 1)
+                store_rows1(j)
+        for j in range(3):
+            add_round(j, 0, 2)
+        for f in range(2):
+            add_round(3, f, f + 1)
         for f in range(2):
             res_quantise(1, f)
             store_words(1, f, f + 1)

@@ -211,10 +211,17 @@ def tile_radixsplitattentionpointwise_x1_kernel(tc, x, w, bias, gs, wa, ba, out_
         s_ps = {}
 
         def sum_rows(src, key, t0, t1):
-            sum_ps[key] = bank("sum_ps_" + key, [128, t1 - t0, 128])
+            n = (t1 - t0) // 2
+            for odd in range(2):
+                sum_ps[key, odd] = bank("sum_ps_%s%d" % (key, odd), [128, n, 128])
             for j in range(4):
-                for t in range(t0, t1):
-                    turn_add(sum_ps[key][:, t - t0, :], src[:, j, t, :], j == 0 and t == t0, j == 3 and t == t1 - 1)
+                for t in range(t1 - t0):
+                    turn_add(sum_ps[key, t % 2][:, t // 2, :], src[:, j, t0 + t, :], j == 0 and t < 2, j == 3 and t // 2 == n - 1)
+
+        def rows_out_of(key, n):
+            for odd in range(2):
+                sum_sb[key, odd] = sbuf("sum_sb_%s%d" % (key, odd), [128, n, 128], F32)
+                nc.scalar.copy(out=sum_sb[key, odd][:], in_=sum_ps[key, odd][:])
 
         def sum_pair(t0):
             for t in (t0, t0 + 1):
@@ -318,14 +325,17 @@ def tile_radixsplitattentionpointwise_x1_kernel(tc, x, w, bias, gs, wa, ba, out_
             for t in range(4):
                 nc.tensor.transpose(res_ps[0, j][:, t, :], res[:, j, t, :], ident[:])
 
-        def turn_u1(j):
-            res_ps[1, j] = bank("res_ps1%d" % j, [128, 4, 128])
+        def turn_u1(k):
+            for j in (2 * k, 2 * k + 1):
+                res_ps[1, j] = bank("res_ps1%d" % j, [128, 4, 128])
             for t in range(4):
-                turn_add(res_ps[1, j][:, t, :], u1[:, j, t, :], t == 0, False)
+                for j in (2 * k, 2 * k + 1):
+                    turn_add(res_ps[1, j][:, t, :], u1[:, j, t, :], t == 0, False)
 
-        def turn_weighted(j):
+        def turn_weighted(k):
             for t in range(4):
-                turn_add(res_ps[1, j][:, t, :], weighted1[:, j, t, :], False, t == 3)
+                for j in (2 * k, 2 * k + 1):
+                    turn_add(res_ps[1, j][:, t, :], weighted1[:, j, t, :], False, t == 3)
 
         def res_out(c, j):
             nc.scalar.copy(out=res_rows[c][:, j], in_=res_ps[c, j][:].rearrange("q t p -> q p t"))
@@ -454,15 +464,15 @@ def tile_radixsplitattentionpointwise_x1_kernel(tc, x, w, bias, gs, wa, ba, out_
         for t in range(1, 4):
             diff0(1, t)
         sum_rows(u1, "u", 0, 4)
-        sum_out("u", 4)
+        rows_out_of("u", 2)
         for t0 in (0, 2):
             sum_rows(d, "d%d" % t0, t0, t0 + 2)
-            sum_out("d%d" % t0, 2)
+            rows_out_of("d%d" % t0, 1)
         fold_open(1)
         for t in range(4):
-            fold_in(1, t, sum_sb["u"][:, t], fold[:, 1], False)
+            fold_in(1, t, sum_sb["u", t % 2][:, t // 2], fold[:, 1], False)
         for t in range(4):
-            fold_in(1, t, sum_sb["d%d" % (t - t % 2)][:, t % 2], fold[:, 0], t == 3)
+            fold_in(1, t, sum_sb["d%d" % (t - t % 2), t % 2][:, 0], fold[:, 0], t == 3)
 
         for t in range(4):
             weigh(0, 0, t)
@@ -472,8 +482,8 @@ def tile_radixsplitattentionpointwise_x1_kernel(tc, x, w, bias, gs, wa, ba, out_
         res_round(0, 0, 2, S)
         for j in range(2):
             res_turn(j)
-            res_out(0, j)
-            store_rows(0, j, j + 1, nc.sync)
+        res_out(0, 0)
+        store_rows(0, 0, 1, nc.sync)
         for t in range(1, 4):
             weigh(0, 1, t)
         sg_round(1)
@@ -482,10 +492,10 @@ def tile_radixsplitattentionpointwise_x1_kernel(tc, x, w, bias, gs, wa, ba, out_
         add_u1(2, 1, 2)
         add_u1(3, 0, 1)
         add_u1(3, 1, 2)
-        turn_u1(0)
-        turn_u1(1)
         logits(1)
         softmax(1)
+        res_out(0, 1)
+        store_rows(0, 1, 2, nc.sync)
         for f in range(2):
             res_round(1, f, f + 1, V)
         for f in range(2):
@@ -496,14 +506,13 @@ def tile_radixsplitattentionpointwise_x1_kernel(tc, x, w, bias, gs, wa, ba, out_
             res_out(0, j)
             store_rows(0, j, j + 1, nc.sync)
 
-        for j in range(2, 4):
-            turn_u1(j)
-        warm(zeros[:])
+        for k in range(2):
+            turn_u1(k)
         for k in range(2):
             for t in range(4):
                 weigh(1, k, t)
+            turn_weighted(k)
             for j in (2 * k, 2 * k + 1):
-                turn_weighted(j)
                 res_out(1, j)
                 store_rows1(j)
         for j in range(3):

@@ -387,8 +387,7 @@ def tile_radixsplitattentionpointwise_x1_kernel(tc, x, w, bias, gs, wa, ba, out_
 
         def store_scales():
             for quad in range(4):
-                queue = nc.scalar if quad % 2 else nc.sync
-                queue.dma_start(
+                nc.scalar.dma_start(
                     out=scales_out[4 * quad : 4 * quad + 4, :], in_=res_scales[32 * quad : 32 * quad + 4, :].bitcast(I32)
                 )
 

@@ -431,9 +431,8 @@ def tile_radixsplitattentionpointwise_x1_kernel(tc, x, w, bias, gs, wa, ba, out_
         x_turn(0, 1)
         x_quantise(1, 1)
         w_lay("wa1", 64, 128, V)
-        w_lay_negated("wa1", 32, 64, V)
+        w_lay_negated("wa1", 0, 64, V)
         x_quantise(0, 1)
-        w_lay_negated("wa1", 0, 32, S)
 
         for t0 in (0, 2):
             sum_pair(t0)

@@ -480,35 +480,37 @@ def tile_radixsplitattentionpointwise_x1_kernel(tc, x, w, bias, gs, wa, ba, out_
         res_round(0, 0, 2, S)
         for j in range(2):
             res_turn(j)
+        turn_u1(0)
         res_out(0, 0)
         store_rows(0, 0, 1, nc.sync)
-        for t in range(1, 4):
-            weigh(0, 1, t)
+        res_out(0, 1)
+        store_rows(0, 1, 2, nc.sync)
+        weigh(0, 1, 1)
+        weigh(0, 1, 2)
+        weigh(0, 1, 3)
         sg_round(1)
         add_u1(2, 0, 1)
         sg_quantise(1)
-        add_u1(2, 1, 2)
         add_u1(3, 0, 1)
+        add_u1(2, 1, 2)
+        res_round(1, 0, 1, V)
         add_u1(3, 1, 2)
+        res_quantise(0, 0)
         logits(1)
         softmax(1)
-        res_out(0, 1)
-        store_rows(0, 1, 2, nc.sync)
-        for f in range(2):
-            res_round(1, f, f + 1, V)
-        for f in range(2):
-            res_quantise(0, f)
-        store_words(0, 0, 2)
+        res_round(1, 1, 2, S)
         for j in range(2, 4):
             res_turn(j)
             res_out(0, j)
             store_rows(0, j, j + 1, nc.sync)
 
-        for k in range(2):
-            turn_u1(k)
+        turn_u1(1)
         for k in range(2):
             for t in range(4):
                 weigh(1, k, t)
+            if k == 0:
+                res_quantise(0, 1)
+                store_words(0, 0, 2)
             turn_weighted(k)
             for j in (2 * k, 2 * k + 1):
                 res_out(1, j)

@@ -387,7 +387,7 @@ def tile_radixsplitattentionpointwise_x1_kernel(tc, x, w, bias, gs, wa, ba, out_
 
         def store_scales():
             for quad in range(4):
-                nc.scalar.dma_start(
+                (nc.scalar if quad < 2 else nc.sync).dma_start(
                     out=scales_out[4 * quad : 4 * quad + 4, :], in_=res_scales[32 * quad : 32 * quad + 4, :].bitcast(I32)
                 )
 
@@ -430,7 +430,8 @@ def tile_radixsplitattentionpointwise_x1_kernel(tc, x, w, bias, gs, wa, ba, out_
         w_lay_negated("wa0", 64, 128, S)
         x_turn(0, 1)
         x_quantise(1, 1)
-        w_lay("wa1", 64, 128, V)
+        w_lay("wa1", 112, 128, S)
+        w_lay("wa1", 64, 112, V)
         w_lay_negated("wa1", 0, 64, V)
         x_quantise(0, 1)
 

from contextlib import ExitStack

import concourse.mybir as mybir
from concourse.masks import make_identity

F32 = mybir.dt.float32
BF16 = mybir.dt.bfloat16
U32 = mybir.dt.uint32
I32 = mybir.dt.int32
U8 = mybir.dt.uint8
FP8X4 = mybir.dt.float8_e4m3fn_x4
ADD = mybir.AluOpType.add
SUB = mybir.AluOpType.subtract
MUL = mybir.AluOpType.mult
MAX = mybir.AluOpType.max
AF = mybir.ActivationFunctionType

R, B, N, C, E = 2, 128, 8, 512, 512
T = B * N
FLOPS = 2 * R * T * C * E + 2 * R * B * E * E

CB = 64
CH = CB * N
NCH = B // CB
BANKS = 8
WARM = 256


def tile_radixsplitattentionpointwise_x1_kernel(tc, x, w, bias, gs, wa, ba, out_0, out_1, out_2):
    nc = tc.nc
    with ExitStack() as ctx:
        sb = ctx.enter_context(tc.tile_pool(name="sb", bufs=1))
        pp = ctx.enter_context(tc.psum_pool(name="pp", bufs=1))
        ctx.enter_context(tc.manual_schedule())
        V, S = nc.vector, nc.scalar

        def sbuf(name, shape, dtype):
            return sb.tile(shape, dtype, name=name, align_bytes=64)

        def bank(name, shape):
            return pp.tile(shape, F32, name=name, tag="bank", bufs=BANKS)

        def copy(eng, dst, src):
            if eng is V:
                nc.vector.tensor_copy(out=dst, in_=src)
            else:
                nc.scalar.copy(out=dst, in_=src)

        bias_c = sbuf("bias_c", [128, 2, 16], BF16)
        ba_c = sbuf("ba_c", [128, 2, 16], BF16)
        gs_c = sbuf("gs_c", [128, 16], BF16)
        nc.scalar.dma_start(out=bias_c[:, :, 0:4], in_=bias.rearrange("r (p t) -> p r t", t=4))
        zeros = sbuf("zeros", [128, WARM], F32)
        nc.vector.memset(zeros[:], 0.0)
        one_half = sbuf("one_half", [128, 1], F32)
        nc.scalar.activation(out=one_half[:], in_=zeros[:, 0:1], func=AF.Sigmoid)

        ident = sbuf("ident", [128, 128], F32)
        make_identity(nc, ident[:])
        ident_bf = sbuf("ident_bf", [128, 128], BF16)
        nc.vector.tensor_copy(out=ident_bf[:], in_=ident[:])
        fold = sbuf("fold", [128, 2, CB], F32)
        nc.vector.tensor_add(out=fold[:, 0], in0=ident[:, 0:128:2], in1=ident[:, 1:128:2])
        nc.vector.tensor_scalar(out=fold[:, 1], in0=fold[:, 0], scalar1=2.0, scalar2=None, op0=MUL)
        fold_du = sbuf("fold_du", [128, CB], F32)
        nc.vector.scalar_tensor_tensor(out=fold_du[:], in0=ident[:, CB:128], scalar=2.0, in1=ident[:, 0:CB], op0=MUL, op1=ADD)
        sg_codes = sbuf("sg_codes", [128, B], U32)
        sg_scales = sbuf("sg_scales", [128, B], U8)
        nc.gpsimd.memset(sg_codes[:], 0)
        nc.gpsimd.memset(sg_scales[:].bitcast(U32), 0)
        sign = sbuf("sign", [128, 1], F32)
        nc.gpsimd.memset(sign[0:64], 1.0)
        nc.gpsimd.memset(sign[64:128], -1.0)

        neg_bias0 = sbuf("neg_bias0", [128, 4], F32)
        bias0_sum = sbuf("bias0_sum", [128, 4, CB], BF16)
        gain = sbuf("gain", [128, 4], F32)
        ba_diff = sbuf("ba_diff", [128, 4], F32)

        def bias_constants():
            nc.scalar.activation(out=neg_bias0[:], in_=bias_c[:, 0, 0:4], func=AF.Copy, scale=-1.0)
            nc.scalar.activation(
                out=bias0_sum[:], in_=bias_c[:, 0, 0:4].unsqueeze(2).to_broadcast([128, 4, CB]), func=AF.Copy, scale=float(N)
            )

        def load_gate_vectors():
            nc.sync.dma_start(out=gs_c[:, 0:4], in_=gs.rearrange("(p t) -> p t", t=4))
            nc.sync.dma_start(out=ba_c[:, :, 0:4], in_=ba.rearrange("r (p t) -> p r t", t=4))

        def gate_constants():
            nc.vector.tensor_scalar(out=gain[:], in0=gs_c[:, 0:4], scalar1=one_half[:], scalar2=2.0 / N, op0=MUL, op1=MUL)
            nc.vector.tensor_sub(out=ba_diff[:], in0=ba_c[:, 0, 0:4], in1=ba_c[:, 1, 0:4])

        def warm(moving):
            scrap = bank("warm", [128, WARM])
            nc.tensor.matmul(out=scrap[:], lhsT=zeros[:, 0:128], rhs=moving, start=True, stop=True)

        x_rows = {}
        x_bf = {}
        x_codes = {}
        x_scales = {}
        for c in range(NCH):
            for r in range(R):
                x_bf[r, c] = sbuf("x_bf%d%d" % (r, c), [128, 4 * CH], BF16)
                x_codes[r, c] = sbuf("x_codes%d%d" % (r, c), [128, CH], U32)
                x_scales[r, c] = sbuf("x_scales%d%d" % (r, c), [128, CH], U8)

        def load_x(r, c, k0, k1):
            src = x[r, CB * c : CB * (c + 1)].rearrange("b n e -> (b n) e").rearrange("(q j) e -> q (j e)", j=4)
            part = sbuf("x_rows%d%d%d" % (r, c, k0), [128, 2 * C * (k1 - k0)], BF16)
            nc.sync.dma_start(out=part[:], in_=src[:, 2 * C * k0 : 2 * C * k1])
            for k in range(k0, k1):
                x_rows[r, c, k] = part[:, 2 * C * (k - k0) : 2 * C * (k - k0 + 1)]

        def x_turn(r, c):
            for k in range(2):
                ps = bank("x_ps%d%d%d" % (r, c, k), [128, 2, 2, 128])
                pairs = x_rows[r, c, k].bitcast(F32)
                for j in range(2):
                    for i in range(2):
                        nc.tensor.transpose(ps[:, j, i, :], pairs[:, 256 * j + i : 256 * (j + 1) : 2], ident[:])
                dst = x_bf[r, c][:, 2 * C * k : 2 * C * (k + 1)].bitcast(F32)
                if c == 0:
                    nc.scalar.copy(
                        out=dst.rearrange("p (j h b i) -> p j h b i", j=2, h=2, i=2),
                        in_=ps[:].rearrange("p j i (b h) -> p j h b i", h=2),
                    )
                else:
                    nc.scalar.copy(
                        out=x_bf[r, c][:].bitcast(F32).rearrange("p (h k b o i) -> p k h b o i", h=2, k=2, o=2, i=2)[:, k],
                        in_=ps[:].rearrange("p o i (b h) -> p h b o i", h=2),
                    )

        def x_quantise(r, c):
            nc.vector.quantize_mx(out=x_codes[r, c][:].bitcast(FP8X4), scales=x_scales[r, c][:], in_=x_bf[r, c][:])

        w_src = {"w0": w[0], "w1": w[1], "wa0": wa[0], "wa1": wa[1]}
        w_rows = {}
        w_bf = {}
        w_codes = {}
        w_scales = {}
        for nm in w_src:
            w_rows[nm] = sbuf("w_rows_" + nm, [128, 4, E], BF16)
            w_bf[nm] = sbuf("w_bf_" + nm, [128, 4 * E], BF16)
            w_codes[nm] = sbuf("w_codes_" + nm, [128, E], U32)
            w_scales[nm] = sbuf("w_scales_" + nm, [128, E], U8)

        def load_w(nm):
            nc.sync.dma_start(out=w_rows[nm][:], in_=w_src[nm].rearrange("(p s) e -> p s e", s=4))

        def w_lay(nm, m0, m1, eng):
            walk = "p a s o t" if eng is V else "p a t o s"
            dst = w_bf[nm][:].rearrange("p (t a o s) -> " + walk, t=4, o=2, s=4)
            src = w_rows[nm][:].rearrange("p s (a o t) -> " + walk, o=2, t=4)
            copy(eng, dst[:, m0 // 2 : m1 // 2], src[:, m0 // 2 : m1 // 2])

        def w_lay_negated(nm, m0, m1, eng):
            dst = w_bf[nm][:].rearrange("p (t m s) -> p t m s", t=4, s=4)[:, :, m0:m1]
            src = w_rows[nm][:].rearrange("p s (m t) -> p t m s", t=4)[:, :, m0:m1]
            if eng is V:
                nc.vector.tensor_scalar(out=dst, in0=src, scalar1=-1.0, scalar2=None, op0=MUL)
            else:
                nc.scalar.activation(out=dst, in_=src, func=AF.Copy, scale=-1.0)

        def w_quantise(nm, t0, t1):
            cols = slice(128 * t0, 128 * t1)
            nc.vector.quantize_mx(
                out=w_codes[nm][:, cols].bitcast(FP8X4), scales=w_scales[nm][:, cols], in_=w_bf[nm][:, 512 * t0 : 512 * t1]
            )

        def mx_pass(out, nm, t, codes, scales, start, stop):
            cols = slice(128 * t, 128 * (t + 1))
            nc.tensor.matmul_mx(
                out=out,
                lhsT=w_codes[nm][:, cols].bitcast(FP8X4),
                lhsT_scale=w_scales[nm][:, cols],
                rhs=codes[:].bitcast(FP8X4),
                rhs_scale=scales[:],
                start=start,
                stop=stop,
            )

        y = {}
        du = sbuf("du", [128, 4, N, 2, CB], F32)
        d = sbuf("d", [128, 4, 4, 128], F32)
        u1 = sbuf("u1", [128, 4, 4, 128], F32)

        def product(r, c, t):
            y[r, c, t] = bank("y%d%d%d" % (r, c, t), [128, N, CB] if c == 0 else [128, 4, 128])
            mx_pass(y[r, c, t][:].rearrange("p g b -> p (g b)"), "w%d" % r, t, x_codes[r, c], x_scales[r, c], True, True)

        def d_of(c, t):
            return du[:, t, :, 0, :] if c == 0 else d[:, :, t, :]

        def u1_of(c, t):
            return du[:, t, :, 1, :] if c == 0 else u1[:, :, t, :]

        def relu1(c, t):
            nc.scalar.activation(out=u1_of(c, t), in_=y[1, c, t][:], func=AF.Relu, bias=bias_c[:, 1, t : t + 1])

        def diff0(c, t):
            nc.vector.scalar_tensor_tensor(
                out=d_of(c, t), in0=y[0, c, t][:], scalar=neg_bias0[:, t : t + 1], in1=u1_of(c, t), op0=MAX, op1=SUB
            )

        def turn_add(out, src, start, stop):
            nc.tensor.matmul(out=out, lhsT=src, rhs=ident[:], start=start, stop=stop, is_transpose=True)

        sum_ps = {}
        sum_sb = {}
        s_ps = {}

        def sum_rows(src, key, t0, t1):
            n = (t1 - t0) // 2
            for odd in range(2):
                sum_ps[key, odd] = bank("sum_ps_%s%d" % (key, odd), [128, n, 128])
            for j in range(4):
                for t in range(t1 - t0):
                    turn_add(sum_ps[key, t % 2][:, t // 2, :], src[:, j, t0 + t, :], j == 0 and t < 2, j == 3 and t // 2 == n - 1)

        def rows_out_of(key, n):
            for odd in range(2):
                sum_sb[key, odd] = sbuf("sum_sb_%s%d" % (key, odd), [128, n, 128], F32)
                nc.scalar.copy(out=sum_sb[key, odd][:], in_=sum_ps[key, odd][:])

        def sum_pair(t0):
            for t in (t0, t0 + 1):
                sum_ps["du%d" % t] = bank("sum_ps_du%d" % t, [128, 1, 128])
            for g in range(N):
                for t in (t0, t0 + 1):
                    turn_add(sum_ps["du%d" % t][:, 0, :], du[:, t, g].rearrange("p a b -> p (a b)"), g == 0, g == N - 1)

        def sum_out(key, n):
            sum_sb[key] = sbuf("sum_sb_" + key, [128, n, 128], F32)
            nc.scalar.copy(out=sum_sb[key][:], in_=sum_ps[key][:])

        def fold_open(c):
            s_ps[c] = bank("s_ps%d" % c, [128, 4, CB])
            nc.tensor.matmul(
                out=s_ps[c][:].rearrange("p t b -> p (t b)"),
                lhsT=ident_bf[:],
                rhs=bias0_sum[:].rearrange("p t b -> p (t b)"),
                start=True,
                stop=False,
            )

        def fold_in(c, t, rows, matrix, stop):
            nc.tensor.matmul(out=s_ps[c][:, t, :], lhsT=rows, rhs=matrix, start=False, stop=stop)

        sg_bf = {}
        l_ps = {}
        a0 = {}

        def sg_round(c):
            sg_bf[c] = sbuf("sg_bf%d" % c, [128, CB, 4], BF16)
            nc.vector.tensor_mul(
                out=sg_bf[c][:], in0=s_ps[c][:].rearrange("p t b -> p b t"), in1=gain[:].unsqueeze(1).to_broadcast([128, CB, 4])
            )

        def sg_quantise(c):
            cols = slice(CB * c, CB * (c + 1))
            nc.vector.quantize_mx(
                out=sg_codes[:, cols].bitcast(FP8X4), scales=sg_scales[:, cols], in_=sg_bf[c][:].rearrange("p b t -> p (b t)")
            )

        def logits(c):
            for t0 in (0, 2):
                l_ps[c, t0] = bank("l_ps%d%d" % (c, t0), [128, 2, B])
                for r in range(R):
                    for t in (t0, t0 + 1):
                        first, last = (r == 0 and t == t0), (r == R - 1 and t == t0 + 1)
                        mx_pass(l_ps[c, t0][:, t - t0, :], "wa%d" % r, t, sg_codes, sg_scales, first, last)

        def softmax(c):
            copies = 1 + c
            a0[c] = sbuf("a0_%d" % c, [128, 4, CB, copies], F32)
            for t in range(4):
                nc.scalar.activation(
                    out=a0[c][:, t],
                    in_=l_ps[c, t - t % 2][:, t % 2, CB * c : CB * (c + 1)].unsqueeze(2).to_broadcast([128, CB, copies]),
                    func=AF.Sigmoid,
                    bias=ba_diff[:, t : t + 1],
                    scale=sign[:],
                )

        weighted0 = sbuf("weighted0", [128, 4, N, CB], F32)
        weighted1 = sbuf("weighted1", [128, 4, 4, 128], F32)
        res = sbuf("res", [128, 4, 4, 128], F32)
        res_bf = {}
        res_codes = {}
        res_rows = {}
        res_ps = {}
        for c in range(NCH):
            res_bf[c] = sbuf("res_bf%d" % c, [128, CH * 4], BF16)
            res_codes[c] = sbuf("res_codes%d" % c, [128, CH], U32)
            res_rows[c] = sbuf("res_rows%d" % c, [128, 4, 128, 4], F32)
        res_scales = sbuf("res_scales", [128, T], U8)

        def weigh(c, k, t):
            if c == 0:
                out, src, reps = weighted0[:, t, 4 * k : 4 * k + 4], du[:, t, 4 * k : 4 * k + 4, 0, :], 4
            else:
                out, src, reps = weighted1[:, 2 * k : 2 * k + 2, t, :], d[:, 2 * k : 2 * k + 2, t, :], 2
            nc.vector.scalar_tensor_tensor(
                out=out,
                in0=src,
                scalar=bias_c[:, 0, t : t + 1],
                in1=a0[c][:, t].rearrange("p b h -> p (b h)").unsqueeze(1).to_broadcast([128, reps, 256 // reps]),
                op0=ADD,
                op1=MUL,
            )

        def add_u1(j, f0=0, f1=2):
            items = slice(32 * f0, 32 * f1)
            nc.vector.tensor_add(
                out=res[:, j].rearrange("p t (b h) -> p t b h", h=2)[:, :, items],
                in0=weighted0[:, :, 2 * j : 2 * j + 2, items].rearrange("p t h b -> p t b h"),
                in1=du[:, :, 2 * j : 2 * j + 2, 1, items].rearrange("p t h b -> p t b h"),
            )

        rows_out = out_0.rearrange("b n e -> (b n) e").rearrange("(c q j) e -> c q j e", c=NCH, j=4)

        def res_turn(j):
            res_ps[0, j] = bank("res_ps0%d" % j, [128, 4, 128])
            for t in range(4):
                nc.tensor.transpose(res_ps[0, j][:, t, :], res[:, j, t, :], ident[:])

        def turn_u1(k):
            for j in (2 * k, 2 * k + 1):
                res_ps[1, j] = bank("res_ps1%d" % j, [128, 4, 128])
            for t in range(4):
                for j in (2 * k, 2 * k + 1):
                    turn_add(res_ps[1, j][:, t, :], u1[:, j, t, :], t == 0, False)

        def turn_weighted(k):
            for t in range(4):
                for j in (2 * k, 2 * k + 1):
                    turn_add(res_ps[1, j][:, t, :], weighted1[:, j, t, :], False, t == 3)

        def res_out(c, j):
            nc.scalar.copy(out=res_rows[c][:, j], in_=res_ps[c, j][:].rearrange("q t p -> q p t"))

        def store_rows1(j):
            nc.sync.dma_start(
                out=out_0[CB:B, 2 * j : 2 * j + 2, :].rearrange("b o e -> b (o e)"),
                in_=res_rows[1][:, j].rearrange("q p t -> q (p t)"),
            )

        def store_rows(c, j0, j1, queue):
            queue.dma_start(
                out=rows_out[c, :, j0:j1, :].rearrange("q j e -> q (j e)"),
                in_=res_rows[c][:, j0:j1].rearrange("q j p t -> q (j p t)"),
            )

        words_out = out_1.rearrange("one p token t -> (one p) (token t)").bitcast(I32)
        scales_out = out_2.rearrange("one block token -> (one block) token").bitcast(I32)

        def pairs_of(tile, k, f0, f1):
            return tile[:, 2 * k : 2 * k + 2].rearrange("p j t (a o) -> p a (j t) o", o=2)[:, 32 * f0 : 32 * f1]

        def rounded(c, k, f0, f1):
            return res_bf[c][:].rearrange("p (a o k jt) -> p k a jt o", o=2, k=2, jt=8)[:, k, 32 * f0 : 32 * f1]

        def res_round(k, f0, f1, eng):
            copy(eng, rounded(0, k, f0, f1), pairs_of(res, k, f0, f1))

        def add_round(j, f0, f1):
            items = slice(32 * f0, 32 * f1)
            walk = "p t (b o) -> p b t o"
            nc.vector.tensor_add(
                out=res_bf[1][:].rearrange("p (b j o t) -> p j b t o", j=4, o=2, t=4)[:, j, items],
                in0=weighted1[:, j].rearrange(walk, o=2)[:, items],
                in1=u1[:, j].rearrange(walk, o=2)[:, items],
            )

        def res_quantise(c, f):
            nc.vector.quantize_mx(
                out=res_codes[c][:, 256 * f : 256 * (f + 1)].bitcast(FP8X4),
                scales=res_scales[:, CH * c + 256 * f : CH * c + 256 * (f + 1)],
                in_=res_bf[c][:, 1024 * f : 1024 * (f + 1)],
            )

        def store_words(c, f0, f1):
            nc.sync.dma_start(
                out=words_out[:, CH * c + 256 * f0 : CH * c + 256 * f1], in_=res_codes[c][:, 256 * f0 : 256 * f1].bitcast(I32)
            )

        def store_scales():
            for quad in range(4):
                (nc.scalar if quad < 2 else nc.sync).dma_start(
                    out=scales_out[4 * quad : 4 * quad + 4, :], in_=res_scales[32 * quad : 32 * quad + 4, :].bitcast(I32)
                )


        load_x(1, 0, 0, 1)
        load_x(1, 0, 1, 2)
        load_w("w1")
        load_x(0, 0, 0, 2)
        load_w("w0")
        for r in (1, 0):
            load_x(r, 1, 0, 2)
            load_w("wa%d" % (1 - r))
        load_gate_vectors()

        warm(zeros[:])
        warm(zeros[:])
        bias_constants()
        x_turn(1, 0)
        warm(zeros[:])
        warm(zeros[:])
        w_lay("w1", 0, 96, V)
        w_lay("w1", 96, 128, S)
        x_turn(0, 0)
        x_quantise(1, 0)
        w_quantise("w1", 0, 2)
        w_quantise("w1", 2, 4)
        for t in range(4):
            product(1, 0, t)
            relu1(0, t)

        w_lay("w0", 0, 128, V)
        x_quantise(0, 0)
        w_quantise("w0", 0, 2)
        w_quantise("w0", 2, 4)
        x_turn(1, 1)
        w_lay("wa0", 0, 64, V)
        for t in range(4):
            product(0, 0, t)
            diff0(0, t)
        w_lay_negated("wa0", 64, 128, S)
        x_turn(0, 1)
        x_quantise(1, 1)
        w_lay("wa1", 112, 128, S)
        w_lay("wa1", 64, 112, V)
        w_lay_negated("wa1", 0, 64, V)
        x_quantise(0, 1)

        for t0 in (0, 2):
            sum_pair(t0)
            sum_out("du%d" % t0, 1)
            sum_out("du%d" % (t0 + 1), 1)
        w_quantise("wa0", 0, 4)
        gate_constants()
        w_quantise("wa1", 2, 4)
        for t in range(2):
            product(1, 1, t)
            relu1(1, t)
        fold_open(0)
        for t in range(4):
            fold_in(0, t, sum_sb["du%d" % t][:, 0], fold_du[:], t == 3)
        sg_round(0)
        w_quantise("wa1", 0, 2)
        sg_quantise(0)
        product(0, 1, 0)
        for t in range(2, 4):
            product(1, 1, t)
            relu1(1, t)
        diff0(1, 0)
        for t in range(1, 4):
            product(0, 1, t)
        logits(0)
        softmax(0)
        for t in range(1, 4):
            diff0(1, t)
        sum_rows(u1, "u", 0, 4)
        rows_out_of("u", 2)
        for t0 in (0, 2):
            sum_rows(d, "d%d" % t0, t0, t0 + 2)
            rows_out_of("d%d" % t0, 1)
        fold_open(1)
        for t in range(4):
            fold_in(1, t, sum_sb["u", t % 2][:, t // 2], fold[:, 1], False)
        for t in range(4):
            fold_in(1, t, sum_sb["d%d" % (t - t % 2), t % 2][:, 0], fold[:, 0], t == 3)

        for t in range(4):
            weigh(0, 0, t)
        weigh(0, 1, 0)
        add_u1(0)
        add_u1(1)
        res_round(0, 0, 2, S)
        for j in range(2):
            res_turn(j)
        turn_u1(0)
        res_out(0, 0)
        store_rows(0, 0, 1, nc.sync)
        res_out(0, 1)
        store_rows(0, 1, 2, nc.sync)
        weigh(0, 1, 1)
        weigh(0, 1, 2)
        weigh(0, 1, 3)
        sg_round(1)
        add_u1(2, 0, 1)
        sg_quantise(1)
        add_u1(3, 0, 1)
        add_u1(2, 1, 2)
        res_round(1, 0, 1, V)
        add_u1(3, 1, 2)
        res_quantise(0, 0)
        logits(1)
        softmax(1)
        res_round(1, 1, 2, S)
        for j in range(2, 4):
            res_turn(j)
            res_out(0, j)
            store_rows(0, j, j + 1, nc.sync)

        turn_u1(1)
        for k in range(2):
            for t in range(4):
                weigh(1, k, t)
            if k == 0:
                res_quantise(0, 1)
                store_words(0, 0, 2)
            turn_weighted(k)
            for j in (2 * k, 2 * k + 1):
                res_out(1, j)
                store_rows1(j)
        for j in range(3):
            add_round(j, 0, 2)
        for f in range(2):
            add_round(3, f, f + 1)
        for f in range(2):
            res_quantise(1, f)
            store_words(1, f, f + 1)
        store_scales()
